import numpy as np
import ml_dtypes


def mxq(x, axis, fmt="e4m3"):
    dtype, down = {"e4m3": (ml_dtypes.float8_e4m3fn, 7), "e5m2": (ml_dtypes.float8_e5m2, 14)}[fmt]
    v = np.moveaxis(np.asarray(x, np.float32).astype(ml_dtypes.bfloat16).astype(np.float64), axis, -1)
    blocks = v.reshape(v.shape[:-1] + (-1, 32))
    amax = np.abs(blocks).max(-1, keepdims=True)
    byte = np.maximum(np.where(amax > 0, np.frexp(amax)[1] - 1 + 127, 0) - down, 1)
    scale = np.exp2(byte - 127.0)
    codes = (blocks / scale).astype(np.float32).astype(dtype).astype(np.float64)
    return np.moveaxis((codes * scale).reshape(v.shape), -1, axis)


WIDE = False


def mx_kscale(k):
    if not WIDE:
        return np.ones(k)
    levels = np.array([10, -10, 5, -5, 0])
    if k % 512:
        return np.exp2(np.random.permutation(np.resize(levels, k // 32))).repeat(32)
    a = np.empty((k // 512, 16))
    for p in range(k // 512):
        a[p, :8] = np.random.permutation(np.resize(levels, 8))
        for g in range(8):
            far = levels[np.abs(levels - a[p, g]) >= 10]
            a[p, g + 8] = far[np.random.randint(len(far))]
    return np.exp2(a.ravel()).repeat(32)


def f64(x):
    return np.asarray(x).astype(np.float64)


def striped(idx):
    return np.tile(idx.reshape(-1, 16).T, (8, 1)).astype(np.uint16)


def unstriped(offs):
    return offs[:16].T.reshape(-1).astype(np.int64)


E2M1 = np.array([0.0, 0.5, 1.0, 1.5, 2.0, 3.0, 4.0, 6.0, -0.0, -0.5, -1.0, -1.5, -2.0, -3.0, -4.0, -6.0])


def pack_weight(w, fmt):
    k, n = w.shape
    w = f64(np.asarray(w, np.float32).astype(ml_dtypes.bfloat16)).reshape(k // 32, 32, n)
    amax = np.abs(w).max(1)
    if fmt == "e4m3":
        byte = np.frexp(amax)[1] - 1 + 127 - 7
    else:
        mant, ex = np.frexp(amax / 6.0)
        byte = np.where(mant > 0.5, ex, ex - 1) + 127
    byte = np.clip(np.where(amax > 0, byte, 1), 1, 254)
    scaled = (w * np.exp2(127.0 - byte)[:, None, :]).reshape(k, n).astype(np.float32)
    by_word = np.ascontiguousarray(scaled.reshape(k // 512, 128, 4, n).transpose(0, 1, 3, 2))
    if fmt == "e4m3":
        words = by_word.astype(ml_dtypes.float8_e4m3fn).view(np.uint8)
    else:
        c = by_word.astype(ml_dtypes.float4_e2m1fn).view(np.uint8) & 0xF
        words = (c[..., 0::2] | (c[..., 1::2] << 4)).reshape(k // 512, 128, 2 * n)
    return np.ascontiguousarray(words), np.ascontiguousarray(byte.astype(np.uint8).reshape(k // 512, 16, n))


def unpack_weight(words, scales, fmt):
    g, _, n = scales.shape
    words = np.ascontiguousarray(words).reshape(g, 128, n, -1)
    if fmt == "e4m3":
        vals = words.view(ml_dtypes.float8_e4m3fn).astype(np.float64)
    else:
        nib = np.empty((g, 128, n, 4), np.uint8)
        nib[..., 0::2] = words & 0xF
        nib[..., 1::2] = words >> 4
        vals = E2M1[nib]
    vals = vals * np.repeat(np.exp2(scales.astype(np.float64) - 127.0), 8, axis=1)[..., None]
    return vals.transpose(0, 1, 3, 2).reshape(g * 512, n)


def gelu(v):
    return 0.5 * v * (1.0 + np.tanh(np.sqrt(2.0 / np.pi) * (v + 0.044715 * v**3)))


K, K2, H, N, T, S, T2 = 1024, 512, 1024, 256, 2048, 1024, 2048

def setup_inputs():
    n = np.random.standard_normal
    s = mx_kscale(K)[:, None]
    s2 = mx_kscale(K2)[:, None]
    u = mx_kscale(H)[:, None]
    perm = np.random.permutation(T2)
    tab_words, tab_scales = pack_weight(n((K, T)) * s, "e4m3")
    tab2_words, tab2_scales = pack_weight(n((K2, T)) * s2, "e4m3")
    w1_words, w1_scales = pack_weight(n((K, H)) / np.sqrt(K) / s, "e2m1")
    w4_words, w4_scales = pack_weight(n((H, N)) / np.sqrt(H) / u, "e4m3")
    return {
        "tab_words": tab_words, "tab_scales": tab_scales,
        "tab2_words": tab2_words, "tab2_scales": tab2_scales,
        "w1_words": w1_words, "w1_scales": w1_scales,
        "w2": (0.8 * n((K2, H)) / np.sqrt(K2) / s2).astype(np.float32),
        "w3": (0.6 * n((K2, H)) / np.sqrt(K2) / s2).astype(np.float32),
        "field": (n((K2, S)) * s2).astype(np.float32),
        "gain": (np.exp(0.3 * n(H)) * u[:, 0]).astype(np.float32),
        "wg1": np.exp(0.3 * n((128, S))).astype(np.float32),
        "wg2": np.exp(0.3 * n((128, S))).astype(np.float32),
        "w4_words": w4_words, "w4_scales": w4_scales,
        "offs": striped(np.random.permutation(T)[:S]),
        "offs2": striped(np.random.permutation(T)[:S]),
        "offs3": striped(perm[:S]), "offs4": striped(perm[S:]),
    }

def reference(tab_words, tab_scales, tab2_words, tab2_scales, w1_words, w1_scales, w2, w3, field, gain, wg1, wg2, w4_words, w4_scales, offs, offs2, offs3, offs4):
    v = unpack_weight(tab_words, tab_scales, "e4m3")[:, unstriped(offs)]
    v2 = unpack_weight(tab2_words, tab2_scales, "e4m3")[:, unstriped(offs2)]
    b = unpack_weight(w1_words, w1_scales, "e2m1").T @ v
    sq = b * b
    h1 = (b + sq) / (1.0 + sq)
    h2 = np.tanh(mxq(f64(w2), 0, "e4m3").T @ v2 + mxq(f64(w3), 0, "e4m3").T @ mxq(f64(field), 0, "e4m3"))
    page = np.zeros((H, T2))
    page[:, unstriped(offs3)] = np.tile(f64(wg1), (H // 128, 1)) * h1
    page[:, unstriped(offs4)] = np.tile(f64(wg2), (H // 128, 1)) * h2
    z = f64(gain)[:, None] * page
    return unpack_weight(w4_words, w4_scales, "e4m3").T @ mxq(z, 0, "e4m3")

@@ -1,0 +1,363 @@
+from contextlib import ExitStack
+
+import concourse.mybir as mybir
+from concourse.masks import make_identity
+
+K, K2, H, N, T, S, T2 = 1024, 512, 1024, 256, 2048, 1024, 2048
+FLOPS = 2 * K * H * S + 2 * 2 * K2 * H * S + 2 * H * N * T2
+
+F32 = mybir.dt.float32
+BF16 = mybir.dt.bfloat16
+I32 = mybir.dt.int32
+U32 = mybir.dt.uint32
+U16 = mybir.dt.uint16
+U8 = mybir.dt.uint8
+E4M3 = mybir.dt.float8_e4m3fn_x4
+E2M1 = mybir.dt.float4_e2m1fn_x4
+ACT = mybir.ActivationFunctionType
+MULT = mybir.AluOpType.mult
+
+P = 128
+PACK = 4
+BANK = 512
+QUADS = 4
+
+
+def tile_list_stellarator_mode_weave_kernel(
+    tc, tab_words, tab_scales, tab2_words, tab2_scales, w1_words, w1_scales, w2, w3, field, gain,
+    wg1, wg2, w4_words, w4_scales, offs, offs2, offs3, offs4, out,
+):
+    nc = tc.nc
+    with ExitStack() as ctx:
+        keep = ctx.enter_context(tc.tile_pool(name="keep", bufs=1))
+        ring = ctx.enter_context(tc.tile_pool(name="ring", bufs=1))
+        psum = ctx.enter_context(tc.psum_pool(name="psum", bufs=1))
+
+        def held(shape, dtype, name):
+            return keep.tile(shape, dtype, name=name, align_bytes=64)
+
+        def big(shape, dtype, name):
+            return ring.tile(shape, dtype, name=name, tag="big", bufs=3, align_bytes=64)
+
+        def bank(tag, name):
+            return psum.tile([P, BANK], F32, name=name, tag=tag, bufs={"bt": 2, "act": 2, "num": 4}[tag])
+
+        lists = [held([P, S // 16], U16, "list%d" % i) for i in range(4)]
+        idx, idx2, idx3, idx4 = lists
+
+        tab_sc = ring.tile([P, 2, T], U8, name="tab_sc", tag="sc_a", bufs=1, align_bytes=64)
+        tab2_sc = ring.tile([P, T], U8, name="tab2_sc", tag="sc_b", bufs=1, align_bytes=64)
+        w1_sc = [held([P, 2, BANK], U8, "w1_sc%d" % a) for a in range(2)]
+        w4_sc = held([P, 2, N], U8, "w4_sc")
+
+        def clear(engine, planes):
+            engine.memset(planes[:].rearrange("p a c -> p (a c)").bitcast(I32), 0)
+
+        clear(nc.vector, tab_sc)
+        clear(nc.vector, w1_sc[0])
+        nc.vector.memset(tab2_sc[:].bitcast(I32), 0)
+        clear(nc.vector, w1_sc[1])
+        clear(nc.vector, w4_sc)
+
+        def edge_slot(shape, dtype, name):
+            return ring.tile(shape, dtype, name=name, tag="h2", bufs=3, align_bytes=64)
+
+        def load_scales(dst, src, cols):
+            for q in range(QUADS):
+                rows = src[:, 4 * q : 4 * q + 4, cols].rearrange("g r c -> r g c")
+                nc.sync.dma_start(dst[32 * q : 32 * q + 4, :, :].bitcast(I32), rows.bitcast(I32))
+
+        ident = held([P, P], F32, "ident")
+        make_identity(nc, ident[:])
+        warm = held([P, 1], F32, "warm")
+        nc.scalar.activation(warm[:], ident[:, 0:1], ACT.Ln, bias=1.0)
+
+        for tile_, src in zip(lists, (offs, offs2, offs3, offs4)):
+            nc.sync.dma_start(tile_[:], src)
+        tab_w = [big([P, T], U32, "tab_w%d" % g) for g in range(2)]
+
+        def load_words(dst, src):
+            nc.sync.dma_start(dst[:].bitcast(I32), src.rearrange("p n i -> p (n i)").bitcast(I32))
+
+        w1_w = [held([P, 2, 2 * BANK], U8, "w1_w0"), held([P, 2, 2 * BANK], U8, "w1_w1")]
+
+        def load_w1(a):
+            src = w1_words.rearrange("g p c -> p g c")[:, :, 2 * BANK * a : 2 * BANK * (a + 1)]
+            nc.sync.dma_start(w1_w[a][:].bitcast(I32), src.bitcast(I32))
+
+        gain_sb = held([P, 2, PACK], F32, "gain_sb")
+        nc.sync.dma_start(gain_sb[:], gain.rearrange("(a p t) -> p a t", a=2, t=PACK))
+        load_words(tab_w[0], tab_words[0])
+        load_words(tab_w[1], tab_words[1])
+        load_w1(0)
+        load_scales(tab_sc, tab_scales, slice(0, T))
+        load_scales(w1_sc[0], w1_scales, slice(0, BANK))
+
+        v_w = [held([P, 2, BANK], U32, "v_w0"), held([P, 2, BANK], U32, "v_w1")]
+        v_sc = [held([P, 2, BANK], U8, "v_sc0"), held([P, 2, BANK], U8, "v_sc1")]
+        for h in range(2):
+            entries = idx[:, 32 * h : 32 * h + 32]
+            for g in range(2):
+                nc.vector.tensor_copy(v_w[h][:, g, :], tab_w[g][:].indirect(entries))
+            for g in range(2):
+                nc.vector.tensor_copy(v_sc[h][:, g, :], tab_sc[:, g, :].indirect(entries))
+
+        tab2_w = big([P, T], U32, "tab2_w")
+        load_words(tab2_w, tab2_words[0])
+        for q in range(QUADS):
+            nc.sync.dma_start(
+                tab2_sc[32 * q : 32 * q + 4, :].bitcast(I32), tab2_scales[0, 4 * q : 4 * q + 4, :].bitcast(I32)
+            )
+        wg1_sb = [[held([P, 2, BANK], F32, "wg1_sb%d%d" % (h, u)) for u in range(2)] for h in range(2)]
+        wg2_sb = [held([P, S], F32, "wg2_sb%d" % t) for t in range(PACK)]
+
+        def load_wg1(h, u):
+            rows = wg1.rearrange("(m t) j -> m t j", t=PACK)[:, 2 * u : 2 * u + 2, BANK * h : BANK * (h + 1)]
+            for q in range(QUADS):
+                nc.sync.dma_start(wg1_sb[h][u][32 * q : 32 * q + 32, :, :], rows)
+
+        def load_wg2(t):
+            rows = wg2.rearrange("(m t) j -> m t j", t=PACK)[:, t, :]
+            for q in range(QUADS):
+                nc.sync.dma_start(wg2_sb[t][32 * q : 32 * q + 32, :], rows)
+
+        def load_raw(src, half, name):
+            raw = big([P, PACK, BANK], F32, name)
+            nc.sync.dma_start(
+                raw[:], src.rearrange("(p i) c -> p i c", i=PACK)[:, :, BANK * half : BANK * (half + 1)]
+            )
+            return raw
+
+        field_raw = [load_raw(field, h, "field_raw%d" % h) for h in range(2)]
+        load_wg1(0, 0)
+        load_wg1(0, 1)
+        load_wg1(1, 0)
+        load_wg1(1, 1)
+        for t in range(PACK):
+            load_wg2(t)
+        w4_w = held([P, 2, N], U32, "w4_w")
+        nc.sync.dma_start(w4_w[:].bitcast(I32), w4_words.rearrange("a p c i -> p a (c i)").bitcast(I32))
+        load_scales(w4_sc, w4_scales, slice(0, N))
+        load_scales(w1_sc[1], w1_scales, slice(BANK, 2 * BANK))
+        load_w1(1)
+        w_raw = {}
+        for a in range(2):
+            for name, src in (("w2", w2), ("w3", w3)):
+                w_raw[name, a] = load_raw(src, a, "%s_raw%d" % (name, a))
+
+        v2_sc = held([P, S], U8, "v2_sc")
+        v2_w = held([P, S], U32, "v2_w")
+        nc.vector.tensor_copy(v2_sc[:], tab2_sc[:].indirect(idx2[:]))
+        nc.vector.tensor_copy(v2_w[:], tab2_w[:].indirect(idx2[:]))
+
+        def grouped(name):
+            return ring.tile([P, BANK * PACK], BF16, name=name, tag="grouped", bufs=4, align_bytes=64)
+
+        def quantise(src, words, scales):
+            nc.vector.quantize_mx(out=words.bitcast(E4M3), scales=scales, in_=src[:])
+
+        def weave(copy, dst, planes):
+            copy(
+                dst[:].rearrange("p (c e i) -> p c i e", e=4, i=PACK),
+                planes.rearrange("p i (c e) -> p c i e", e=4),
+            )
+
+        q_w = {name: [held([P, BANK], U32, "q_%s%d" % (name, x)) for x in range(2)] for name in ("w2", "w3")}
+        q_sc = {name: [held([P, BANK], U8, "qs_%s%d" % (name, x)) for x in range(2)] for name in ("w2", "w3", "field")}
+        field_g = [grouped("field_g%d" % h) for h in range(2)]
+        for h in range(2):
+            weave(nc.vector.tensor_copy, field_g[h], field_raw[h][:])
+
+        def quantise_field():
+            words = ring.tile([P, 2, BANK], U32, name="q_field", tag="log_t", bufs=1, align_bytes=64)
+            q_w["field"] = [words[:, h, :] for h in range(2)]
+            for h in range(2):
+                quantise(field_g[h], q_w["field"][h], q_sc["field"][h][:])
+
+        def prepare_weight(name, a):
+            g = grouped("%s_g%d" % (name, a))
+            nc.scalar.copy(
+                g[:].rearrange("p (t m i) -> p m t i", t=PACK, i=PACK),
+                w_raw[name, a][:].rearrange("p i (m t) -> p m t i", t=PACK),
+            )
+            quantise(g, q_w[name][a][:], q_sc[name][a][:])
+
+        pages = {}
+
+        def page(a, t):
+            if (a, t) not in pages:
+                pages[a, t] = ring.tile([P, T2], F32, name="page%d%d" % (a, t), tag="page", bufs=8, align_bytes=64)
+            return pages[a, t]
+
+        state = {}
+
+        def core_products(a, h):
+            b_t = ring.tile([P, 4, BANK], F32, name="b_t", tag="b_t", bufs=1, align_bytes=64)
+            sq_t = ring.tile([P, 4, BANK], F32, name="sq_t", tag="sq_t", bufs=1, align_bytes=64)
+            for jb in range(4):
+                acc = bank("bt", "acc_b")
+                cols = slice(P * jb, P * (jb + 1))
+                for g in range(2):
+                    nc.tensor.matmul_mx(
+                        out=acc[:],
+                        lhsT=v_w[h][:, g, cols].bitcast(E4M3),
+                        lhsT_scale=v_sc[h][:, g, cols],
+                        rhs=w1_w[a][:, g, :].bitcast(E2M1),
+                        rhs_scale=w1_sc[a][:, g, :],
+                        start=(g == 0),
+                        stop=(g == 1),
+                    )
+                by_slot = acc[:].rearrange("p (m t) -> p t m", t=PACK)
+                nc.scalar.activation(sq_t[:, jb, :].rearrange("p (t m) -> p t m", t=PACK), by_slot, ACT.Square)
+                nc.scalar.copy(b_t[:, jb, :].rearrange("p (t m) -> p t m", t=PACK), by_slot)
+            state[a, h] = (b_t, sq_t)
+
+        def core_features(a, h, between=()):
+            b_t, sq_t = state[a, h]
+            log_t = ring.tile([P, 4, BANK], F32, name="log_t", tag="log_t", bufs=1, align_bytes=64)
+            for t in range(PACK):
+                rows = slice(P * t, P * (t + 1))
+                nc.scalar.activation(log_t[:, :, rows], sq_t[:, :, rows], ACT.Ln, bias=1.0)
+            nums, recips = [], []
+            for t in range(PACK):
+                rows = slice(P * t, P * (t + 1))
+                logs = bank("act", "logs")
+                num = bank("num", "num")
+                for jb in range(4):
+                    nc.tensor.transpose(logs[:, P * jb : P * (jb + 1)], log_t[:, jb, rows], ident[:])
+                for jb in range(4):
+                    cols = slice(P * jb, P * (jb + 1))
+                    nc.tensor.matmul(num[:, cols], b_t[:, jb, rows], ident[:], start=True, stop=False, is_transpose=True)
+                    nc.tensor.matmul(num[:, cols], sq_t[:, jb, rows], ident[:], start=False, stop=True, is_transpose=True)
+                recip = ring.tile([P, BANK], F32, name="recip", tag="recip", bufs=8)
+                nc.scalar.activation(recip[:], logs[:], ACT.Exp, scale=-1.0)
+                nums.append(num)
+                recips.append(recip)
+                if t == 1:
+                    for step in between:
+                        step()
+            h1 = []
+            for t in range(PACK + 1):
+                if t < PACK:
+                    h1.append(ring.tile([P, BANK], F32, name="h1", tag="h1", bufs=3))
+                    nc.vector.tensor_tensor(h1[t][:], nums[t][:], recips[t][:], MULT)
+                if t > 0:
+                    s = t - 1
+                    nc.vector.tensor_tensor(
+                        page(a, s)[:].indirect(idx3[:, 32 * h : 32 * h + 32]),
+                        h1[s][:],
+                        wg1_sb[h][s // 2][:, s % 2, :],
+                        MULT,
+                    )
+
+        def edge_features(a, t):
+            h2 = edge_slot([P, S], F32, "h2")
+            rows = slice(P * t, P * (t + 1))
+            for h in range(2):
+                acc = bank("act", "acc_e")
+                cols = slice(BANK * h, BANK * (h + 1))
+                nc.tensor.matmul_mx(
+                    out=acc[:], lhsT=q_w["w3"][a][:, rows].bitcast(E4M3), lhsT_scale=q_sc["w3"][a][:, rows],
+                    rhs=q_w["field"][h].bitcast(E4M3), rhs_scale=q_sc["field"][h][:], start=True, stop=False,
+                )
+                nc.tensor.matmul_mx(
+                    out=acc[:], lhsT=q_w["w2"][a][:, rows].bitcast(E4M3), lhsT_scale=q_sc["w2"][a][:, rows],
+                    rhs=v2_w[:, cols].bitcast(E4M3), rhs_scale=v2_sc[:, cols], start=False, stop=True,
+                )
+                nc.scalar.activation(h2[:, cols], acc[:], ACT.Tanh)
+            nc.vector.tensor_tensor(page(a, t)[:].indirect(idx4[:]), h2[:], wg2_sb[t][:], MULT)
+
+        planes = {}
+
+        def round_page(a, t, chunks, width=2 * BANK):
+            for c in chunks:
+                half, at = divmod(width * c, 2 * BANK)
+                if (a, half) not in planes:
+                    shape, name = [P, PACK, 2 * BANK], "planes%d%d" % (a, half)
+                    if a == 0:
+                        planes[a, half] = ring.tile(shape, BF16, name=name, tag=("b_t", "sq_t")[half], bufs=1, align_bytes=64)
+                    else:
+                        planes[a, half] = big(shape, BF16, name)
+                nc.scalar.activation(
+                    planes[a, half][:, t, at : at + width], page(a, t)[:, width * c : width * (c + 1)], ACT.Copy,
+                    scale=gain_sb[:, a, t : t + 1],
+                )
+
+        z_w, z_sc = {}, {}
+
+        z_g = {}
+
+        def weave_z(a, c, copy, lanes):
+            if (a, c) not in z_g:
+                z_g[a, c] = grouped("z_g%d%d" % (a, c))
+            src = planes[a, c // 2][:, lanes, BANK * (c % 2) : BANK * (c % 2 + 1)]
+            dst = z_g[a, c][:].rearrange("p (c e i) -> p c i e", e=4, i=PACK)[:, :, lanes, :]
+            copy(dst, src.rearrange("p i (c e) -> p c i e", e=4))
+
+        def quantise_z(a, c):
+            if a not in z_w:
+                if a == 0:
+                    z_w[a] = ring.tile([P, T2], U32, name="z_w0", tag="page", bufs=8, align_bytes=64)
+                else:
+                    z_w[a] = big([P, T2], U32, "z_w1")
+                z_sc[a] = ring.tile([P, T2], U8, name="z_sc%d" % a, tag=("sc_a", "sc_b")[a], bufs=1, align_bytes=64)
+            cols = slice(BANK * c, BANK * (c + 1))
+            quantise(z_g[a, c], z_w[a][:, cols], z_sc[a][:, cols])
+
+        accs = {}
+
+        def project(a, c):
+            cols = slice(BANK * c, BANK * (c + 1))
+            for nt in range(2):
+                if a == 0:
+                    accs[c, nt] = bank(("bt", "num", "num", "act")[c], "acc_o")
+                rows = slice(P * nt, P * (nt + 1))
+                nc.tensor.matmul_mx(
+                    out=accs[c, nt][:], lhsT=w4_w[:, a, rows].bitcast(E4M3), lhsT_scale=w4_sc[:, a, rows],
+                    rhs=z_w[a][:, cols].bitcast(E4M3), rhs_scale=z_sc[a][:, cols], start=(a == 0), stop=(a == 1),
+                )
+                if a == 1:
+                    res = ring.tile([P, BANK], F32, name="res", tag="recip", bufs=8)
+                    if c == 2 or (c, nt) == (3, 0):
+                        nc.vector.tensor_copy(res[:], accs[c, nt][:])
+                    else:
+                        nc.scalar.copy(res[:], accs[c, nt][:])
+                    nc.sync.dma_start(out[rows, cols], res[:])
+
+        both = range(2)
+        every, low, high = slice(0, 4), slice(0, 2), slice(2, 4)
+        for a, h in ((0, 0), (0, 1), (1, 0), (1, 1)):
+            core_products(a, h)
+            core_features(a, h)
+            if (a, h) == (1, 0):
+                prepare_weight("w2", 0)
+                prepare_weight("w3", 0)
+        quantise_field()
+        rows = [(a, t) for a in range(2) for t in range(PACK)]
+        edge_features(0, 0)
+        edge_features(0, 1)
+        prepare_weight("w2", 1)
+        prepare_weight("w3", 1)
+        for n in range(2, 8):
+            edge_features(*rows[n])
+            round_page(*rows[n - 2], both)
+            if n in (5, 6):
+                for c in (2 * n - 10, 2 * n - 9):
+                    weave_z(0, c, nc.scalar.copy, every)
+                    quantise_z(0, c)
+        for c in range(4):
+            project(0, c)
+        for c in range(2):
+            weave_z(1, c, nc.scalar.copy, low)
+        round_page(1, 2, both)
+        for c in range(2, 4):
+            weave_z(1, c, nc.scalar.copy, low)
+        round_page(1, 3, range(4), width=BANK)
+        weave_z(1, 3, nc.scalar.copy, high)
+        weave_z(1, 0, nc.vector.tensor_copy, high)
+        for c in range(4):
+            if c < 2:
+                weave_z(1, c + 1, nc.vector.tensor_copy, high)
+            quantise_z(1, c)
+        for c in range(4):
+            project(1, c)

@@ -37,7 +37,10 @@ def tile_list_stellarator_mode_weave_kernel(
             return keep.tile(shape, dtype, name=name, align_bytes=64)
 
         def big(shape, dtype, name):
-            return ring.tile(shape, dtype, name=name, tag="big", bufs=3, align_bytes=64)
+            return ring.tile(shape, dtype, name=name, tag="big", bufs=2, align_bytes=64)
+
+        def page_slot(shape, dtype, name):
+            return ring.tile(shape, dtype, name=name, tag="page", bufs=8, align_bytes=64)
 
         def bank(tag, name):
             return psum.tile([P, BANK], F32, name=name, tag=tag, bufs={"bt": 2, "act": 2, "num": 4}[tag])
@@ -59,6 +62,9 @@ def tile_list_stellarator_mode_weave_kernel(
         clear(nc.vector, w1_sc[1])
         clear(nc.vector, w4_sc)
 
+        def small(name):
+            return ring.tile([P, BANK], F32, name=name, tag="small", bufs=5)
+
         def edge_slot(shape, dtype, name):
             return ring.tile(shape, dtype, name=name, tag="h2", bufs=3, align_bytes=64)
 
@@ -69,32 +75,72 @@ def tile_list_stellarator_mode_weave_kernel(
 
         ident = held([P, P], F32, "ident")
         make_identity(nc, ident[:])
-        warm = held([P, 1], F32, "warm")
-        nc.scalar.activation(warm[:], ident[:, 0:1], ACT.Ln, bias=1.0)
 
-        for tile_, src in zip(lists, (offs, offs2, offs3, offs4)):
-            nc.sync.dma_start(tile_[:], src)
         tab_w = [big([P, T], U32, "tab_w%d" % g) for g in range(2)]
 
         def load_words(dst, src):
             nc.sync.dma_start(dst[:].bitcast(I32), src.rearrange("p n i -> p (n i)").bitcast(I32))
 
-        w1_w = [held([P, 2, 2 * BANK], U8, "w1_w0"), held([P, 2, 2 * BANK], U8, "w1_w1")]
+        w1_w = [ring.tile([P, 2, 2 * BANK], U8, name="w1_w0", tag="words", bufs=1, align_bytes=64), held([P, 2, 2 * BANK], U8, "w1_w1")]
 
         def load_w1(a):
             src = w1_words.rearrange("g p c -> p g c")[:, :, 2 * BANK * a : 2 * BANK * (a + 1)]
             nc.sync.dma_start(w1_w[a][:].bitcast(I32), src.bitcast(I32))
 
+        nc.sync.dma_start(idx[:], offs)
+        load_words(tab_w[0], tab_words[0])
+        for tile_, src in zip(lists[1:], (offs2, offs3, offs4)):
+            nc.sync.dma_start(tile_[:], src)
         gain_sb = held([P, 2, PACK], F32, "gain_sb")
         nc.sync.dma_start(gain_sb[:], gain.rearrange("(a p t) -> p a t", a=2, t=PACK))
-        load_words(tab_w[0], tab_words[0])
+        wg1_sb = [small("wg1_sb%d" % h) for h in range(2)]
+        nc.sync.dma_start(wg1_sb[0][:], wg1[:, 0:BANK])
         load_words(tab_w[1], tab_words[1])
-        load_w1(0)
+        def load_raw(pool, src, half, name):
+            raw = pool([P, PACK, BANK], F32, name)
+            nc.sync.dma_start(
+                raw[:], src.rearrange("(p i) c -> p i c", i=PACK)[:, :, BANK * half : BANK * (half + 1)]
+            )
+            return raw
+
+        tab2_w = page_slot([P, T], U32, "tab2_w")
+        wg2_sb = [held([P, S], F32, "wg2_sb%d" % t) for t in range(PACK)]
+
+        def load_wg2(t):
+            rows = wg2.rearrange("(m t) j -> m t j", t=PACK)[:, t, :]
+            for q in range(QUADS):
+                nc.sync.dma_start(wg2_sb[t][32 * q : 32 * q + 32, :], rows)
+
+        def load_tab2_scales():
+            for q in range(QUADS):
+                nc.sync.dma_start(
+                    tab2_sc[32 * q : 32 * q + 4, :].bitcast(I32), tab2_scales[0, 4 * q : 4 * q + 4, :].bitcast(I32)
+                )
+
+        field_raw, w_raw = {}, {}
         load_scales(tab_sc, tab_scales, slice(0, T))
+        load_w1(0)
+        nc.sync.dma_start(wg1_sb[1][:], wg1[:, BANK:S])
+        load_words(tab2_w, tab2_words[0])
+        load_tab2_scales()
         load_scales(w1_sc[0], w1_scales, slice(0, BANK))
 
-        v_w = [held([P, 2, BANK], U32, "v_w0"), held([P, 2, BANK], U32, "v_w1")]
-        v_sc = [held([P, 2, BANK], U8, "v_sc0"), held([P, 2, BANK], U8, "v_sc1")]
+        neg_log_wg = [held([P, 4, PACK, QUADS, 32], F32, "neg_log_wg%d" % h) for h in range(2)]
+        for h in range(2):
+            log_wg = small("log_wg")
+            nc.scalar.activation(log_wg[:], wg1_sb[h][:], ACT.Ln)
+            turned = bank("bt", "turned")
+            for jb in range(4):
+                cols = slice(P * jb, P * (jb + 1))
+                nc.tensor.transpose(turned[:, cols], log_wg[:, cols], ident[:])
+            for jb in range(4):
+                src = turned[:, P * jb : P * (jb + 1)].rearrange("p (m t) -> p t m", t=PACK)
+                nc.scalar.activation(
+                    neg_log_wg[h][:, jb], src.unsqueeze(2).to_broadcast([P, PACK, QUADS, 32]), ACT.Copy, scale=-1.0
+                )
+
+        v_w = [ring.tile([P, 2, BANK], U32, name="v_w0", tag="planes0", bufs=1, align_bytes=64), held([P, 2, BANK], U32, "v_w1")]
+        v_sc = [ring.tile([P, 2, BANK], U8, name="v_sc0", tag="planes1", bufs=1, align_bytes=64), held([P, 2, BANK], U8, "v_sc1")]
         for h in range(2):
             entries = idx[:, 32 * h : 32 * h + 32]
             for g in range(2):
@@ -102,48 +148,19 @@ def tile_list_stellarator_mode_weave_kernel(
             for g in range(2):
                 nc.vector.tensor_copy(v_sc[h][:, g, :], tab_sc[:, g, :].indirect(entries))
 
-        tab2_w = big([P, T], U32, "tab2_w")
-        load_words(tab2_w, tab2_words[0])
-        for q in range(QUADS):
-            nc.sync.dma_start(
-                tab2_sc[32 * q : 32 * q + 4, :].bitcast(I32), tab2_scales[0, 4 * q : 4 * q + 4, :].bitcast(I32)
-            )
-        wg1_sb = [[held([P, 2, BANK], F32, "wg1_sb%d%d" % (h, u)) for u in range(2)] for h in range(2)]
-        wg2_sb = [held([P, S], F32, "wg2_sb%d" % t) for t in range(PACK)]
-
-        def load_wg1(h, u):
-            rows = wg1.rearrange("(m t) j -> m t j", t=PACK)[:, 2 * u : 2 * u + 2, BANK * h : BANK * (h + 1)]
-            for q in range(QUADS):
-                nc.sync.dma_start(wg1_sb[h][u][32 * q : 32 * q + 32, :, :], rows)
-
-        def load_wg2(t):
-            rows = wg2.rearrange("(m t) j -> m t j", t=PACK)[:, t, :]
-            for q in range(QUADS):
-                nc.sync.dma_start(wg2_sb[t][32 * q : 32 * q + 32, :], rows)
-
-        def load_raw(src, half, name):
-            raw = big([P, PACK, BANK], F32, name)
-            nc.sync.dma_start(
-                raw[:], src.rearrange("(p i) c -> p i c", i=PACK)[:, :, BANK * half : BANK * (half + 1)]
-            )
-            return raw
-
-        field_raw = [load_raw(field, h, "field_raw%d" % h) for h in range(2)]
-        load_wg1(0, 0)
-        load_wg1(0, 1)
-        load_wg1(1, 0)
-        load_wg1(1, 1)
-        for t in range(PACK):
-            load_wg2(t)
-        w4_w = held([P, 2, N], U32, "w4_w")
-        nc.sync.dma_start(w4_w[:].bitcast(I32), w4_words.rearrange("a p c i -> p a (c i)").bitcast(I32))
-        load_scales(w4_sc, w4_scales, slice(0, N))
+        field_raw[0] = load_raw(page_slot, field, 0, "field_raw0")
+        field_raw[1] = load_raw(page_slot, field, 1, "field_raw1")
+        w_raw["w3", 0] = load_raw(page_slot, w3, 0, "w3_raw0")
+        w_raw["w2", 0] = load_raw(page_slot, w2, 0, "w2_raw0")
+        load_wg2(0)
+        load_wg2(1)
+        w_raw["w3", 1] = load_raw(big, w3, 1, "w3_raw1")
+        w_raw["w2", 1] = load_raw(big, w2, 1, "w2_raw1")
         load_scales(w1_sc[1], w1_scales, slice(BANK, 2 * BANK))
         load_w1(1)
-        w_raw = {}
-        for a in range(2):
-            for name, src in (("w2", w2), ("w3", w3)):
-                w_raw[name, a] = load_raw(src, a, "%s_raw%d" % (name, a))
+        load_wg2(2)
+        load_wg2(3)
+        load_scales(w4_sc, w4_scales, slice(0, N))
 
         v2_sc = held([P, S], U8, "v2_sc")
         v2_w = held([P, S], U32, "v2_w")
@@ -164,15 +181,16 @@ def tile_list_stellarator_mode_weave_kernel(
 
         q_w = {name: [held([P, BANK], U32, "q_%s%d" % (name, x)) for x in range(2)] for name in ("w2", "w3")}
         q_sc = {name: [held([P, BANK], U8, "qs_%s%d" % (name, x)) for x in range(2)] for name in ("w2", "w3", "field")}
-        field_g = [grouped("field_g%d" % h) for h in range(2)]
-        for h in range(2):
-            weave(nc.vector.tensor_copy, field_g[h], field_raw[h][:])
+        q_field = held([P, 2, BANK], U32, "q_field")
+        q_w["field"] = [q_field[:, h, :] for h in range(2)]
 
-        def quantise_field():
-            words = ring.tile([P, 2, BANK], U32, name="q_field", tag="log_t", bufs=1, align_bytes=64)
-            q_w["field"] = [words[:, h, :] for h in range(2)]
-            for h in range(2):
-                quantise(field_g[h], q_w["field"][h], q_sc["field"][h][:])
+        def prepare_field(h, copy):
+            g = grouped("field_g%d" % h)
+            weave(copy, g, field_raw[h][:])
+            quantise(g, q_w["field"][h], q_sc["field"][h][:])
+
+        prepare_field(0, nc.vector.tensor_copy)
+        prepare_field(1, nc.vector.tensor_copy)
 
         def prepare_weight(name, a):
             g = grouped("%s_g%d" % (name, a))
@@ -186,15 +204,18 @@ def tile_list_stellarator_mode_weave_kernel(
 
         def page(a, t):
             if (a, t) not in pages:
-                pages[a, t] = ring.tile([P, T2], F32, name="page%d%d" % (a, t), tag="page", bufs=8, align_bytes=64)
+                pages[a, t] = page_slot([P, T2], F32, "page%d%d" % (a, t))
             return pages[a, t]
 
         state = {}
 
-        def core_products(a, h):
-            b_t = ring.tile([P, 4, BANK], F32, name="b_t", tag="b_t", bufs=1, align_bytes=64)
-            sq_t = ring.tile([P, 4, BANK], F32, name="sq_t", tag="sq_t", bufs=1, align_bytes=64)
-            for jb in range(4):
+        def core_products(a, h, blocks):
+            if (a, h) not in state:
+                b_t = ring.tile([P, 4, BANK], F32, name="b_t", tag="b_t", bufs=1, align_bytes=64)
+                sq_t = ring.tile([P, 4, BANK], F32, name="sq_t", tag="sq_t", bufs=1, align_bytes=64)
+                state[a, h] = (b_t, sq_t)
+            b_t, sq_t = state[a, h]
+            for jb in blocks:
                 acc = bank("bt", "acc_b")
                 cols = slice(P * jb, P * (jb + 1))
                 for g in range(2):
@@ -210,51 +231,38 @@ def tile_list_stellarator_mode_weave_kernel(
                 by_slot = acc[:].rearrange("p (m t) -> p t m", t=PACK)
                 nc.scalar.activation(sq_t[:, jb, :].rearrange("p (t m) -> p t m", t=PACK), by_slot, ACT.Square)
                 nc.scalar.copy(b_t[:, jb, :].rearrange("p (t m) -> p t m", t=PACK), by_slot)
-            state[a, h] = (b_t, sq_t)
 
-        def core_features(a, h, between=()):
+        def core_features(a, h, between):
             b_t, sq_t = state[a, h]
             log_t = ring.tile([P, 4, BANK], F32, name="log_t", tag="log_t", bufs=1, align_bytes=64)
             for t in range(PACK):
                 rows = slice(P * t, P * (t + 1))
                 nc.scalar.activation(log_t[:, :, rows], sq_t[:, :, rows], ACT.Ln, bias=1.0)
-            nums, recips = [], []
             for t in range(PACK):
                 rows = slice(P * t, P * (t + 1))
                 logs = bank("act", "logs")
                 num = bank("num", "num")
-                for jb in range(4):
-                    nc.tensor.transpose(logs[:, P * jb : P * (jb + 1)], log_t[:, jb, rows], ident[:])
-                for jb in range(4):
-                    cols = slice(P * jb, P * (jb + 1))
-                    nc.tensor.matmul(num[:, cols], b_t[:, jb, rows], ident[:], start=True, stop=False, is_transpose=True)
-                    nc.tensor.matmul(num[:, cols], sq_t[:, jb, rows], ident[:], start=False, stop=True, is_transpose=True)
-                recip = ring.tile([P, BANK], F32, name="recip", tag="recip", bufs=8)
-                nc.scalar.activation(recip[:], logs[:], ACT.Exp, scale=-1.0)
-                nums.append(num)
-                recips.append(recip)
-                if t == 1:
-                    for step in between:
-                        step()
-            h1 = []
-            for t in range(PACK + 1):
-                if t < PACK:
-                    h1.append(ring.tile([P, BANK], F32, name="h1", tag="h1", bufs=3))
-                    nc.vector.tensor_tensor(h1[t][:], nums[t][:], recips[t][:], MULT)
-                if t > 0:
-                    s = t - 1
-                    nc.vector.tensor_tensor(
-                        page(a, s)[:].indirect(idx3[:, 32 * h : 32 * h + 32]),
-                        h1[s][:],
-                        wg1_sb[h][s // 2][:, s % 2, :],
-                        MULT,
-                    )
+                for dst, one, other in (
+                    (logs, lambda jb: log_t[:, jb, rows], lambda jb: neg_log_wg[h][:, jb, t].rearrange("p g m -> p (g m)")),
+                    (num, lambda jb: b_t[:, jb, rows], lambda jb: sq_t[:, jb, rows]),
+                ):
+                    for jb in range(4):
+                        cols = slice(P * jb, P * (jb + 1))
+                        nc.tensor.matmul(dst[:, cols], one(jb), ident[:], start=True, stop=False, is_transpose=True)
+                        nc.tensor.matmul(dst[:, cols], other(jb), ident[:], start=False, stop=True, is_transpose=True)
+                factor = small("factor")
+                nc.scalar.activation(factor[:], logs[:], ACT.Exp, scale=-1.0)
+                numer = ring.tile([P, BANK], F32, name="numer", tag="numer", bufs=4)
+                nc.scalar.copy(numer[:], num[:])
+                nc.vector.tensor_tensor(page(a, t)[:].indirect(idx3[:, 32 * h : 32 * h + 32]), numer[:], factor[:], MULT)
+                if t in between:
+                    between[t]()
 
         def edge_features(a, t):
             h2 = edge_slot([P, S], F32, "h2")
             rows = slice(P * t, P * (t + 1))
             for h in range(2):
-                acc = bank("act", "acc_e")
+                acc = bank("num" if (a, t) >= (1, 2) else "bt", "acc_e")
                 cols = slice(BANK * h, BANK * (h + 1))
                 nc.tensor.matmul_mx(
                     out=acc[:], lhsT=q_w["w3"][a][:, rows].bitcast(E4M3), lhsT_scale=q_sc["w3"][a][:, rows],
@@ -274,10 +282,10 @@ def tile_list_stellarator_mode_weave_kernel(
                 half, at = divmod(width * c, 2 * BANK)
                 if (a, half) not in planes:
                     shape, name = [P, PACK, 2 * BANK], "planes%d%d" % (a, half)
-                    if a == 0:
+                    if a == 1:
                         planes[a, half] = ring.tile(shape, BF16, name=name, tag=("b_t", "sq_t")[half], bufs=1, align_bytes=64)
                     else:
-                        planes[a, half] = big(shape, BF16, name)
+                        planes[a, half] = ring.tile(shape, BF16, name=name, tag="planes%d" % half, bufs=1, align_bytes=64)
                 nc.scalar.activation(
                     planes[a, half][:, t, at : at + width], page(a, t)[:, width * c : width * (c + 1)], ACT.Copy,
                     scale=gain_sb[:, a, t : t + 1],
@@ -289,7 +297,8 @@ def tile_list_stellarator_mode_weave_kernel(
 
         def weave_z(a, c, copy, lanes):
             if (a, c) not in z_g:
-                z_g[a, c] = grouped("z_g%d%d" % (a, c))
+                name = "z_g%d%d" % (a, c)
+                z_g[a, c] = edge_slot([P, BANK * PACK], BF16, name) if (a, c) == (1, 3) else grouped(name)
             src = planes[a, c // 2][:, lanes, BANK * (c % 2) : BANK * (c % 2 + 1)]
             dst = z_g[a, c][:].rearrange("p (c e i) -> p c i e", e=4, i=PACK)[:, :, lanes, :]
             copy(dst, src.rearrange("p i (c e) -> p c i e", e=4))
@@ -297,27 +306,29 @@ def tile_list_stellarator_mode_weave_kernel(
         def quantise_z(a, c):
             if a not in z_w:
                 if a == 0:
-                    z_w[a] = ring.tile([P, T2], U32, name="z_w0", tag="page", bufs=8, align_bytes=64)
+                    z_w[a] = page_slot([P, T2], U32, "z_w0")
                 else:
                     z_w[a] = big([P, T2], U32, "z_w1")
                 z_sc[a] = ring.tile([P, T2], U8, name="z_sc%d" % a, tag=("sc_a", "sc_b")[a], bufs=1, align_bytes=64)
             cols = slice(BANK * c, BANK * (c + 1))
             quantise(z_g[a, c], z_w[a][:, cols], z_sc[a][:, cols])
 
+        w4_w = ring.tile([P, 2, N], U32, name="w4_w", tag="words", bufs=1, align_bytes=64)
+        nc.sync.dma_start(w4_w[:].bitcast(I32), w4_words.rearrange("a p c i -> p a (c i)").bitcast(I32))
         accs = {}
 
         def project(a, c):
             cols = slice(BANK * c, BANK * (c + 1))
             for nt in range(2):
                 if a == 0:
-                    accs[c, nt] = bank(("bt", "num", "num", "act")[c], "acc_o")
+                    accs[c, nt] = bank(("bt", "act", "num", "num")[c], "acc_o")
                 rows = slice(P * nt, P * (nt + 1))
                 nc.tensor.matmul_mx(
                     out=accs[c, nt][:], lhsT=w4_w[:, a, rows].bitcast(E4M3), lhsT_scale=w4_sc[:, a, rows],
                     rhs=z_w[a][:, cols].bitcast(E4M3), rhs_scale=z_sc[a][:, cols], start=(a == 0), stop=(a == 1),
                 )
                 if a == 1:
-                    res = ring.tile([P, BANK], F32, name="res", tag="recip", bufs=8)
+                    res = small("res") if nt == 0 else ring.tile([P, BANK], F32, name="res", tag="numer", bufs=4)
                     if c == 2 or (c, nt) == (3, 0):
                         nc.vector.tensor_copy(res[:], accs[c, nt][:])
                     else:
@@ -326,25 +337,32 @@ def tile_list_stellarator_mode_weave_kernel(
 
         both = range(2)
         every, low, high = slice(0, 4), slice(0, 2), slice(2, 4)
-        for a, h in ((0, 0), (0, 1), (1, 0), (1, 1)):
-            core_products(a, h)
-            core_features(a, h)
-            if (a, h) == (1, 0):
-                prepare_weight("w2", 0)
-                prepare_weight("w3", 0)
-        quantise_field()
-        rows = [(a, t) for a in range(2) for t in range(PACK)]
+        core_products(0, 0, range(4))
+        core_features(0, 0, {1: lambda: prepare_weight("w3", 0), 2: lambda: prepare_weight("w2", 0)})
+        core_products(0, 1, range(3))
         edge_features(0, 0)
         edge_features(0, 1)
-        prepare_weight("w2", 1)
-        prepare_weight("w3", 1)
-        for n in range(2, 8):
-            edge_features(*rows[n])
-            round_page(*rows[n - 2], both)
-            if n in (5, 6):
-                for c in (2 * n - 10, 2 * n - 9):
-                    weave_z(0, c, nc.scalar.copy, every)
-                    quantise_z(0, c)
+        core_products(0, 1, range(3, 4))
+        core_features(0, 1, {1: lambda: prepare_weight("w3", 1), 2: lambda: prepare_weight("w2", 1)})
+        edge_features(0, 2)
+        edge_features(0, 3)
+        core_products(1, 0, range(4))
+        core_features(1, 0, {})
+        edge_features(1, 0)
+        edge_features(1, 1)
+        round_page(0, 0, both)
+        round_page(0, 1, both)
+        core_products(1, 1, range(4))
+        core_features(1, 1, {})
+        round_page(0, 2, both)
+        round_page(0, 3, both)
+        for c in range(4):
+            if c >= 2:
+                edge_features(1, c)
+            weave_z(0, c, nc.scalar.copy, every)
+            quantise_z(0, c)
+        round_page(1, 0, both)
+        round_page(1, 1, both)
         for c in range(4):
             project(0, c)
         for c in range(2):

@@ -43,7 +43,7 @@ def tile_list_stellarator_mode_weave_kernel(
             return ring.tile(shape, dtype, name=name, tag="page", bufs=8, align_bytes=64)
 
         def bank(tag, name):
-            return psum.tile([P, BANK], F32, name=name, tag=tag, bufs={"bt": 2, "act": 2, "num": 4}[tag])
+            return psum.tile([P, BANK], F32, name=name, tag=tag, bufs={"bt": 3, "act": 2, "num": 3}[tag])
 
         lists = [held([P, S // 16], U16, "list%d" % i) for i in range(4)]
         idx, idx2, idx3, idx4 = lists
@@ -81,7 +81,7 @@ def tile_list_stellarator_mode_weave_kernel(
         def load_words(dst, src):
             nc.sync.dma_start(dst[:].bitcast(I32), src.rearrange("p n i -> p (n i)").bitcast(I32))
 
-        w1_w = [ring.tile([P, 2, 2 * BANK], U8, name="w1_w0", tag="words", bufs=1, align_bytes=64), held([P, 2, 2 * BANK], U8, "w1_w1")]
+        w1_w = [held([P, 2, 2 * BANK], U8, "w1_w0"), held([P, 2, 2 * BANK], U8, "w1_w1")]
 
         def load_w1(a):
             src = w1_words.rearrange("g p c -> p g c")[:, :, 2 * BANK * a : 2 * BANK * (a + 1)]
@@ -111,8 +111,8 @@ def tile_list_stellarator_mode_weave_kernel(
             for q in range(QUADS):
                 nc.sync.dma_start(wg2_sb[t][32 * q : 32 * q + 32, :], rows)
 
-        def load_tab2_scales():
-            for q in range(QUADS):
+        def load_tab2_scales(quads):
+            for q in quads:
                 nc.sync.dma_start(
                     tab2_sc[32 * q : 32 * q + 4, :].bitcast(I32), tab2_scales[0, 4 * q : 4 * q + 4, :].bitcast(I32)
                 )
@@ -121,8 +121,9 @@ def tile_list_stellarator_mode_weave_kernel(
         load_scales(tab_sc, tab_scales, slice(0, T))
         load_w1(0)
         nc.sync.dma_start(wg1_sb[1][:], wg1[:, BANK:S])
+        load_tab2_scales(range(2))
         load_words(tab2_w, tab2_words[0])
-        load_tab2_scales()
+        load_tab2_scales(range(2, QUADS))
         load_scales(w1_sc[0], w1_scales, slice(0, BANK))
 
         neg_log_wg = [held([P, 4, PACK, QUADS, 32], F32, "neg_log_wg%d" % h) for h in range(2)]
@@ -156,10 +157,10 @@ def tile_list_stellarator_mode_weave_kernel(
         load_wg2(1)
         w_raw["w3", 1] = load_raw(big, w3, 1, "w3_raw1")
         w_raw["w2", 1] = load_raw(big, w2, 1, "w2_raw1")
-        load_scales(w1_sc[1], w1_scales, slice(BANK, 2 * BANK))
-        load_w1(1)
         load_wg2(2)
         load_wg2(3)
+        load_scales(w1_sc[1], w1_scales, slice(BANK, 2 * BANK))
+        load_w1(1)
         load_scales(w4_sc, w4_scales, slice(0, N))
 
         v2_sc = held([P, S], U8, "v2_sc")
@@ -262,7 +263,7 @@ def tile_list_stellarator_mode_weave_kernel(
             h2 = edge_slot([P, S], F32, "h2")
             rows = slice(P * t, P * (t + 1))
             for h in range(2):
-                acc = bank("num" if (a, t) >= (1, 2) else "bt", "acc_e")
+                acc = bank("num" if (a, t) == (1, 3) else "bt", "acc_e")
                 cols = slice(BANK * h, BANK * (h + 1))
                 nc.tensor.matmul_mx(
                     out=acc[:], lhsT=q_w["w3"][a][:, rows].bitcast(E4M3), lhsT_scale=q_sc["w3"][a][:, rows],
@@ -281,13 +282,13 @@ def tile_list_stellarator_mode_weave_kernel(
             for c in chunks:
                 half, at = divmod(width * c, 2 * BANK)
                 if (a, half) not in planes:
-                    shape, name = [P, PACK, 2 * BANK], "planes%d%d" % (a, half)
+                    shape, name = [P, 2, 2 * BANK, 2], "planes%d%d" % (a, half)
                     if a == 1:
                         planes[a, half] = ring.tile(shape, BF16, name=name, tag=("b_t", "sq_t")[half], bufs=1, align_bytes=64)
                     else:
                         planes[a, half] = ring.tile(shape, BF16, name=name, tag="planes%d" % half, bufs=1, align_bytes=64)
                 nc.scalar.activation(
-                    planes[a, half][:, t, at : at + width], page(a, t)[:, width * c : width * (c + 1)], ACT.Copy,
+                    planes[a, half][:, t // 2, at : at + width, t % 2], page(a, t)[:, width * c : width * (c + 1)], ACT.Copy,
                     scale=gain_sb[:, a, t : t + 1],
                 )
 
@@ -295,13 +296,14 @@ def tile_list_stellarator_mode_weave_kernel(
 
         z_g = {}
 
-        def weave_z(a, c, copy, lanes):
-            if (a, c) not in z_g:
-                name = "z_g%d%d" % (a, c)
-                z_g[a, c] = edge_slot([P, BANK * PACK], BF16, name) if (a, c) == (1, 3) else grouped(name)
-            src = planes[a, c // 2][:, lanes, BANK * (c % 2) : BANK * (c % 2 + 1)]
-            dst = z_g[a, c][:].rearrange("p (c e i) -> p c i e", e=4, i=PACK)[:, :, lanes, :]
-            copy(dst, src.rearrange("p i (c e) -> p c i e", e=4))
+        def weave_z(a, c, copy):
+            name = "z_g%d%d" % (a, c)
+            z_g[a, c] = edge_slot([P, BANK * PACK], BF16, name) if (a, c) == (0, 3) else grouped(name)
+            words = planes[a, c // 2][:].rearrange("p u c e -> p u (c e)").bitcast(F32)
+            copy(
+                z_g[a, c][:].bitcast(F32).rearrange("p (c u) -> p c u", u=2),
+                words[:, :, BANK * (c % 2) : BANK * (c % 2 + 1)].rearrange("p u c -> p c u"),
+            )
 
         def quantise_z(a, c):
             if a not in z_w:
@@ -313,15 +315,13 @@ def tile_list_stellarator_mode_weave_kernel(
             cols = slice(BANK * c, BANK * (c + 1))
             quantise(z_g[a, c], z_w[a][:, cols], z_sc[a][:, cols])
 
-        w4_w = ring.tile([P, 2, N], U32, name="w4_w", tag="words", bufs=1, align_bytes=64)
-        nc.sync.dma_start(w4_w[:].bitcast(I32), w4_words.rearrange("a p c i -> p a (c i)").bitcast(I32))
         accs = {}
 
         def project(a, c):
             cols = slice(BANK * c, BANK * (c + 1))
             for nt in range(2):
                 if a == 0:
-                    accs[c, nt] = bank(("bt", "act", "num", "num")[c], "acc_o")
+                    accs[c, nt] = bank(("act", "act", "bt", "bt", "bt", "num", "num", "num")[2 * c + nt], "acc_o")
                 rows = slice(P * nt, P * (nt + 1))
                 nc.tensor.matmul_mx(
                     out=accs[c, nt][:], lhsT=w4_w[:, a, rows].bitcast(E4M3), lhsT_scale=w4_sc[:, a, rows],
@@ -329,14 +329,13 @@ def tile_list_stellarator_mode_weave_kernel(
                 )
                 if a == 1:
                     res = small("res") if nt == 0 else ring.tile([P, BANK], F32, name="res", tag="numer", bufs=4)
-                    if c == 2 or (c, nt) == (3, 0):
+                    if (c, nt) in ((2, 1), (3, 0)):
                         nc.vector.tensor_copy(res[:], accs[c, nt][:])
                     else:
                         nc.scalar.copy(res[:], accs[c, nt][:])
                     nc.sync.dma_start(out[rows, cols], res[:])
 
         both = range(2)
-        every, low, high = slice(0, 4), slice(0, 2), slice(2, 4)
         core_products(0, 0, range(4))
         core_features(0, 0, {1: lambda: prepare_weight("w3", 0), 2: lambda: prepare_weight("w2", 0)})
         core_products(0, 1, range(3))
@@ -359,23 +358,20 @@ def tile_list_stellarator_mode_weave_kernel(
         for c in range(4):
             if c >= 2:
                 edge_features(1, c)
-            weave_z(0, c, nc.scalar.copy, every)
+            weave_z(0, c, nc.scalar.copy)
             quantise_z(0, c)
         round_page(1, 0, both)
         round_page(1, 1, both)
+        w4_w = edge_slot([P, 2, N], U32, "w4_w")
+        nc.sync.dma_start(w4_w[:].bitcast(I32), w4_words.rearrange("a p c i -> p a (c i)").bitcast(I32))
         for c in range(4):
             project(0, c)
-        for c in range(2):
-            weave_z(1, c, nc.scalar.copy, low)
         round_page(1, 2, both)
-        for c in range(2, 4):
-            weave_z(1, c, nc.scalar.copy, low)
         round_page(1, 3, range(4), width=BANK)
-        weave_z(1, 3, nc.scalar.copy, high)
-        weave_z(1, 0, nc.vector.tensor_copy, high)
+        weave_z(1, 0, nc.vector.tensor_copy)
         for c in range(4):
-            if c < 2:
-                weave_z(1, c + 1, nc.vector.tensor_copy, high)
+            if c < 3:
+                weave_z(1, c + 1, nc.vector.tensor_copy)
             quantise_z(1, c)
         for c in range(4):
             project(1, c)

@@ -21,6 +21,8 @@ P = 128
 PACK = 4
 BANK = 512
 QUADS = 4
+LIST_COLS = BANK // 16
+BANKS = {"product": 3, "exponent": 2, "numerator": 3}
 
 
 def tile_list_stellarator_mode_weave_kernel(
@@ -30,107 +32,95 @@ def tile_list_stellarator_mode_weave_kernel(
     nc = tc.nc
     with ExitStack() as ctx:
         keep = ctx.enter_context(tc.tile_pool(name="keep", bufs=1))
-        ring = ctx.enter_context(tc.tile_pool(name="ring", bufs=1))
+        shared = ctx.enter_context(tc.tile_pool(name="shared", bufs=1))
         psum = ctx.enter_context(tc.psum_pool(name="psum", bufs=1))
 
         def held(shape, dtype, name):
             return keep.tile(shape, dtype, name=name, align_bytes=64)
 
-        def big(shape, dtype, name):
-            return ring.tile(shape, dtype, name=name, tag="big", bufs=2, align_bytes=64)
+        def placed(place, shape, dtype, name, bufs=1):
+            return shared.tile(shape, dtype, name=name, tag=place, bufs=bufs, align_bytes=64)
 
-        def page_slot(shape, dtype, name):
-            return ring.tile(shape, dtype, name=name, tag="page", bufs=8, align_bytes=64)
+        def bank(role, name):
+            return psum.tile([P, BANK], F32, name=name, tag=role, bufs=BANKS[role])
 
-        def bank(tag, name):
-            return psum.tile([P, BANK], F32, name=name, tag=tag, bufs={"bt": 3, "act": 2, "num": 3}[tag])
+        def factor_tile(name):
+            return placed("factor", [P, BANK], F32, name, bufs=5)
 
-        lists = [held([P, S // 16], U16, "list%d" % i) for i in range(4)]
-        idx, idx2, idx3, idx4 = lists
+        def numerator_tile(name):
+            return placed("numerator", [P, BANK], F32, name, bufs=4)
 
-        tab_sc = ring.tile([P, 2, T], U8, name="tab_sc", tag="sc_a", bufs=1, align_bytes=64)
-        tab2_sc = ring.tile([P, T], U8, name="tab2_sc", tag="sc_b", bufs=1, align_bytes=64)
+        def grouped_tile(name):
+            return placed("grouped", [P, BANK * PACK], BF16, name, bufs=4)
+
+        def page_place(a, t):
+            return "page%d%d" % (a, t)
+
+        idx, idx2, idx3, idx4 = [held([P, S // 16], U16, "list%d" % i) for i in range(4)]
+        tab_sc = placed("z_sc0", [P, 2, T], U8, "tab_sc")
+        tab2_sc = placed("z_sc1", [P, 1, T], U8, "tab2_sc")
         w1_sc = [held([P, 2, BANK], U8, "w1_sc%d" % a) for a in range(2)]
         w4_sc = held([P, 2, N], U8, "w4_sc")
-
-        def clear(engine, planes):
-            engine.memset(planes[:].rearrange("p a c -> p (a c)").bitcast(I32), 0)
-
-        clear(nc.vector, tab_sc)
-        clear(nc.vector, w1_sc[0])
-        nc.vector.memset(tab2_sc[:].bitcast(I32), 0)
-        clear(nc.vector, w1_sc[1])
-        clear(nc.vector, w4_sc)
-
-        def small(name):
-            return ring.tile([P, BANK], F32, name=name, tag="small", bufs=5)
-
-        def edge_slot(shape, dtype, name):
-            return ring.tile(shape, dtype, name=name, tag="h2", bufs=3, align_bytes=64)
+        for planes in (tab_sc, w1_sc[0], tab2_sc, w1_sc[1], w4_sc):
+            nc.vector.memset(planes[:].rearrange("p g c -> p (g c)").bitcast(I32), 0)
+        ident = held([P, P], F32, "ident")
+        make_identity(nc, ident[:])
 
         def load_scales(dst, src, cols):
             for q in range(QUADS):
                 rows = src[:, 4 * q : 4 * q + 4, cols].rearrange("g r c -> r g c")
                 nc.sync.dma_start(dst[32 * q : 32 * q + 4, :, :].bitcast(I32), rows.bitcast(I32))
 
-        ident = held([P, P], F32, "ident")
-        make_identity(nc, ident[:])
-
-        tab_w = [big([P, T], U32, "tab_w%d" % g) for g in range(2)]
-
-        def load_words(dst, src):
-            nc.sync.dma_start(dst[:].bitcast(I32), src.rearrange("p n i -> p (n i)").bitcast(I32))
-
-        w1_w = [held([P, 2, 2 * BANK], U8, "w1_w0"), held([P, 2, 2 * BANK], U8, "w1_w1")]
+        def load_table(place, src, name):
+            words = placed(place, [P, T], U32, name)
+            nc.sync.dma_start(words[:].bitcast(I32), src.rearrange("p n i -> p (n i)").bitcast(I32))
+            return words
 
         def load_w1(a):
+            words = held([P, 2, 2 * BANK], U8, "w1_w%d" % a)
             src = w1_words.rearrange("g p c -> p g c")[:, :, 2 * BANK * a : 2 * BANK * (a + 1)]
-            nc.sync.dma_start(w1_w[a][:].bitcast(I32), src.bitcast(I32))
+            nc.sync.dma_start(words[:].bitcast(I32), src.bitcast(I32))
+            load_scales(w1_sc[a], w1_scales, slice(BANK * a, BANK * (a + 1)))
+            return words
 
-        nc.sync.dma_start(idx[:], offs)
-        load_words(tab_w[0], tab_words[0])
-        for tile_, src in zip(lists[1:], (offs2, offs3, offs4)):
-            nc.sync.dma_start(tile_[:], src)
-        gain_sb = held([P, 2, PACK], F32, "gain_sb")
-        nc.sync.dma_start(gain_sb[:], gain.rearrange("(a p t) -> p a t", a=2, t=PACK))
-        wg1_sb = [small("wg1_sb%d" % h) for h in range(2)]
-        nc.sync.dma_start(wg1_sb[0][:], wg1[:, 0:BANK])
-        load_words(tab_w[1], tab_words[1])
-        def load_raw(pool, src, half, name):
-            raw = pool([P, PACK, BANK], F32, name)
-            nc.sync.dma_start(
-                raw[:], src.rearrange("(p i) c -> p i c", i=PACK)[:, :, BANK * half : BANK * (half + 1)]
-            )
+        def load_raw(place, src, half, name):
+            raw = placed(place, [P, PACK, BANK], F32, name)
+            rows = src.rearrange("(p i) c -> p i c", i=PACK)
+            nc.sync.dma_start(raw[:], rows[:, :, BANK * half : BANK * (half + 1)])
             return raw
 
-        tab2_w = page_slot([P, T], U32, "tab2_w")
-        wg2_sb = [held([P, S], F32, "wg2_sb%d" % t) for t in range(PACK)]
+        def load_wg1(h):
+            half = factor_tile("wg1_sb%d" % h)
+            nc.sync.dma_start(half[:], wg1[:, BANK * h : BANK * (h + 1)])
+            return half
 
         def load_wg2(t):
-            rows = wg2.rearrange("(m t) j -> m t j", t=PACK)[:, t, :]
+            rows = held([P, S], F32, "wg2_sb%d" % t)
             for q in range(QUADS):
-                nc.sync.dma_start(wg2_sb[t][32 * q : 32 * q + 32, :], rows)
+                nc.sync.dma_start(rows[32 * q : 32 * q + 32, :], wg2.rearrange("(m t) j -> m t j", t=PACK)[:, t, :])
+            return rows
 
-        def load_tab2_scales(quads):
-            for q in quads:
-                nc.sync.dma_start(
-                    tab2_sc[32 * q : 32 * q + 4, :].bitcast(I32), tab2_scales[0, 4 * q : 4 * q + 4, :].bitcast(I32)
-                )
-
-        field_raw, w_raw = {}, {}
+        nc.sync.dma_start(idx[:], offs)
+        tab_w = [load_table("z_w1", tab_words[0], "tab_w0")]
+        nc.sync.dma_start(idx2[:], offs2)
+        nc.sync.dma_start(idx3[:], offs3)
+        nc.sync.dma_start(idx4[:], offs4)
+        wg1_sb = [load_wg1(0)]
+        tab_w.append(load_table(page_place(0, 1), tab_words[1], "tab_w1"))
+        wg1_sb.append(load_wg1(1))
         load_scales(tab_sc, tab_scales, slice(0, T))
-        load_w1(0)
-        nc.sync.dma_start(wg1_sb[1][:], wg1[:, BANK:S])
-        load_tab2_scales(range(2))
-        load_words(tab2_w, tab2_words[0])
-        load_tab2_scales(range(2, QUADS))
-        load_scales(w1_sc[0], w1_scales, slice(0, BANK))
+        w1_w = [load_w1(0)]
+        tab2_w = load_table(page_place(1, 0), tab2_words[0], "tab2_w")
+        load_scales(tab2_sc, tab2_scales, slice(0, T))
+        field_raw = [load_raw(page_place(1, 1), field, 0, "field_raw0"), load_raw(page_place(0, 0), field, 1, "field_raw1")]
+        w_raw = {("w3", 0): load_raw(page_place(0, 2), w3, 0, "w3_raw0")}
+        w_raw["w2", 0] = load_raw(page_place(0, 3), w2, 0, "w2_raw0")
 
         neg_log_wg = [held([P, 4, PACK, QUADS, 32], F32, "neg_log_wg%d" % h) for h in range(2)]
         for h in range(2):
-            log_wg = small("log_wg")
+            log_wg = factor_tile("log_wg")
             nc.scalar.activation(log_wg[:], wg1_sb[h][:], ACT.Ln)
-            turned = bank("bt", "turned")
+            turned = bank("product", "turned")
             for jb in range(4):
                 cols = slice(P * jb, P * (jb + 1))
                 nc.tensor.transpose(turned[:, cols], log_wg[:, cols], ident[:])
@@ -140,39 +130,18 @@ def tile_list_stellarator_mode_weave_kernel(
                     neg_log_wg[h][:, jb], src.unsqueeze(2).to_broadcast([P, PACK, QUADS, 32]), ACT.Copy, scale=-1.0
                 )
 
-        v_w = [ring.tile([P, 2, BANK], U32, name="v_w0", tag="planes0", bufs=1, align_bytes=64), held([P, 2, BANK], U32, "v_w1")]
-        v_sc = [ring.tile([P, 2, BANK], U8, name="v_sc0", tag="planes1", bufs=1, align_bytes=64), held([P, 2, BANK], U8, "v_sc1")]
+        v_w = [placed("planes00", [P, 2, BANK], U32, "v_w0"), held([P, 2, BANK], U32, "v_w1")]
+        v_sc = [placed("planes01", [P, 2, BANK], U8, "v_sc0"), held([P, 2, BANK], U8, "v_sc1")]
         for h in range(2):
-            entries = idx[:, 32 * h : 32 * h + 32]
+            entries = idx[:, LIST_COLS * h : LIST_COLS * (h + 1)]
             for g in range(2):
                 nc.vector.tensor_copy(v_w[h][:, g, :], tab_w[g][:].indirect(entries))
             for g in range(2):
                 nc.vector.tensor_copy(v_sc[h][:, g, :], tab_sc[:, g, :].indirect(entries))
-
-        field_raw[0] = load_raw(page_slot, field, 0, "field_raw0")
-        field_raw[1] = load_raw(page_slot, field, 1, "field_raw1")
-        w_raw["w3", 0] = load_raw(page_slot, w3, 0, "w3_raw0")
-        w_raw["w2", 0] = load_raw(page_slot, w2, 0, "w2_raw0")
-        load_wg2(0)
-        load_wg2(1)
-        w_raw["w3", 1] = load_raw(big, w3, 1, "w3_raw1")
-        w_raw["w2", 1] = load_raw(big, w2, 1, "w2_raw1")
-        load_wg2(2)
-        load_wg2(3)
-        load_scales(w1_sc[1], w1_scales, slice(BANK, 2 * BANK))
-        load_w1(1)
-        load_scales(w4_sc, w4_scales, slice(0, N))
-
-        v2_sc = held([P, S], U8, "v2_sc")
         v2_w = held([P, S], U32, "v2_w")
-        nc.vector.tensor_copy(v2_sc[:], tab2_sc[:].indirect(idx2[:]))
+        v2_sc = held([P, S], U8, "v2_sc")
         nc.vector.tensor_copy(v2_w[:], tab2_w[:].indirect(idx2[:]))
-
-        def grouped(name):
-            return ring.tile([P, BANK * PACK], BF16, name=name, tag="grouped", bufs=4, align_bytes=64)
-
-        def quantise(src, words, scales):
-            nc.vector.quantize_mx(out=words.bitcast(E4M3), scales=scales, in_=src[:])
+        nc.vector.tensor_copy(v2_sc[:], tab2_sc[:, 0, :].indirect(idx2[:]))
 
         def weave(copy, dst, planes):
             copy(
@@ -180,44 +149,43 @@ def tile_list_stellarator_mode_weave_kernel(
                 planes.rearrange("p i (c e) -> p c i e", e=4),
             )
 
-        q_w = {name: [held([P, BANK], U32, "q_%s%d" % (name, x)) for x in range(2)] for name in ("w2", "w3")}
+        def quantise(src, words, scales):
+            nc.vector.quantize_mx(out=words.bitcast(E4M3), scales=scales, in_=src[:])
+
+        q_w = {name: [held([P, BANK], U32, "q_%s%d" % (name, x)) for x in range(2)] for name in ("w2", "w3", "field")}
         q_sc = {name: [held([P, BANK], U8, "qs_%s%d" % (name, x)) for x in range(2)] for name in ("w2", "w3", "field")}
-        q_field = held([P, 2, BANK], U32, "q_field")
-        q_w["field"] = [q_field[:, h, :] for h in range(2)]
-
-        def prepare_field(h, copy):
-            g = grouped("field_g%d" % h)
-            weave(copy, g, field_raw[h][:])
-            quantise(g, q_w["field"][h], q_sc["field"][h][:])
-
-        prepare_field(0, nc.vector.tensor_copy)
-        prepare_field(1, nc.vector.tensor_copy)
+        for h in range(2):
+            name = "field_g%d" % h
+            grouped = placed(page_place(0, 1), [P, BANK * PACK], BF16, name) if h == 1 else grouped_tile(name)
+            weave(nc.vector.tensor_copy, grouped, field_raw[h][:])
+            quantise(grouped, q_w["field"][h][:], q_sc["field"][h][:])
 
         def prepare_weight(name, a):
-            g = grouped("%s_g%d" % (name, a))
+            if a == 0:
+                grouped = placed({"w3": "b_t", "w2": "sq_t"}[name], [P, BANK * PACK], BF16, name + "_g0")
+            else:
+                grouped = grouped_tile("%s_g%d" % (name, a))
             nc.scalar.copy(
-                g[:].rearrange("p (t m i) -> p m t i", t=PACK, i=PACK),
+                grouped[:].rearrange("p (t m i) -> p m t i", t=PACK, i=PACK),
                 w_raw[name, a][:].rearrange("p i (m t) -> p m t i", t=PACK),
             )
-            quantise(g, q_w[name][a][:], q_sc[name][a][:])
+            quantise(grouped, q_w[name][a][:], q_sc[name][a][:])
 
-        pages = {}
+        pages, turned_sums = {}, {}
 
         def page(a, t):
             if (a, t) not in pages:
-                pages[a, t] = page_slot([P, T2], F32, "page%d%d" % (a, t))
+                pages[a, t] = placed(page_place(a, t), [P, T2], F32, "page%d%d" % (a, t))
             return pages[a, t]
 
-        state = {}
-
         def core_products(a, h, blocks):
-            if (a, h) not in state:
-                b_t = ring.tile([P, 4, BANK], F32, name="b_t", tag="b_t", bufs=1, align_bytes=64)
-                sq_t = ring.tile([P, 4, BANK], F32, name="sq_t", tag="sq_t", bufs=1, align_bytes=64)
-                state[a, h] = (b_t, sq_t)
-            b_t, sq_t = state[a, h]
+            if (a, h) not in turned_sums:
+                b_t = placed("b_t", [P, 4, BANK], F32, "b_t")
+                sq_t = placed("sq_t", [P, 4, BANK], F32, "sq_t")
+                turned_sums[a, h] = (b_t, sq_t)
+            b_t, sq_t = turned_sums[a, h]
             for jb in blocks:
-                acc = bank("bt", "acc_b")
+                acc = bank("product", "acc_core")
                 cols = slice(P * jb, P * (jb + 1))
                 for g in range(2):
                     nc.tensor.matmul_mx(
@@ -229,45 +197,46 @@ def tile_list_stellarator_mode_weave_kernel(
                         start=(g == 0),
                         stop=(g == 1),
                     )
-                by_slot = acc[:].rearrange("p (m t) -> p t m", t=PACK)
-                nc.scalar.activation(sq_t[:, jb, :].rearrange("p (t m) -> p t m", t=PACK), by_slot, ACT.Square)
-                nc.scalar.copy(b_t[:, jb, :].rearrange("p (t m) -> p t m", t=PACK), by_slot)
+                by_lane = acc[:].rearrange("p (m t) -> p t m", t=PACK)
+                nc.scalar.activation(sq_t[:, jb, :].rearrange("p (t m) -> p t m", t=PACK), by_lane, ACT.Square)
+                nc.scalar.copy(b_t[:, jb, :].rearrange("p (t m) -> p t m", t=PACK), by_lane)
 
-        def core_features(a, h, between):
-            b_t, sq_t = state[a, h]
-            log_t = ring.tile([P, 4, BANK], F32, name="log_t", tag="log_t", bufs=1, align_bytes=64)
+        def turn_and_add(dst, first, second):
+            for jb in range(4):
+                cols = slice(P * jb, P * (jb + 1))
+                nc.tensor.matmul(dst[:, cols], first[:, jb, :], ident[:], start=True, stop=False, is_transpose=True)
+                nc.tensor.matmul(dst[:, cols], second[:, jb, :], ident[:], start=False, stop=True, is_transpose=True)
+
+        def core_features(a, h, after_lane):
+            b_t, sq_t = turned_sums[a, h]
+            log_t = placed("log_t", [P, 4, BANK], F32, "log_t")
             for t in range(PACK):
                 rows = slice(P * t, P * (t + 1))
                 nc.scalar.activation(log_t[:, :, rows], sq_t[:, :, rows], ACT.Ln, bias=1.0)
             for t in range(PACK):
                 rows = slice(P * t, P * (t + 1))
-                logs = bank("act", "logs")
-                num = bank("num", "num")
-                for dst, one, other in (
-                    (logs, lambda jb: log_t[:, jb, rows], lambda jb: neg_log_wg[h][:, jb, t].rearrange("p g m -> p (g m)")),
-                    (num, lambda jb: b_t[:, jb, rows], lambda jb: sq_t[:, jb, rows]),
-                ):
-                    for jb in range(4):
-                        cols = slice(P * jb, P * (jb + 1))
-                        nc.tensor.matmul(dst[:, cols], one(jb), ident[:], start=True, stop=False, is_transpose=True)
-                        nc.tensor.matmul(dst[:, cols], other(jb), ident[:], start=False, stop=True, is_transpose=True)
-                factor = small("factor")
-                nc.scalar.activation(factor[:], logs[:], ACT.Exp, scale=-1.0)
-                numer = ring.tile([P, BANK], F32, name="numer", tag="numer", bufs=4)
-                nc.scalar.copy(numer[:], num[:])
-                nc.vector.tensor_tensor(page(a, t)[:].indirect(idx3[:, 32 * h : 32 * h + 32]), numer[:], factor[:], MULT)
-                if t in between:
-                    between[t]()
+                exponent = bank("exponent", "exponent")
+                turn_and_add(exponent, log_t[:, :, rows], neg_log_wg[h][:, :, t].rearrange("p b g m -> p b (g m)"))
+                num = bank("numerator", "num")
+                turn_and_add(num, b_t[:, :, rows], sq_t[:, :, rows])
+                factor = factor_tile("factor")
+                nc.scalar.activation(factor[:], exponent[:], ACT.Exp, scale=-1.0)
+                numerator = numerator_tile("numerator")
+                nc.scalar.copy(numerator[:], num[:])
+                entries = idx3[:, LIST_COLS * h : LIST_COLS * (h + 1)]
+                nc.vector.tensor_tensor(page(a, t)[:].indirect(entries), numerator[:], factor[:], MULT)
+                if t in after_lane:
+                    prepare_weight(*after_lane[t])
 
         def edge_features(a, t):
-            h2 = edge_slot([P, S], F32, "h2")
+            h2 = placed("w4_w", [P, S], F32, "h2") if (a, t) == (1, 2) else placed("h2", [P, S], F32, "h2", bufs=3)
             rows = slice(P * t, P * (t + 1))
             for h in range(2):
-                acc = bank("num" if (a, t) == (1, 3) else "bt", "acc_e")
+                acc = bank("numerator" if (a, t) == (1, 3) else "product", "acc_edge")
                 cols = slice(BANK * h, BANK * (h + 1))
                 nc.tensor.matmul_mx(
                     out=acc[:], lhsT=q_w["w3"][a][:, rows].bitcast(E4M3), lhsT_scale=q_sc["w3"][a][:, rows],
-                    rhs=q_w["field"][h].bitcast(E4M3), rhs_scale=q_sc["field"][h][:], start=True, stop=False,
+                    rhs=q_w["field"][h][:].bitcast(E4M3), rhs_scale=q_sc["field"][h][:], start=True, stop=False,
                 )
                 nc.tensor.matmul_mx(
                     out=acc[:], lhsT=q_w["w2"][a][:, rows].bitcast(E4M3), lhsT_scale=q_sc["w2"][a][:, rows],
@@ -276,102 +245,103 @@ def tile_list_stellarator_mode_weave_kernel(
                 nc.scalar.activation(h2[:, cols], acc[:], ACT.Tanh)
             nc.vector.tensor_tensor(page(a, t)[:].indirect(idx4[:]), h2[:], wg2_sb[t][:], MULT)
 
-        planes = {}
+        planes, z_g, z_w, z_sc, accs = {}, {}, {}, {}, {}
 
-        def round_page(a, t, chunks, width=2 * BANK):
-            for c in chunks:
-                half, at = divmod(width * c, 2 * BANK)
+        def round_page(a, t, width):
+            for start in range(0, T2, width):
+                half, at = divmod(start, 2 * BANK)
                 if (a, half) not in planes:
-                    shape, name = [P, 2, 2 * BANK, 2], "planes%d%d" % (a, half)
-                    if a == 1:
-                        planes[a, half] = ring.tile(shape, BF16, name=name, tag=("b_t", "sq_t")[half], bufs=1, align_bytes=64)
-                    else:
-                        planes[a, half] = ring.tile(shape, BF16, name=name, tag="planes%d" % half, bufs=1, align_bytes=64)
+                    place = ("planes00", "planes01", "b_t", "sq_t")[2 * a + half]
+                    planes[a, half] = placed(place, [P, PACK * 2 * BANK], BF16, "planes%d%d" % (a, half))
+                if a == 0:
+                    lane = planes[a, half][:].rearrange("p (i c) -> p i c", i=PACK)[:, t, :]
+                else:
+                    lane = planes[a, half][:].rearrange("p (u c e) -> p u c e", u=2, e=2)[:, t // 2, :, t % 2]
                 nc.scalar.activation(
-                    planes[a, half][:, t // 2, at : at + width, t % 2], page(a, t)[:, width * c : width * (c + 1)], ACT.Copy,
+                    lane[:, at : at + width], page(a, t)[:, start : start + width], ACT.Copy,
                     scale=gain_sb[:, a, t : t + 1],
                 )
 
-        z_w, z_sc = {}, {}
-
-        z_g = {}
-
-        def weave_z(a, c, copy):
-            name = "z_g%d%d" % (a, c)
-            z_g[a, c] = edge_slot([P, BANK * PACK], BF16, name) if (a, c) == (0, 3) else grouped(name)
-            words = planes[a, c // 2][:].rearrange("p u c e -> p u (c e)").bitcast(F32)
-            copy(
-                z_g[a, c][:].bitcast(F32).rearrange("p (c u) -> p c u", u=2),
-                words[:, :, BANK * (c % 2) : BANK * (c % 2 + 1)].rearrange("p u c -> p c u"),
-            )
+        def weave_z(a, c):
+            z_g[a, c] = grouped_tile("z_g%d%d" % (a, c))
+            cols = slice(BANK * (c % 2), BANK * (c % 2 + 1))
+            if a == 0:
+                weave(nc.scalar.copy, z_g[a, c], planes[a, c // 2][:].rearrange("p (i c) -> p i c", i=PACK)[:, :, cols])
+            else:
+                pairs = planes[a, c // 2][:].bitcast(F32).rearrange("p (u c) -> p c u", u=2)
+                nc.vector.tensor_copy(z_g[a, c][:].bitcast(F32).rearrange("p (c u) -> p c u", u=2), pairs[:, cols, :])
 
         def quantise_z(a, c):
             if a not in z_w:
-                if a == 0:
-                    z_w[a] = page_slot([P, T2], U32, "z_w0")
-                else:
-                    z_w[a] = big([P, T2], U32, "z_w1")
-                z_sc[a] = ring.tile([P, T2], U8, name="z_sc%d" % a, tag=("sc_a", "sc_b")[a], bufs=1, align_bytes=64)
+                z_w[a] = placed((page_place(0, 0), "z_w1")[a], [P, T2], U32, "z_w%d" % a)
+                z_sc[a] = placed("z_sc%d" % a, [P, T2], U8, "z_sc%d" % a)
             cols = slice(BANK * c, BANK * (c + 1))
             quantise(z_g[a, c], z_w[a][:, cols], z_sc[a][:, cols])
 
-        accs = {}
+        out_banks = [role for role in ("exponent", "product", "numerator") for copies in range(BANKS[role])]
 
         def project(a, c):
             cols = slice(BANK * c, BANK * (c + 1))
             for nt in range(2):
                 if a == 0:
-                    accs[c, nt] = bank(("act", "act", "bt", "bt", "bt", "num", "num", "num")[2 * c + nt], "acc_o")
+                    accs[c, nt] = bank(out_banks[2 * c + nt], "acc_out")
                 rows = slice(P * nt, P * (nt + 1))
                 nc.tensor.matmul_mx(
                     out=accs[c, nt][:], lhsT=w4_w[:, a, rows].bitcast(E4M3), lhsT_scale=w4_sc[:, a, rows],
                     rhs=z_w[a][:, cols].bitcast(E4M3), rhs_scale=z_sc[a][:, cols], start=(a == 0), stop=(a == 1),
                 )
                 if a == 1:
-                    res = small("res") if nt == 0 else ring.tile([P, BANK], F32, name="res", tag="numer", bufs=4)
+                    res = factor_tile("res") if nt == 0 else numerator_tile("res")
                     if (c, nt) in ((2, 1), (3, 0)):
                         nc.vector.tensor_copy(res[:], accs[c, nt][:])
                     else:
                         nc.scalar.copy(res[:], accs[c, nt][:])
                     nc.sync.dma_start(out[rows, cols], res[:])
 
-        both = range(2)
         core_products(0, 0, range(4))
-        core_features(0, 0, {1: lambda: prepare_weight("w3", 0), 2: lambda: prepare_weight("w2", 0)})
-        core_products(0, 1, range(3))
+        wg2_sb = [load_wg2(0), load_wg2(1)]
+        w_raw["w3", 1] = load_raw(page_place(1, 2), w3, 1, "w3_raw1")
+        w_raw["w2", 1] = load_raw(page_place(1, 3), w2, 1, "w2_raw1")
+        wg2_sb.extend([load_wg2(2), load_wg2(3)])
+        w1_w.append(load_w1(1))
+        gain_sb = held([P, 2, PACK], F32, "gain_sb")
+        nc.sync.dma_start(gain_sb[:], gain.rearrange("(a p t) -> p a t", a=2, t=PACK))
+        load_scales(w4_sc, w4_scales, slice(0, N))
+
+        core_features(0, 0, {1: ("w3", 0), 2: ("w2", 0)})
+        core_products(0, 1, range(1))
         edge_features(0, 0)
         edge_features(0, 1)
-        core_products(0, 1, range(3, 4))
-        core_features(0, 1, {1: lambda: prepare_weight("w3", 1), 2: lambda: prepare_weight("w2", 1)})
+        core_products(0, 1, range(1, 4))
+        core_features(0, 1, {1: ("w3", 1), 2: ("w2", 1)})
         edge_features(0, 2)
         edge_features(0, 3)
         core_products(1, 0, range(4))
         core_features(1, 0, {})
         edge_features(1, 0)
         edge_features(1, 1)
-        round_page(0, 0, both)
-        round_page(0, 1, both)
+        round_page(0, 0, 2 * BANK)
+        round_page(0, 1, 2 * BANK)
         core_products(1, 1, range(4))
         core_features(1, 1, {})
-        round_page(0, 2, both)
-        round_page(0, 3, both)
+        round_page(0, 2, 2 * BANK)
+        round_page(0, 3, 2 * BANK)
         for c in range(4):
             if c >= 2:
                 edge_features(1, c)
-            weave_z(0, c, nc.scalar.copy)
+            weave_z(0, c)
             quantise_z(0, c)
-        round_page(1, 0, both)
-        round_page(1, 1, both)
-        w4_w = edge_slot([P, 2, N], U32, "w4_w")
+        w4_w = placed("w4_w", [P, 2, N], U32, "w4_w")
         nc.sync.dma_start(w4_w[:].bitcast(I32), w4_words.rearrange("a p c i -> p a (c i)").bitcast(I32))
         for c in range(4):
             project(0, c)
-        round_page(1, 2, both)
-        round_page(1, 3, range(4), width=BANK)
-        weave_z(1, 0, nc.vector.tensor_copy)
+        for t in range(3):
+            round_page(1, t, 2 * BANK)
+        round_page(1, 3, BANK)
+        weave_z(1, 0)
         for c in range(4):
             if c < 3:
-                weave_z(1, c + 1, nc.vector.tensor_copy)
+                weave_z(1, c + 1)
             quantise_z(1, c)
         for c in range(4):
             project(1, c)

@@ -57,11 +57,12 @@ def tile_list_stellarator_mode_weave_kernel(
             return "page%d%d" % (a, t)
 
         idx, idx2, idx3, idx4 = [held([P, S // 16], U16, "list%d" % i) for i in range(4)]
-        tab_sc = placed("z_sc0", [P, 2, T], U8, "tab_sc")
+        tab_sc = placed("z_sc0", [P, 1, T], U8, "tab_sc")
         tab2_sc = placed("z_sc1", [P, 1, T], U8, "tab2_sc")
         w1_sc = [held([P, 2, BANK], U8, "w1_sc%d" % a) for a in range(2)]
         w4_sc = held([P, 2, N], U8, "w4_sc")
-        for planes in (tab_sc, w1_sc[0], tab2_sc, w1_sc[1], w4_sc):
+        v_sc1 = held([P, 1, S], U8, "v_sc1")
+        for planes in (tab_sc, w1_sc[0], v_sc1, tab2_sc, w1_sc[1], w4_sc):
             nc.vector.memset(planes[:].rearrange("p g c -> p (g c)").bitcast(I32), 0)
         ident = held([P, P], F32, "ident")
         make_identity(nc, ident[:])
@@ -101,47 +102,57 @@ def tile_list_stellarator_mode_weave_kernel(
             return rows
 
         nc.sync.dma_start(idx[:], offs)
-        tab_w = [load_table("z_w1", tab_words[0], "tab_w0")]
         nc.sync.dma_start(idx2[:], offs2)
-        nc.sync.dma_start(idx3[:], offs3)
-        nc.sync.dma_start(idx4[:], offs4)
+        for r in range(4):
+            rows = tab_scales.rearrange("g (q r) c -> q g r c", r=4)[:, :, r, :]
+            nc.sync.dma_start(tab_sc[r:P:16, 0, :].bitcast(I32), rows.bitcast(I32))
+        tab_w = [load_table("z_w1", tab_words[0], "tab_w0")]
         wg1_sb = [load_wg1(0)]
         tab_w.append(load_table(page_place(0, 1), tab_words[1], "tab_w1"))
-        wg1_sb.append(load_wg1(1))
-        load_scales(tab_sc, tab_scales, slice(0, T))
         w1_w = [load_w1(0)]
-        tab2_w = load_table(page_place(1, 0), tab2_words[0], "tab2_w")
+        wg1_sb.append(load_wg1(1))
         load_scales(tab2_sc, tab2_scales, slice(0, T))
+        tab2_w = load_table(page_place(1, 0), tab2_words[0], "tab2_w")
+        nc.sync.dma_start(idx3[:], offs3)
+        nc.sync.dma_start(idx4[:], offs4)
         field_raw = [load_raw(page_place(1, 1), field, 0, "field_raw0"), load_raw(page_place(0, 0), field, 1, "field_raw1")]
         w_raw = {("w3", 0): load_raw(page_place(0, 2), w3, 0, "w3_raw0")}
         w_raw["w2", 0] = load_raw(page_place(0, 3), w2, 0, "w2_raw0")
 
         neg_log_wg = [held([P, 4, PACK, QUADS, 32], F32, "neg_log_wg%d" % h) for h in range(2)]
-        for h in range(2):
-            log_wg = factor_tile("log_wg")
-            nc.scalar.activation(log_wg[:], wg1_sb[h][:], ACT.Ln)
-            turned = bank("product", "turned")
+        log_wg = {}
+
+        def take_log_wg(h):
+            log_wg[h] = factor_tile("log_wg")
+            nc.scalar.activation(log_wg[h][:], wg1_sb[h][:], ACT.Ln)
+
+        def turn_log_wg(h, role):
+            turned = bank(role, "turned")
             for jb in range(4):
                 cols = slice(P * jb, P * (jb + 1))
-                nc.tensor.transpose(turned[:, cols], log_wg[:, cols], ident[:])
+                nc.tensor.transpose(turned[:, cols], log_wg[h][:, cols], ident[:])
             for jb in range(4):
                 src = turned[:, P * jb : P * (jb + 1)].rearrange("p (m t) -> p t m", t=PACK)
                 nc.scalar.activation(
                     neg_log_wg[h][:, jb], src.unsqueeze(2).to_broadcast([P, PACK, QUADS, 32]), ACT.Copy, scale=-1.0
                 )
 
+        take_log_wg(0)
+        turn_log_wg(0, "product")
+
+        v_sc0 = held([P, S], U8, "v_sc0")
+        nc.vector.tensor_copy(v_sc0[:], tab_sc[:, 0, :].indirect(idx[:]))
+        nc.gpsimd.dma_start(v_sc1[0:100, 0, :].bitcast(I32), v_sc0[16:116, :].bitcast(I32))
+        v_sc = [v_sc0[:], v_sc1[:, 0, :]]
         v_w = [placed("planes00", [P, 2, BANK], U32, "v_w0"), held([P, 2, BANK], U32, "v_w1")]
-        v_sc = [placed("planes01", [P, 2, BANK], U8, "v_sc0"), held([P, 2, BANK], U8, "v_sc1")]
-        for h in range(2):
-            entries = idx[:, LIST_COLS * h : LIST_COLS * (h + 1)]
-            for g in range(2):
+        for g in range(2):
+            for h in range(2):
+                entries = idx[:, LIST_COLS * h : LIST_COLS * (h + 1)]
                 nc.vector.tensor_copy(v_w[h][:, g, :], tab_w[g][:].indirect(entries))
-            for g in range(2):
-                nc.vector.tensor_copy(v_sc[h][:, g, :], tab_sc[:, g, :].indirect(entries))
         v2_w = held([P, S], U32, "v2_w")
         v2_sc = held([P, S], U8, "v2_sc")
-        nc.vector.tensor_copy(v2_w[:], tab2_w[:].indirect(idx2[:]))
         nc.vector.tensor_copy(v2_sc[:], tab2_sc[:, 0, :].indirect(idx2[:]))
+        nc.vector.tensor_copy(v2_w[:], tab2_w[:].indirect(idx2[:]))
 
         def weave(copy, dst, planes):
             copy(
@@ -191,7 +202,7 @@ def tile_list_stellarator_mode_weave_kernel(
                     nc.tensor.matmul_mx(
                         out=acc[:],
                         lhsT=v_w[h][:, g, cols].bitcast(E4M3),
-                        lhsT_scale=v_sc[h][:, g, cols],
+                        lhsT_scale=v_sc[g][:, BANK * h + P * jb : BANK * h + P * (jb + 1)],
                         rhs=w1_w[a][:, g, :].bitcast(E2M1),
                         rhs_scale=w1_sc[a][:, g, :],
                         start=(g == 0),
@@ -213,6 +224,8 @@ def tile_list_stellarator_mode_weave_kernel(
             for t in range(PACK):
                 rows = slice(P * t, P * (t + 1))
                 nc.scalar.activation(log_t[:, :, rows], sq_t[:, :, rows], ACT.Ln, bias=1.0)
+            if (a, h) == (0, 0):
+                take_log_wg(1)
             for t in range(PACK):
                 rows = slice(P * t, P * (t + 1))
                 exponent = bank("exponent", "exponent")
@@ -309,6 +322,7 @@ def tile_list_stellarator_mode_weave_kernel(
         load_scales(w4_sc, w4_scales, slice(0, N))
 
         core_features(0, 0, {1: ("w3", 0), 2: ("w2", 0)})
+        turn_log_wg(1, "product")
         core_products(0, 1, range(1))
         edge_features(0, 0)
         edge_features(0, 1)

@@ -22,7 +22,7 @@ PACK = 4
 BANK = 512
 QUADS = 4
 LIST_COLS = BANK // 16
-BANKS = {"product": 3, "exponent": 2, "numerator": 3}
+BANKS = {"product": 4, "exponent": 2, "numerator": 2}
 
 
 def tile_list_stellarator_mode_weave_kernel(
@@ -62,7 +62,8 @@ def tile_list_stellarator_mode_weave_kernel(
         w1_sc = [held([P, 2, BANK], U8, "w1_sc%d" % a) for a in range(2)]
         w4_sc = held([P, 2, N], U8, "w4_sc")
         v_sc1 = held([P, 1, S], U8, "v_sc1")
-        for planes in (tab_sc, w1_sc[0], v_sc1, tab2_sc, w1_sc[1], w4_sc):
+        nc.gpsimd.memset(tab_sc[:, 0, :].bitcast(I32), 0)
+        for planes in (w1_sc[0], v_sc1, tab2_sc, w1_sc[1], w4_sc):
             nc.vector.memset(planes[:].rearrange("p g c -> p (g c)").bitcast(I32), 0)
         ident = held([P, P], F32, "ident")
         make_identity(nc, ident[:])
@@ -81,7 +82,6 @@ def tile_list_stellarator_mode_weave_kernel(
             words = held([P, 2, 2 * BANK], U8, "w1_w%d" % a)
             src = w1_words.rearrange("g p c -> p g c")[:, :, 2 * BANK * a : 2 * BANK * (a + 1)]
             nc.sync.dma_start(words[:].bitcast(I32), src.bitcast(I32))
-            load_scales(w1_sc[a], w1_scales, slice(BANK * a, BANK * (a + 1)))
             return words
 
         def load_raw(place, src, half, name):
@@ -108,15 +108,16 @@ def tile_list_stellarator_mode_weave_kernel(
             nc.sync.dma_start(tab_sc[r:P:16, 0, :].bitcast(I32), rows.bitcast(I32))
         tab_w = [load_table("z_w1", tab_words[0], "tab_w0")]
         wg1_sb = [load_wg1(0)]
+        load_scales(w1_sc[0], w1_scales, slice(0, BANK))
         tab_w.append(load_table(page_place(0, 1), tab_words[1], "tab_w1"))
-        w1_w = [load_w1(0)]
         wg1_sb.append(load_wg1(1))
+        w1_w = [load_w1(0)]
         load_scales(tab2_sc, tab2_scales, slice(0, T))
         tab2_w = load_table(page_place(1, 0), tab2_words[0], "tab2_w")
         nc.sync.dma_start(idx3[:], offs3)
         nc.sync.dma_start(idx4[:], offs4)
         field_raw = [load_raw(page_place(1, 1), field, 0, "field_raw0"), load_raw(page_place(0, 0), field, 1, "field_raw1")]
-        w_raw = {("w3", 0): load_raw(page_place(0, 2), w3, 0, "w3_raw0")}
+        w_raw = {("w3", 0): load_raw("z_w1", w3, 0, "w3_raw0")}
         w_raw["w2", 0] = load_raw(page_place(0, 3), w2, 0, "w2_raw0")
 
         neg_log_wg = [held([P, 4, PACK, QUADS, 32], F32, "neg_log_wg%d" % h) for h in range(2)]
@@ -139,11 +140,15 @@ def tile_list_stellarator_mode_weave_kernel(
 
         take_log_wg(0)
         turn_log_wg(0, "product")
+        take_log_wg(1)
 
         v_sc0 = held([P, S], U8, "v_sc0")
-        nc.vector.tensor_copy(v_sc0[:], tab_sc[:, 0, :].indirect(idx[:]))
-        nc.gpsimd.dma_start(v_sc1[0:100, 0, :].bitcast(I32), v_sc0[16:116, :].bitcast(I32))
         v_sc = [v_sc0[:], v_sc1[:, 0, :]]
+        for h in range(2):
+            cols = slice(BANK * h, BANK * (h + 1))
+            entries = idx[:, LIST_COLS * h : LIST_COLS * (h + 1)]
+            nc.vector.tensor_copy(v_sc0[:, cols], tab_sc[:, 0, :].indirect(entries))
+            nc.gpsimd.dma_start(v_sc1[0:100, 0, cols].bitcast(I32), v_sc0[16:116, cols].bitcast(I32))
         v_w = [placed("planes00", [P, 2, BANK], U32, "v_w0"), held([P, 2, BANK], U32, "v_w1")]
         for g in range(2):
             for h in range(2):
@@ -189,6 +194,21 @@ def tile_list_stellarator_mode_weave_kernel(
                 pages[a, t] = placed(page_place(a, t), [P, T2], F32, "page%d%d" % (a, t))
             return pages[a, t]
 
+        def core_product(a, h, jb, role):
+            acc = bank(role, "acc_core")
+            cols = slice(P * jb, P * (jb + 1))
+            for g in range(2):
+                nc.tensor.matmul_mx(
+                    out=acc[:],
+                    lhsT=v_w[h][:, g, cols].bitcast(E4M3),
+                    lhsT_scale=v_sc[g][:, BANK * h + P * jb : BANK * h + P * (jb + 1)],
+                    rhs=w1_w[a][:, g, :].bitcast(E2M1),
+                    rhs_scale=w1_sc[a][:, g, :],
+                    start=(g == 0),
+                    stop=(g == 1),
+                )
+            return acc[:].rearrange("p (m t) -> p t m", t=PACK)
+
         def core_products(a, h, blocks):
             if (a, h) not in turned_sums:
                 b_t = placed("b_t", [P, 4, BANK], F32, "b_t")
@@ -196,19 +216,7 @@ def tile_list_stellarator_mode_weave_kernel(
                 turned_sums[a, h] = (b_t, sq_t)
             b_t, sq_t = turned_sums[a, h]
             for jb in blocks:
-                acc = bank("product", "acc_core")
-                cols = slice(P * jb, P * (jb + 1))
-                for g in range(2):
-                    nc.tensor.matmul_mx(
-                        out=acc[:],
-                        lhsT=v_w[h][:, g, cols].bitcast(E4M3),
-                        lhsT_scale=v_sc[g][:, BANK * h + P * jb : BANK * h + P * (jb + 1)],
-                        rhs=w1_w[a][:, g, :].bitcast(E2M1),
-                        rhs_scale=w1_sc[a][:, g, :],
-                        start=(g == 0),
-                        stop=(g == 1),
-                    )
-                by_lane = acc[:].rearrange("p (m t) -> p t m", t=PACK)
+                by_lane = core_product(a, h, jb, "product")
                 nc.scalar.activation(sq_t[:, jb, :].rearrange("p (t m) -> p t m", t=PACK), by_lane, ACT.Square)
                 nc.scalar.copy(b_t[:, jb, :].rearrange("p (t m) -> p t m", t=PACK), by_lane)
 
@@ -224,8 +232,6 @@ def tile_list_stellarator_mode_weave_kernel(
             for t in range(PACK):
                 rows = slice(P * t, P * (t + 1))
                 nc.scalar.activation(log_t[:, :, rows], sq_t[:, :, rows], ACT.Ln, bias=1.0)
-            if (a, h) == (0, 0):
-                take_log_wg(1)
             for t in range(PACK):
                 rows = slice(P * t, P * (t + 1))
                 exponent = bank("exponent", "exponent")
@@ -236,6 +242,41 @@ def tile_list_stellarator_mode_weave_kernel(
                 nc.scalar.activation(factor[:], exponent[:], ACT.Exp, scale=-1.0)
                 numerator = numerator_tile("numerator")
                 nc.scalar.copy(numerator[:], num[:])
+                entries = idx3[:, LIST_COLS * h : LIST_COLS * (h + 1)]
+                nc.vector.tensor_tensor(page(a, t)[:].indirect(entries), numerator[:], factor[:], MULT)
+                if t in after_lane:
+                    prepare_weight(*after_lane[t])
+
+        def first_core_step(after_lane):
+            b_t = placed("b_t", [P, 4, BANK], F32, "b_t")
+            sq_t = placed("sq_t", [P, 4, BANK], F32, "sq_t")
+            log_t = placed("log_t", [P, 4, BANK], F32, "log_t")
+            sums = []
+            for jb in range(4):
+                sums.append(core_product(0, 0, jb, "product"))
+                nc.scalar.activation(sq_t[:, jb, :].rearrange("p (t m) -> p t m", t=PACK), sums[jb], ACT.Square)
+                nc.scalar.activation(log_t[:, jb, :], sq_t[:, jb, :], ACT.Ln, bias=1.0)
+
+
+            def copy_lane(t):
+                for jb in range(4):
+                    nc.scalar.copy(b_t[:, jb, P * t : P * (t + 1)], sums[jb][:, t, :])
+
+            copy_lane(0)
+            for t in range(PACK):
+                a, h = 0, 0
+                rows = slice(P * t, P * (t + 1))
+                exponent = bank("exponent", "exponent")
+                turn_and_add(exponent, log_t[:, :, rows], neg_log_wg[h][:, :, t].rearrange("p b g m -> p b (g m)"))
+                num = bank("numerator", "num")
+                turn_and_add(num, b_t[:, :, rows], sq_t[:, :, rows])
+                factor = factor_tile("factor")
+                nc.scalar.activation(factor[:], exponent[:], ACT.Exp, scale=-1.0)
+                numerator = numerator_tile("numerator")
+                nc.scalar.copy(numerator[:], num[:])
+                if t == 0:
+                    for later in range(1, PACK):
+                        copy_lane(later)
                 entries = idx3[:, LIST_COLS * h : LIST_COLS * (h + 1)]
                 nc.vector.tensor_tensor(page(a, t)[:].indirect(entries), numerator[:], factor[:], MULT)
                 if t in after_lane:
@@ -311,17 +352,17 @@ def tile_list_stellarator_mode_weave_kernel(
                         nc.scalar.copy(res[:], accs[c, nt][:])
                     nc.sync.dma_start(out[rows, cols], res[:])
 
-        core_products(0, 0, range(4))
         wg2_sb = [load_wg2(0), load_wg2(1)]
         w_raw["w3", 1] = load_raw(page_place(1, 2), w3, 1, "w3_raw1")
         w_raw["w2", 1] = load_raw(page_place(1, 3), w2, 1, "w2_raw1")
         wg2_sb.extend([load_wg2(2), load_wg2(3)])
         w1_w.append(load_w1(1))
+        load_scales(w1_sc[1], w1_scales, slice(BANK, 2 * BANK))
         gain_sb = held([P, 2, PACK], F32, "gain_sb")
         nc.sync.dma_start(gain_sb[:], gain.rearrange("(a p t) -> p a t", a=2, t=PACK))
         load_scales(w4_sc, w4_scales, slice(0, N))
 
-        core_features(0, 0, {1: ("w3", 0), 2: ("w2", 0)})
+        first_core_step({1: ("w3", 0), 2: ("w2", 0)})
         turn_log_wg(1, "product")
         core_products(0, 1, range(1))
         edge_features(0, 0)

@@ -22,7 +22,7 @@ PACK = 4
 BANK = 512
 QUADS = 4
 LIST_COLS = BANK // 16
-BANKS = {"product": 4, "exponent": 2, "numerator": 2}
+BANKS = {"product": 4, "turned": 4}
 
 
 def tile_list_stellarator_mode_weave_kernel(
@@ -226,26 +226,36 @@ def tile_list_stellarator_mode_weave_kernel(
                 nc.tensor.matmul(dst[:, cols], first[:, jb, :], ident[:], start=True, stop=False, is_transpose=True)
                 nc.tensor.matmul(dst[:, cols], second[:, jb, :], ident[:], start=False, stop=True, is_transpose=True)
 
-        def core_features(a, h, after_lane):
+        logs, numerators = {}, {}
+
+        def take_logs(a, h, place):
+            sq_t = turned_sums[a, h][1]
+            logs[a, h] = placed(place, [P, 4, BANK], F32, "log_t")
+            for t in range(PACK):
+                rows = slice(P * t, P * (t + 1))
+                nc.scalar.activation(logs[a, h][:, :, rows], sq_t[:, :, rows], ACT.Ln, bias=1.0)
+
+        def make_numerator(a, h, t):
             b_t, sq_t = turned_sums[a, h]
-            log_t = placed("log_t", [P, 4, BANK], F32, "log_t")
+            rows = slice(P * t, P * (t + 1))
+            num = bank("turned", "num")
+            turn_and_add(num, b_t[:, :, rows], sq_t[:, :, rows])
+            numerators[a, h, t] = numerator_tile("numerator")
+            nc.scalar.copy(numerators[a, h, t][:], num[:])
+
+        def core_features(a, h, after_lane):
             for t in range(PACK):
                 rows = slice(P * t, P * (t + 1))
-                nc.scalar.activation(log_t[:, :, rows], sq_t[:, :, rows], ACT.Ln, bias=1.0)
-            for t in range(PACK):
-                rows = slice(P * t, P * (t + 1))
-                exponent = bank("exponent", "exponent")
-                turn_and_add(exponent, log_t[:, :, rows], neg_log_wg[h][:, :, t].rearrange("p b g m -> p b (g m)"))
-                num = bank("numerator", "num")
-                turn_and_add(num, b_t[:, :, rows], sq_t[:, :, rows])
+                exponent = bank("turned", "exponent")
+                turn_and_add(exponent, logs[a, h][:, :, rows], neg_log_wg[h][:, :, t].rearrange("p b g m -> p b (g m)"))
                 factor = factor_tile("factor")
                 nc.scalar.activation(factor[:], exponent[:], ACT.Exp, scale=-1.0)
-                numerator = numerator_tile("numerator")
-                nc.scalar.copy(numerator[:], num[:])
+                if (a, h, t) not in numerators:
+                    make_numerator(a, h, t)
                 entries = idx3[:, LIST_COLS * h : LIST_COLS * (h + 1)]
-                nc.vector.tensor_tensor(page(a, t)[:].indirect(entries), numerator[:], factor[:], MULT)
+                nc.vector.tensor_tensor(page(a, t)[:].indirect(entries), numerators[a, h, t][:], factor[:], MULT)
                 if t in after_lane:
-                    prepare_weight(*after_lane[t])
+                    after_lane[t]()
 
         def first_core_step(after_lane):
             b_t = placed("b_t", [P, 4, BANK], F32, "b_t")
@@ -266,9 +276,9 @@ def tile_list_stellarator_mode_weave_kernel(
             for t in range(PACK):
                 a, h = 0, 0
                 rows = slice(P * t, P * (t + 1))
-                exponent = bank("exponent", "exponent")
+                exponent = bank("turned", "exponent")
                 turn_and_add(exponent, log_t[:, :, rows], neg_log_wg[h][:, :, t].rearrange("p b g m -> p b (g m)"))
-                num = bank("numerator", "num")
+                num = bank("turned", "num")
                 turn_and_add(num, b_t[:, :, rows], sq_t[:, :, rows])
                 factor = factor_tile("factor")
                 nc.scalar.activation(factor[:], exponent[:], ACT.Exp, scale=-1.0)
@@ -280,78 +290,105 @@ def tile_list_stellarator_mode_weave_kernel(
                 entries = idx3[:, LIST_COLS * h : LIST_COLS * (h + 1)]
                 nc.vector.tensor_tensor(page(a, t)[:].indirect(entries), numerator[:], factor[:], MULT)
                 if t in after_lane:
-                    prepare_weight(*after_lane[t])
+                    after_lane[t]()
+
+        def edge_sum(a, t, h, role, dst):
+            rows = slice(P * t, P * (t + 1))
+            cols = slice(BANK * h, BANK * (h + 1))
+            acc = bank(role, "acc_edge")
+            nc.tensor.matmul_mx(
+                out=acc[:], lhsT=q_w["w3"][a][:, rows].bitcast(E4M3), lhsT_scale=q_sc["w3"][a][:, rows],
+                rhs=q_w["field"][h][:].bitcast(E4M3), rhs_scale=q_sc["field"][h][:], start=True, stop=False,
+            )
+            nc.tensor.matmul_mx(
+                out=acc[:], lhsT=q_w["w2"][a][:, rows].bitcast(E4M3), lhsT_scale=q_sc["w2"][a][:, rows],
+                rhs=v2_w[:, cols].bitcast(E4M3), rhs_scale=v2_sc[:, cols], start=False, stop=True,
+            )
+            nc.scalar.activation(dst, acc[:], ACT.Tanh)
 
         def edge_features(a, t):
             h2 = placed("w4_w", [P, S], F32, "h2") if (a, t) == (1, 2) else placed("h2", [P, S], F32, "h2", bufs=3)
-            rows = slice(P * t, P * (t + 1))
             for h in range(2):
-                acc = bank("numerator" if (a, t) == (1, 3) else "product", "acc_edge")
-                cols = slice(BANK * h, BANK * (h + 1))
-                nc.tensor.matmul_mx(
-                    out=acc[:], lhsT=q_w["w3"][a][:, rows].bitcast(E4M3), lhsT_scale=q_sc["w3"][a][:, rows],
-                    rhs=q_w["field"][h][:].bitcast(E4M3), rhs_scale=q_sc["field"][h][:], start=True, stop=False,
-                )
-                nc.tensor.matmul_mx(
-                    out=acc[:], lhsT=q_w["w2"][a][:, rows].bitcast(E4M3), lhsT_scale=q_sc["w2"][a][:, rows],
-                    rhs=v2_w[:, cols].bitcast(E4M3), rhs_scale=v2_sc[:, cols], start=False, stop=True,
-                )
-                nc.scalar.activation(h2[:, cols], acc[:], ACT.Tanh)
+                edge_sum(a, t, h, "product", h2[:, BANK * h : BANK * (h + 1)])
             nc.vector.tensor_tensor(page(a, t)[:].indirect(idx4[:]), h2[:], wg2_sb[t][:], MULT)
+
+        def last_edge_half(h, h2):
+            edge_sum(1, PACK - 1, h, "turned", h2)
+            entries = idx4[:, LIST_COLS * h : LIST_COLS * (h + 1)]
+            weights = wg2_sb[PACK - 1][:, BANK * h : BANK * (h + 1)]
+            nc.vector.tensor_tensor(page(1, PACK - 1)[:].indirect(entries), h2, weights, MULT)
 
         planes, z_g, z_w, z_sc, accs = {}, {}, {}, {}, {}
 
-        def round_page(a, t, width):
-            for start in range(0, T2, width):
-                half, at = divmod(start, 2 * BANK)
-                if (a, half) not in planes:
-                    place = ("planes00", "planes01", "b_t", "sq_t")[2 * a + half]
-                    planes[a, half] = placed(place, [P, PACK * 2 * BANK], BF16, "planes%d%d" % (a, half))
-                if a == 0:
-                    lane = planes[a, half][:].rearrange("p (i c) -> p i c", i=PACK)[:, t, :]
-                else:
-                    lane = planes[a, half][:].rearrange("p (u c e) -> p u c e", u=2, e=2)[:, t // 2, :, t % 2]
-                nc.scalar.activation(
-                    lane[:, at : at + width], page(a, t)[:, start : start + width], ACT.Copy,
-                    scale=gain_sb[:, a, t : t + 1],
-                )
-
-        def weave_z(a, c):
-            z_g[a, c] = grouped_tile("z_g%d%d" % (a, c))
-            cols = slice(BANK * (c % 2), BANK * (c % 2 + 1))
+        def lane_of(a, t, half):
+            if (a, half) not in planes:
+                place = ("planes00", "planes01", "b_t", "sq_t")[2 * a + half]
+                planes[a, half] = placed(place, [P, PACK * 2 * BANK], BF16, "planes%d%d" % (a, half))
             if a == 0:
-                weave(nc.scalar.copy, z_g[a, c], planes[a, c // 2][:].rearrange("p (i c) -> p i c", i=PACK)[:, :, cols])
-            else:
-                pairs = planes[a, c // 2][:].bitcast(F32).rearrange("p (u c) -> p c u", u=2)
-                nc.vector.tensor_copy(z_g[a, c][:].bitcast(F32).rearrange("p (c u) -> p c u", u=2), pairs[:, cols, :])
+                return planes[a, half][:].rearrange("p (i c) -> p i c", i=PACK)[:, t, :]
+            return planes[a, half][:].rearrange("p (u c e) -> p u c e", u=2, e=2)[:, t // 2, :, t % 2]
 
-        def quantise_z(a, c):
+        def round_cols(a, t, start, width, factor=None, on_vector=False):
+            half, at = divmod(start, 2 * BANK)
+            dst = lane_of(a, t, half)[:, at : at + width]
+            src = page(a, t)[:, start : start + width]
+            factor = gain_sb[:, a, t : t + 1] if factor is None else factor
+            if on_vector:
+                nc.vector.tensor_scalar(dst, src, factor, None, MULT)
+            else:
+                nc.scalar.activation(dst, src, ACT.Copy, scale=factor)
+
+        def round_page(a, t):
+            for half in range(2):
+                round_cols(a, t, 2 * BANK * half, 2 * BANK)
+
+        def weave_z(a, start, width):
+            grouped = grouped_tile("z_g")
+            z_g[a, start] = grouped[:, 0 : PACK * width]
+            half, at = divmod(start, 2 * BANK)
+            cols = slice(at, at + width)
+            if a == 0:
+                weave(nc.scalar.copy, grouped, planes[a, half][:].rearrange("p (i c) -> p i c", i=PACK)[:, :, cols])
+            else:
+                pairs = planes[a, half][:].bitcast(F32).rearrange("p (u c) -> p c u", u=2)
+                words = z_g[a, start].bitcast(F32).rearrange("p (c u) -> p c u", u=2)
+                nc.vector.tensor_copy(words, pairs[:, cols, :])
+
+        def quantise_z(a, start, width):
             if a not in z_w:
                 z_w[a] = placed((page_place(0, 0), "z_w1")[a], [P, T2], U32, "z_w%d" % a)
                 z_sc[a] = placed("z_sc%d" % a, [P, T2], U8, "z_sc%d" % a)
-            cols = slice(BANK * c, BANK * (c + 1))
-            quantise(z_g[a, c], z_w[a][:, cols], z_sc[a][:, cols])
+            cols = slice(start, start + width)
+            nc.vector.quantize_mx(out=z_w[a][:, cols].bitcast(E4M3), scales=z_sc[a][:, cols], in_=z_g[a, start])
 
-        out_banks = [role for role in ("exponent", "product", "numerator") for copies in range(BANKS[role])]
+        out_banks = [role for role in ("product", "turned") for copies in range(BANKS[role])]
 
-        def project(a, c):
-            cols = slice(BANK * c, BANK * (c + 1))
+        def project(a, start, width, on_vector=()):
+            cols = slice(start, start + width)
+            side_by_side = BANK // width
             for nt in range(2):
-                if a == 0:
-                    accs[c, nt] = bank(out_banks[2 * c + nt], "acc_out")
+                key = (start, nt // side_by_side)
+                if key not in accs:
+                    accs[key] = bank(out_banks[len(accs)], "acc_out")
+                at = width * (nt % side_by_side)
                 rows = slice(P * nt, P * (nt + 1))
+                last = a == 1 and (nt + 1) % side_by_side == 0
                 nc.tensor.matmul_mx(
-                    out=accs[c, nt][:], lhsT=w4_w[:, a, rows].bitcast(E4M3), lhsT_scale=w4_sc[:, a, rows],
-                    rhs=z_w[a][:, cols].bitcast(E4M3), rhs_scale=z_sc[a][:, cols], start=(a == 0), stop=(a == 1),
+                    out=accs[key][:, at : at + width],
+                    lhsT=w4_w[:, a, rows].bitcast(E4M3), lhsT_scale=w4_sc[:, a, rows],
+                    rhs=z_w[a][:, cols].bitcast(E4M3), rhs_scale=z_sc[a][:, cols],
+                    start=(a == 0 and at == 0), stop=last,
                 )
-                if a == 1:
-                    res = factor_tile("res") if nt == 0 else numerator_tile("res")
-                    if (c, nt) in ((2, 1), (3, 0)):
-                        nc.vector.tensor_copy(res[:], accs[c, nt][:])
-                    else:
-                        nc.scalar.copy(res[:], accs[c, nt][:])
-                    nc.sync.dma_start(out[rows, cols], res[:])
+                if last:
+                    res = factor_tile("res") if len(stored) % 2 == 0 else numerator_tile("res")
+                    stored.append(key)
+                    copy = nc.vector.tensor_copy if nt in on_vector else nc.scalar.copy
+                    copy(res[:], accs[key][:])
+                    first = nt + 1 - side_by_side
+                    dst = out.rearrange("(n p) c -> p n c", p=P)[:, first : nt + 1, cols]
+                    nc.sync.dma_start(dst, res[:].rearrange("p (n c) -> p n c", n=side_by_side))
 
+        stored = []
         wg2_sb = [load_wg2(0), load_wg2(1)]
         w_raw["w3", 1] = load_raw(page_place(1, 2), w3, 1, "w3_raw1")
         w_raw["w2", 1] = load_raw(page_place(1, 3), w2, 1, "w2_raw1")
@@ -361,42 +398,68 @@ def tile_list_stellarator_mode_weave_kernel(
         gain_sb = held([P, 2, PACK], F32, "gain_sb")
         nc.sync.dma_start(gain_sb[:], gain.rearrange("(a p t) -> p a t", a=2, t=PACK))
         load_scales(w4_sc, w4_scales, slice(0, N))
+        lane_gain = placed("last_h2", [P, 1], F32, "lane_gain")
+        nc.scalar.copy(lane_gain[:], gain_sb[:, 1, 2:3])
 
-        first_core_step({1: ("w3", 0), 2: ("w2", 0)})
+        first_core_step({1: lambda: prepare_weight("w3", 0), 2: lambda: prepare_weight("w2", 0)})
         turn_log_wg(1, "product")
         core_products(0, 1, range(1))
         edge_features(0, 0)
         edge_features(0, 1)
         core_products(0, 1, range(1, 4))
-        core_features(0, 1, {1: ("w3", 1), 2: ("w2", 1)})
+        take_logs(0, 1, "log_t")
+        core_features(0, 1, {1: lambda: prepare_weight("w3", 1), 2: lambda: prepare_weight("w2", 1)})
         edge_features(0, 2)
         edge_features(0, 3)
-        core_products(1, 0, range(4))
-        core_features(1, 0, {})
         edge_features(1, 0)
-        edge_features(1, 1)
-        round_page(0, 0, 2 * BANK)
-        round_page(0, 1, 2 * BANK)
+        core_products(1, 0, range(4))
+        take_logs(1, 0, "log_t")
+        for t in range(PACK):
+            make_numerator(1, 0, t)
         core_products(1, 1, range(4))
-        core_features(1, 1, {})
-        round_page(0, 2, 2 * BANK)
-        round_page(0, 3, 2 * BANK)
-        for c in range(4):
-            if c >= 2:
-                edge_features(1, c)
-            weave_z(0, c)
-            quantise_z(0, c)
+        take_logs(1, 1, "z_w1")
+        edge_features(1, 1)
+        round_page(0, 0)
+        round_page(0, 1)
+        core_features(1, 0, {})
+        round_page(0, 2)
+        round_page(0, 3)
+
+        def finish_z0(c):
+            weave_z(0, BANK * c, BANK)
+            quantise_z(0, BANK * c, BANK)
+
+        core_features(1, 1, {t: (lambda c=t: finish_z0(c)) for t in range(3)})
+        edge_features(1, 2)
+        finish_z0(3)
+        last_edge_half(0, placed("h2", [P, S], F32, "h2", bufs=3)[:, 0:BANK])
         w4_w = placed("w4_w", [P, 2, N], U32, "w4_w")
         nc.sync.dma_start(w4_w[:].bitcast(I32), w4_words.rearrange("a p c i -> p a (c i)").bitcast(I32))
-        for c in range(4):
-            project(0, c)
-        for t in range(3):
-            round_page(1, t, 2 * BANK)
-        round_page(1, 3, BANK)
-        weave_z(1, 0)
-        for c in range(4):
-            if c < 3:
-                weave_z(1, c + 1)
-            quantise_z(1, c)
-        for c in range(4):
-            project(1, c)
+        round_page(1, 0)
+        round_page(1, 1)
+        round_cols(1, 2, 0, 2 * BANK, factor=lane_gain[:])
+        last_edge_half(1, placed("last_h2", [P, BANK], F32, "last_h2")[:])
+        round_cols(1, 2, 2 * BANK, 2 * BANK)
+        half = BANK // 2
+        chunks = [(0, half), (half, half), (2 * BANK, BANK), (BANK, BANK), (3 * BANK, BANK)]
+        for chunk in chunks:
+            project(0, *chunk)
+        round_cols(1, 3, 2 * BANK, BANK)
+        round_cols(1, 3, 3 * BANK, BANK)
+        for chunk in chunks[:2]:
+            round_cols(1, 3, *chunk, on_vector=True)
+        for chunk in chunks[:2]:
+            weave_z(1, *chunk)
+        for chunk in chunks[:2]:
+            quantise_z(1, *chunk)
+        weave_z(1, *chunks[2])
+        round_cols(1, 3, *chunks[3], on_vector=True)
+        quantise_z(1, *chunks[2])
+        for chunk in chunks[3:]:
+            weave_z(1, *chunk)
+        for chunk in chunks[3:]:
+            quantise_z(1, *chunk)
+        for chunk in chunks[:3]:
+            project(1, *chunk)
+        for chunk in chunks[3:]:
+            project(1, *chunk, on_vector=(1,))

@@ -91,7 +91,7 @@ def tile_list_stellarator_mode_weave_kernel(
             return raw
 
         def load_wg1(h):
-            half = factor_tile("wg1_sb%d" % h)
+            half = factor_tile("wg1_sb0") if h == 0 else held([P, BANK], F32, "wg1_sb1")
             nc.sync.dma_start(half[:], wg1[:, BANK * h : BANK * (h + 1)])
             return half
 
@@ -108,17 +108,16 @@ def tile_list_stellarator_mode_weave_kernel(
             nc.sync.dma_start(tab_sc[r:P:16, 0, :].bitcast(I32), rows.bitcast(I32))
         tab_w = [load_table("z_w1", tab_words[0], "tab_w0")]
         wg1_sb = [load_wg1(0)]
-        load_scales(w1_sc[0], w1_scales, slice(0, BANK))
         tab_w.append(load_table(page_place(0, 1), tab_words[1], "tab_w1"))
-        wg1_sb.append(load_wg1(1))
+        load_scales(w1_sc[0], w1_scales, slice(0, BANK))
         w1_w = [load_w1(0)]
         load_scales(tab2_sc, tab2_scales, slice(0, T))
         tab2_w = load_table(page_place(1, 0), tab2_words[0], "tab2_w")
         nc.sync.dma_start(idx3[:], offs3)
         nc.sync.dma_start(idx4[:], offs4)
-        field_raw = [load_raw(page_place(1, 1), field, 0, "field_raw0"), load_raw(page_place(0, 0), field, 1, "field_raw1")]
+        field_raw = [load_raw(page_place(0, 0), field, 0, "field_raw0"), load_raw(page_place(1, 1), field, 1, "field_raw1")]
         w_raw = {("w3", 0): load_raw("z_w1", w3, 0, "w3_raw0")}
-        w_raw["w2", 0] = load_raw(page_place(0, 3), w2, 0, "w2_raw0")
+        w_raw["w2", 0] = load_raw(page_place(1, 0), w2, 0, "w2_raw0")
 
         neg_log_wg = [held([P, 4, PACK, QUADS, 32], F32, "neg_log_wg%d" % h) for h in range(2)]
         log_wg = {}
@@ -132,15 +131,17 @@ def tile_list_stellarator_mode_weave_kernel(
             for jb in range(4):
                 cols = slice(P * jb, P * (jb + 1))
                 nc.tensor.transpose(turned[:, cols], log_wg[h][:, cols], ident[:])
+            spread_log_wg(h, turned[:].rearrange("p (b m t) -> p b t m", b=4, t=PACK))
+
+        def spread_log_wg(h, by_lane):
             for jb in range(4):
-                src = turned[:, P * jb : P * (jb + 1)].rearrange("p (m t) -> p t m", t=PACK)
+                src = by_lane[:, jb]
                 nc.scalar.activation(
                     neg_log_wg[h][:, jb], src.unsqueeze(2).to_broadcast([P, PACK, QUADS, 32]), ACT.Copy, scale=-1.0
                 )
 
         take_log_wg(0)
         turn_log_wg(0, "product")
-        take_log_wg(1)
 
         v_sc0 = held([P, S], U8, "v_sc0")
         v_sc = [v_sc0[:], v_sc1[:, 0, :]]
@@ -170,22 +171,31 @@ def tile_list_stellarator_mode_weave_kernel(
 
         q_w = {name: [held([P, BANK], U32, "q_%s%d" % (name, x)) for x in range(2)] for name in ("w2", "w3", "field")}
         q_sc = {name: [held([P, BANK], U8, "qs_%s%d" % (name, x)) for x in range(2)] for name in ("w2", "w3", "field")}
-        for h in range(2):
-            name = "field_g%d" % h
-            grouped = placed(page_place(0, 1), [P, BANK * PACK], BF16, name) if h == 1 else grouped_tile(name)
-            weave(nc.vector.tensor_copy, grouped, field_raw[h][:])
-            quantise(grouped, q_w["field"][h][:], q_sc["field"][h][:])
+        pieces = [slice(0, BANK // 2), slice(BANK // 2, BANK)]
+        woven = [placed(page_place(0, 1 + x), [P, BANK * PACK // 2], BF16, "field_g0") for x in range(2)]
+        for x in range(2):
+            weave(nc.vector.tensor_copy, woven[x], field_raw[0][:, :, pieces[x]])
+        for x in range(2):
+            quantise(woven[x], q_w["field"][0][:, pieces[x]], q_sc["field"][0][:, pieces[x]])
 
-        def prepare_weight(name, a):
-            if a == 0:
-                grouped = placed({"w3": "b_t", "w2": "sq_t"}[name], [P, BANK * PACK], BF16, name + "_g0")
+        def prepare_edge_operands():
+            grouped = grouped_tile("field_g1")
+            weave(nc.scalar.copy, grouped, field_raw[1][:])
+            quantise(grouped, q_w["field"][1][:], q_sc["field"][1][:])
+            prepare_weight("w3", 0, 0, 2)
+            prepare_weight("w2", 0, 0, 2, page_place(0, 3))
+
+        def prepare_weight(name, a, first=0, lanes=PACK, place=None):
+            if place is None:
+                grouped = grouped_tile("%s_g%d" % (name, a))[:, 0 : P * PACK * lanes]
             else:
-                grouped = grouped_tile("%s_g%d" % (name, a))
+                grouped = placed(place, [P, P * PACK * lanes], BF16, name + "_g0")[:]
             nc.scalar.copy(
-                grouped[:].rearrange("p (t m i) -> p m t i", t=PACK, i=PACK),
-                w_raw[name, a][:].rearrange("p i (m t) -> p m t i", t=PACK),
+                grouped.rearrange("p (t m i) -> p m t i", t=lanes, i=PACK),
+                w_raw[name, a][:].rearrange("p i (m t) -> p m t i", t=PACK)[:, :, first : first + lanes, :],
             )
-            quantise(grouped, q_w[name][a][:], q_sc[name][a][:])
+            cols = slice(P * first, P * (first + lanes))
+            nc.vector.quantize_mx(out=q_w[name][a][:, cols].bitcast(E4M3), scales=q_sc[name][a][:, cols], in_=grouped)
 
         pages, turned_sums = {}, {}
 
@@ -258,10 +268,9 @@ def tile_list_stellarator_mode_weave_kernel(
                     after_lane[t]()
 
         def first_core_step(after_lane):
-            b_t = placed("b_t", [P, 4, BANK], F32, "b_t")
             sq_t = placed("sq_t", [P, 4, BANK], F32, "sq_t")
             log_t = placed("log_t", [P, 4, BANK], F32, "log_t")
-            sums = []
+            sums, b_lanes = [], {}
             for jb in range(4):
                 sums.append(core_product(0, 0, jb, "product"))
                 nc.scalar.activation(sq_t[:, jb, :].rearrange("p (t m) -> p t m", t=PACK), sums[jb], ACT.Square)
@@ -269,8 +278,9 @@ def tile_list_stellarator_mode_weave_kernel(
 
 
             def copy_lane(t):
+                b_lanes[t] = placed("b_t", [P, 4, P], F32, "b_lane")
                 for jb in range(4):
-                    nc.scalar.copy(b_t[:, jb, P * t : P * (t + 1)], sums[jb][:, t, :])
+                    nc.scalar.copy(b_lanes[t][:, jb, :], sums[jb][:, t, :])
 
             copy_lane(0)
             for t in range(PACK):
@@ -279,14 +289,13 @@ def tile_list_stellarator_mode_weave_kernel(
                 exponent = bank("turned", "exponent")
                 turn_and_add(exponent, log_t[:, :, rows], neg_log_wg[h][:, :, t].rearrange("p b g m -> p b (g m)"))
                 num = bank("turned", "num")
-                turn_and_add(num, b_t[:, :, rows], sq_t[:, :, rows])
+                turn_and_add(num, b_lanes[t][:], sq_t[:, :, rows])
                 factor = factor_tile("factor")
                 nc.scalar.activation(factor[:], exponent[:], ACT.Exp, scale=-1.0)
                 numerator = numerator_tile("numerator")
-                nc.scalar.copy(numerator[:], num[:])
-                if t == 0:
-                    for later in range(1, PACK):
-                        copy_lane(later)
+                (nc.vector.tensor_copy if t == 0 else nc.scalar.copy)(numerator[:], num[:])
+                if t < PACK - 1:
+                    copy_lane(t + 1)
                 entries = idx3[:, LIST_COLS * h : LIST_COLS * (h + 1)]
                 nc.vector.tensor_tensor(page(a, t)[:].indirect(entries), numerator[:], factor[:], MULT)
                 if t in after_lane:
@@ -309,7 +318,7 @@ def tile_list_stellarator_mode_weave_kernel(
         def edge_features(a, t):
             h2 = placed("w4_w", [P, S], F32, "h2") if (a, t) == (1, 2) else placed("h2", [P, S], F32, "h2", bufs=3)
             for h in range(2):
-                edge_sum(a, t, h, "product", h2[:, BANK * h : BANK * (h + 1)])
+                edge_sum(a, t, h, "turned" if (a, t) == (1, 3) else "product", h2[:, BANK * h : BANK * (h + 1)])
             nc.vector.tensor_tensor(page(a, t)[:].indirect(idx4[:]), h2[:], wg2_sb[t][:], MULT)
 
         def last_edge_half(h, h2):
@@ -390,6 +399,7 @@ def tile_list_stellarator_mode_weave_kernel(
 
         stored = []
         wg2_sb = [load_wg2(0), load_wg2(1)]
+        wg1_sb.append(load_wg1(1))
         w_raw["w3", 1] = load_raw(page_place(1, 2), w3, 1, "w3_raw1")
         w_raw["w2", 1] = load_raw(page_place(1, 3), w2, 1, "w2_raw1")
         wg2_sb.extend([load_wg2(2), load_wg2(3)])
@@ -398,30 +408,37 @@ def tile_list_stellarator_mode_weave_kernel(
         gain_sb = held([P, 2, PACK], F32, "gain_sb")
         nc.sync.dma_start(gain_sb[:], gain.rearrange("(a p t) -> p a t", a=2, t=PACK))
         load_scales(w4_sc, w4_scales, slice(0, N))
-        lane_gain = placed("last_h2", [P, 1], F32, "lane_gain")
-        nc.scalar.copy(lane_gain[:], gain_sb[:, 1, 2:3])
 
-        first_core_step({1: lambda: prepare_weight("w3", 0), 2: lambda: prepare_weight("w2", 0)})
-        turn_log_wg(1, "product")
-        core_products(0, 1, range(1))
+        first_core_step({2: prepare_edge_operands})
         edge_features(0, 0)
+        prepare_weight("w3", 0, 2, 2, "b_t")
+        prepare_weight("w2", 0, 2, 2, "sq_t")
         edge_features(0, 1)
-        core_products(0, 1, range(1, 4))
-        take_logs(0, 1, "log_t")
-        core_features(0, 1, {1: lambda: prepare_weight("w3", 1), 2: lambda: prepare_weight("w2", 1)})
         edge_features(0, 2)
+        prepare_weight("w3", 1)
+        core_products(0, 1, range(4))
+        turned = bank("product", "turned")
+        for jb in range(4):
+            cols = slice(P * jb, P * (jb + 1))
+            nc.tensor.transpose(turned[:, cols], wg1_sb[1][:, cols], ident[:])
+        log_wg[1] = factor_tile("log_wg")
+        by_lane = log_wg[1][:].rearrange("p (b t m) -> p b t m", b=4, t=PACK)
+        nc.scalar.activation(by_lane, turned[:].rearrange("p (b m t) -> p b t m", b=4, t=PACK), ACT.Ln)
+        take_logs(0, 1, "log_t")
+        spread_log_wg(1, by_lane)
+        core_features(0, 1, {1: lambda: prepare_weight("w2", 1)})
         edge_features(0, 3)
         edge_features(1, 0)
+        edge_features(1, 1)
         core_products(1, 0, range(4))
         take_logs(1, 0, "log_t")
         for t in range(PACK):
             make_numerator(1, 0, t)
         core_products(1, 1, range(4))
         take_logs(1, 1, "z_w1")
-        edge_features(1, 1)
+        core_features(1, 0, {})
         round_page(0, 0)
         round_page(0, 1)
-        core_features(1, 0, {})
         round_page(0, 2)
         round_page(0, 3)
 
@@ -431,35 +448,21 @@ def tile_list_stellarator_mode_weave_kernel(
 
         core_features(1, 1, {t: (lambda c=t: finish_z0(c)) for t in range(3)})
         edge_features(1, 2)
+        edge_features(1, 3)
         finish_z0(3)
-        last_edge_half(0, placed("h2", [P, S], F32, "h2", bufs=3)[:, 0:BANK])
         w4_w = placed("w4_w", [P, 2, N], U32, "w4_w")
         nc.sync.dma_start(w4_w[:].bitcast(I32), w4_words.rearrange("a p c i -> p a (c i)").bitcast(I32))
-        round_page(1, 0)
-        round_page(1, 1)
-        round_cols(1, 2, 0, 2 * BANK, factor=lane_gain[:])
-        last_edge_half(1, placed("last_h2", [P, BANK], F32, "last_h2")[:])
-        round_cols(1, 2, 2 * BANK, 2 * BANK)
-        half = BANK // 2
-        chunks = [(0, half), (half, half), (2 * BANK, BANK), (BANK, BANK), (3 * BANK, BANK)]
+        chunks = [(BANK * c, BANK) for c in range(4)]
         for chunk in chunks:
             project(0, *chunk)
-        round_cols(1, 3, 2 * BANK, BANK)
-        round_cols(1, 3, 3 * BANK, BANK)
-        for chunk in chunks[:2]:
-            round_cols(1, 3, *chunk, on_vector=True)
-        for chunk in chunks[:2]:
-            weave_z(1, *chunk)
-        for chunk in chunks[:2]:
-            quantise_z(1, *chunk)
-        weave_z(1, *chunks[2])
-        round_cols(1, 3, *chunks[3], on_vector=True)
-        quantise_z(1, *chunks[2])
-        for chunk in chunks[3:]:
-            weave_z(1, *chunk)
-        for chunk in chunks[3:]:
-            quantise_z(1, *chunk)
-        for chunk in chunks[:3]:
-            project(1, *chunk)
-        for chunk in chunks[3:]:
-            project(1, *chunk, on_vector=(1,))
+        for t in range(3):
+            round_page(1, t)
+        for chunk in chunks:
+            round_cols(1, 3, *chunk)
+        weave_z(1, *chunks[0])
+        for c in range(4):
+            if c < 3:
+                weave_z(1, *chunks[c + 1])
+            quantise_z(1, *chunks[c])
+        for c in range(4):
+            project(1, *chunks[c], on_vector={2: (1,), 3: (0,)}.get(c, ()))

@@ -115,7 +115,7 @@ def tile_list_stellarator_mode_weave_kernel(
         tab2_w = load_table(page_place(1, 0), tab2_words[0], "tab2_w")
         nc.sync.dma_start(idx3[:], offs3)
         nc.sync.dma_start(idx4[:], offs4)
-        field_raw = [load_raw(page_place(0, 0), field, 0, "field_raw0"), load_raw(page_place(1, 1), field, 1, "field_raw1")]
+        field_raw = [load_raw(page_place(1, 1), field, 0, "field_raw0"), load_raw(page_place(0, 0), field, 1, "field_raw1")]
         w_raw = {("w3", 0): load_raw("z_w1", w3, 0, "w3_raw0")}
         w_raw["w2", 0] = load_raw(page_place(1, 0), w2, 0, "w2_raw0")
 
@@ -171,17 +171,17 @@ def tile_list_stellarator_mode_weave_kernel(
 
         q_w = {name: [held([P, BANK], U32, "q_%s%d" % (name, x)) for x in range(2)] for name in ("w2", "w3", "field")}
         q_sc = {name: [held([P, BANK], U8, "qs_%s%d" % (name, x)) for x in range(2)] for name in ("w2", "w3", "field")}
+        grouped = grouped_tile("field_g0")
+        weave(nc.vector.tensor_copy, grouped, field_raw[0][:])
         pieces = [slice(0, BANK // 2), slice(BANK // 2, BANK)]
-        woven = [placed(page_place(0, 1 + x), [P, BANK * PACK // 2], BF16, "field_g0") for x in range(2)]
+        woven = [placed(page_place(0, 1 + x), [P, BANK * PACK // 2], BF16, "field_g1") for x in range(2)]
+        weave(nc.vector.tensor_copy, woven[0], field_raw[1][:, :, pieces[0]])
+        quantise(grouped, q_w["field"][0][:], q_sc["field"][0][:])
+        weave(nc.vector.tensor_copy, woven[1], field_raw[1][:, :, pieces[1]])
         for x in range(2):
-            weave(nc.vector.tensor_copy, woven[x], field_raw[0][:, :, pieces[x]])
-        for x in range(2):
-            quantise(woven[x], q_w["field"][0][:, pieces[x]], q_sc["field"][0][:, pieces[x]])
+            quantise(woven[x], q_w["field"][1][:, pieces[x]], q_sc["field"][1][:, pieces[x]])
 
         def prepare_edge_operands():
-            grouped = grouped_tile("field_g1")
-            weave(nc.scalar.copy, grouped, field_raw[1][:])
-            quantise(grouped, q_w["field"][1][:], q_sc["field"][1][:])
             prepare_weight("w3", 0, 0, 2)
             prepare_weight("w2", 0, 0, 2, page_place(0, 3))
 
@@ -293,7 +293,7 @@ def tile_list_stellarator_mode_weave_kernel(
                 factor = factor_tile("factor")
                 nc.scalar.activation(factor[:], exponent[:], ACT.Exp, scale=-1.0)
                 numerator = numerator_tile("numerator")
-                (nc.vector.tensor_copy if t == 0 else nc.scalar.copy)(numerator[:], num[:])
+                nc.scalar.copy(numerator[:], num[:])
                 if t < PACK - 1:
                     copy_lane(t + 1)
                 entries = idx3[:, LIST_COLS * h : LIST_COLS * (h + 1)]
@@ -410,9 +410,9 @@ def tile_list_stellarator_mode_weave_kernel(
         load_scales(w4_sc, w4_scales, slice(0, N))
 
         first_core_step({2: prepare_edge_operands})
-        edge_features(0, 0)
         prepare_weight("w3", 0, 2, 2, "b_t")
         prepare_weight("w2", 0, 2, 2, "sq_t")
+        edge_features(0, 0)
         edge_features(0, 1)
         edge_features(0, 2)
         prepare_weight("w3", 1)

@@ -69,9 +69,9 @@ def tile_list_stellarator_mode_weave_kernel(
         make_identity(nc, ident[:])
 
         def load_scales(dst, src, cols):
-            for q in range(QUADS):
-                rows = src[:, 4 * q : 4 * q + 4, cols].rearrange("g r c -> r g c")
-                nc.sync.dma_start(dst[32 * q : 32 * q + 4, :, :].bitcast(I32), rows.bitcast(I32))
+            for r in range(4):
+                rows = src.rearrange("g (q r) c -> q r g c", r=4)[:, r, :, cols]
+                nc.sync.dma_start(dst[r:P:32, :, :].bitcast(I32), rows.bitcast(I32))
 
         def load_table(place, src, name):
             words = placed(place, [P, T], U32, name)

@@ -102,15 +102,15 @@ def tile_list_stellarator_mode_weave_kernel(
             return rows
 
         nc.sync.dma_start(idx[:], offs)
-        nc.sync.dma_start(idx2[:], offs2)
+        wg1_sb = [load_wg1(0)]
         for r in range(4):
             rows = tab_scales.rearrange("g (q r) c -> q g r c", r=4)[:, :, r, :]
             nc.sync.dma_start(tab_sc[r:P:16, 0, :].bitcast(I32), rows.bitcast(I32))
         tab_w = [load_table("z_w1", tab_words[0], "tab_w0")]
-        wg1_sb = [load_wg1(0)]
         tab_w.append(load_table(page_place(0, 1), tab_words[1], "tab_w1"))
         load_scales(w1_sc[0], w1_scales, slice(0, BANK))
         w1_w = [load_w1(0)]
+        nc.sync.dma_start(idx2[:], offs2)
         load_scales(tab2_sc, tab2_scales, slice(0, T))
         tab2_w = load_table(page_place(1, 0), tab2_words[0], "tab2_w")
         nc.sync.dma_start(idx3[:], offs3)
@@ -149,7 +149,7 @@ def tile_list_stellarator_mode_weave_kernel(
             cols = slice(BANK * h, BANK * (h + 1))
             entries = idx[:, LIST_COLS * h : LIST_COLS * (h + 1)]
             nc.vector.tensor_copy(v_sc0[:, cols], tab_sc[:, 0, :].indirect(entries))
-            nc.gpsimd.dma_start(v_sc1[0:100, 0, cols].bitcast(I32), v_sc0[16:116, cols].bitcast(I32))
+            (nc.scalar if h == 0 else nc.gpsimd).dma_start(v_sc1[0:100, 0, cols].bitcast(I32), v_sc0[16:116, cols].bitcast(I32))
         v_w = [placed("planes00", [P, 2, BANK], U32, "v_w0"), held([P, 2, BANK], U32, "v_w1")]
         for g in range(2):
             for h in range(2):

@@ -149,7 +149,9 @@ def tile_list_stellarator_mode_weave_kernel(
             cols = slice(BANK * h, BANK * (h + 1))
             entries = idx[:, LIST_COLS * h : LIST_COLS * (h + 1)]
             nc.vector.tensor_copy(v_sc0[:, cols], tab_sc[:, 0, :].indirect(entries))
-            (nc.scalar if h == 0 else nc.gpsimd).dma_start(v_sc1[0:100, 0, cols].bitcast(I32), v_sc0[16:116, cols].bitcast(I32))
+            for r in range(4):
+                queue = nc.scalar if h == 0 and r % 2 == 1 else nc.gpsimd
+                queue.dma_start(v_sc1[r:P:32, 0, cols].bitcast(I32), v_sc0[16 + r : P : 32, cols].bitcast(I32))
         v_w = [placed("planes00", [P, 2, BANK], U32, "v_w0"), held([P, 2, BANK], U32, "v_w1")]
         for g in range(2):
             for h in range(2):

@@ -33,6 +33,7 @@ def tile_list_stellarator_mode_weave_kernel(
     with ExitStack() as ctx:
         keep = ctx.enter_context(tc.tile_pool(name="keep", bufs=1))
         shared = ctx.enter_context(tc.tile_pool(name="shared", bufs=1))
+        region = ctx.enter_context(tc.tile_pool(name="region", bufs=1))
         psum = ctx.enter_context(tc.psum_pool(name="psum", bufs=1))
 
         def held(shape, dtype, name):
@@ -50,8 +51,8 @@ def tile_list_stellarator_mode_weave_kernel(
         def numerator_tile(name):
             return placed("numerator", [P, BANK], F32, name, bufs=4)
 
-        def grouped_tile(name):
-            return placed("grouped", [P, BANK * PACK], BF16, name, bufs=4)
+        def in_region(quarter, shape, dtype, name):
+            return region.tile(shape, dtype, name=name, align_bytes=64, offset=2 * PACK * BANK * quarter)
 
         def page_place(a, t):
             return "page%d%d" % (a, t)
@@ -152,7 +153,7 @@ def tile_list_stellarator_mode_weave_kernel(
             for r in range(4):
                 queue = nc.scalar if h == 0 and r % 2 == 1 else nc.gpsimd
                 queue.dma_start(v_sc1[r:P:32, 0, cols].bitcast(I32), v_sc0[16 + r : P : 32, cols].bitcast(I32))
-        v_w = [placed("planes00", [P, 2, BANK], U32, "v_w0"), held([P, 2, BANK], U32, "v_w1")]
+        v_w = [placed("planes00", [P, 2, BANK], U32, "v_w0"), in_region(2, [P, 2, BANK], U32, "v_w1")]
         for g in range(2):
             for h in range(2):
                 entries = idx[:, LIST_COLS * h : LIST_COLS * (h + 1)]
@@ -173,7 +174,7 @@ def tile_list_stellarator_mode_weave_kernel(
 
         q_w = {name: [held([P, BANK], U32, "q_%s%d" % (name, x)) for x in range(2)] for name in ("w2", "w3", "field")}
         q_sc = {name: [held([P, BANK], U8, "qs_%s%d" % (name, x)) for x in range(2)] for name in ("w2", "w3", "field")}
-        grouped = grouped_tile("field_g0")
+        grouped = in_region(0, [P, BANK * PACK], BF16, "field_g0")
         weave(nc.vector.tensor_copy, grouped, field_raw[0][:])
         pieces = [slice(0, BANK // 2), slice(BANK // 2, BANK)]
         woven = [placed(page_place(0, 1 + x), [P, BANK * PACK // 2], BF16, "field_g1") for x in range(2)]
@@ -189,7 +190,7 @@ def tile_list_stellarator_mode_weave_kernel(
 
         def prepare_weight(name, a, first=0, lanes=PACK, place=None):
             if place is None:
-                grouped = grouped_tile("%s_g%d" % (name, a))[:, 0 : P * PACK * lanes]
+                grouped = in_region(1 - a if name == "w3" else 3, [P, P * PACK * lanes], BF16, "%s_g%d" % (name, a))[:]
             else:
                 grouped = placed(place, [P, P * PACK * lanes], BF16, name + "_g0")[:]
             nc.scalar.copy(
@@ -223,8 +224,9 @@ def tile_list_stellarator_mode_weave_kernel(
 
         def core_products(a, h, blocks):
             if (a, h) not in turned_sums:
-                b_t = placed("b_t", [P, 4, BANK], F32, "b_t")
-                sq_t = placed("sq_t", [P, 4, BANK], F32, "sq_t")
+                places = ("planes00", "planes01") if (a, h) == (1, 1) else ("b_t", "sq_t")
+                b_t = placed(places[0], [P, 4, BANK], F32, "b_t")
+                sq_t = placed(places[1], [P, 4, BANK], F32, "sq_t")
                 turned_sums[a, h] = (b_t, sq_t)
             b_t, sq_t = turned_sums[a, h]
             for jb in blocks:
@@ -332,11 +334,12 @@ def tile_list_stellarator_mode_weave_kernel(
         planes, z_g, z_w, z_sc, accs = {}, {}, {}, {}, {}
 
         def lane_of(a, t, half):
-            if (a, half) not in planes:
-                place = ("planes00", "planes01", "b_t", "sq_t")[2 * a + half]
-                planes[a, half] = placed(place, [P, PACK * 2 * BANK], BF16, "planes%d%d" % (a, half))
             if a == 0:
-                return planes[a, half][:].rearrange("p (i c) -> p i c", i=PACK)[:, t, :]
+                if 0 not in planes:
+                    planes[0] = in_region(0, [P, PACK * T2], BF16, "planes0")
+                return planes[0][:, T2 * t + 2 * BANK * half : T2 * t + 2 * BANK * (half + 1)]
+            if (a, half) not in planes:
+                planes[a, half] = placed("planes0%d" % half, [P, PACK * 2 * BANK], BF16, "pairs%d" % half)
             return planes[a, half][:].rearrange("p (u c e) -> p u c e", u=2, e=2)[:, t // 2, :, t % 2]
 
         def round_cols(a, t, start, width, factor=None, on_vector=False):
@@ -354,13 +357,16 @@ def tile_list_stellarator_mode_weave_kernel(
                 round_cols(a, t, 2 * BANK * half, 2 * BANK)
 
         def weave_z(a, start, width):
-            grouped = grouped_tile("z_g")
-            z_g[a, start] = grouped[:, 0 : PACK * width]
             half, at = divmod(start, 2 * BANK)
             cols = slice(at, at + width)
             if a == 0:
-                weave(nc.scalar.copy, grouped, planes[a, half][:].rearrange("p (i c) -> p i c", i=PACK)[:, :, cols])
+                grouped = placed(page_place(0, 1 + start // BANK % 3), [P, PACK * width], BF16, "z_g")
+                z_g[a, start] = grouped[:]
+                weave(nc.scalar.copy, grouped, planes[0][:].rearrange("p (i c) -> p i c", i=PACK)[:, :, start : start + width])
             else:
+                if 1 not in z_g:
+                    z_g[1] = in_region(0, [P, PACK * T2], BF16, "z1_g")
+                z_g[a, start] = z_g[1][:, PACK * start : PACK * (start + width)]
                 pairs = planes[a, half][:].bitcast(F32).rearrange("p (u c) -> p c u", u=2)
                 words = z_g[a, start].bitcast(F32).rearrange("p (c u) -> p c u", u=2)
                 nc.vector.tensor_copy(words, pairs[:, cols, :])
@@ -434,8 +440,6 @@ def tile_list_stellarator_mode_weave_kernel(
         edge_features(1, 1)
         core_products(1, 0, range(4))
         take_logs(1, 0, "log_t")
-        for t in range(PACK):
-            make_numerator(1, 0, t)
         core_products(1, 1, range(4))
         take_logs(1, 1, "z_w1")
         core_features(1, 0, {})

@@ -22,6 +22,7 @@ PACK = 4
 BANK = 512
 QUADS = 4
 LIST_COLS = BANK // 16
+UNIT = 256
 BANKS = {"product": 4, "turned": 4}
 
 
@@ -458,17 +459,21 @@ def tile_list_stellarator_mode_weave_kernel(
         finish_z0(3)
         w4_w = placed("w4_w", [P, 2, N], U32, "w4_w")
         nc.sync.dma_start(w4_w[:].bitcast(I32), w4_words.rearrange("a p c i -> p a (c i)").bitcast(I32))
-        chunks = [(BANK * c, BANK) for c in range(4)]
-        for chunk in chunks:
-            project(0, *chunk)
+        units = [(UNIT * u, UNIT) for u in range(T2 // UNIT)]
+        for unit in units:
+            project(0, *unit)
         for t in range(3):
             round_page(1, t)
-        for chunk in chunks:
-            round_cols(1, 3, *chunk)
-        weave_z(1, *chunks[0])
-        for c in range(4):
-            if c < 3:
-                weave_z(1, *chunks[c + 1])
-            quantise_z(1, *chunks[c])
-        for c in range(4):
-            project(1, *chunks[c], on_vector={2: (1,), 3: (0,)}.get(c, ()))
+        ahead = 4
+        for unit in units[:ahead]:
+            round_cols(1, 3, *unit)
+        weave_z(1, *units[0])
+        for u, unit in enumerate(units):
+            if u + 1 < len(units):
+                weave_z(1, *units[u + 1])
+            quantise_z(1, *unit)
+            if u > 0:
+                project(1, *units[u - 1])
+                if u - 1 + ahead < len(units):
+                    round_cols(1, 3, *units[u - 1 + ahead])
+        project(1, *units[-1], on_vector=(1,))

@@ -65,8 +65,9 @@ def tile_list_stellarator_mode_weave_kernel(
         w4_sc = held([P, 2, N], U8, "w4_sc")
         v_sc1 = held([P, 1, S], U8, "v_sc1")
         nc.gpsimd.memset(tab_sc[:, 0, :].bitcast(I32), 0)
-        for planes in (w1_sc[0], v_sc1, tab2_sc, w1_sc[1], w4_sc):
+        for planes in (w1_sc[0], tab2_sc, w1_sc[1], w4_sc):
             nc.vector.memset(planes[:].rearrange("p g c -> p (g c)").bitcast(I32), 0)
+        nc.vector.memset(v_sc1[96:P, 0, :].bitcast(I32), 0)
         ident = held([P, P], F32, "ident")
         make_identity(nc, ident[:])
 
@@ -151,9 +152,8 @@ def tile_list_stellarator_mode_weave_kernel(
             cols = slice(BANK * h, BANK * (h + 1))
             entries = idx[:, LIST_COLS * h : LIST_COLS * (h + 1)]
             nc.vector.tensor_copy(v_sc0[:, cols], tab_sc[:, 0, :].indirect(entries))
-            for r in range(4):
-                queue = nc.scalar if h == 0 and r % 2 == 1 else nc.gpsimd
-                queue.dma_start(v_sc1[r:P:32, 0, cols].bitcast(I32), v_sc0[16 + r : P : 32, cols].bitcast(I32))
+            queue = nc.scalar if h == 0 else nc.gpsimd
+            queue.dma_start(v_sc1[0 : P - 16, 0, cols].bitcast(I32), v_sc0[16:P, cols].bitcast(I32))
         v_w = [placed("planes00", [P, 2, BANK], U32, "v_w0"), in_region(2, [P, 2, BANK], U32, "v_w1")]
         for g in range(2):
             for h in range(2):

@@ -35,6 +35,7 @@ def tile_list_stellarator_mode_weave_kernel(
         keep = ctx.enter_context(tc.tile_pool(name="keep", bufs=1))
         shared = ctx.enter_context(tc.tile_pool(name="shared", bufs=1))
         region = ctx.enter_context(tc.tile_pool(name="region", bufs=1))
+        pair = ctx.enter_context(tc.tile_pool(name="pair", bufs=1))
         psum = ctx.enter_context(tc.psum_pool(name="psum", bufs=1))
 
         def held(shape, dtype, name):
@@ -118,9 +119,15 @@ def tile_list_stellarator_mode_weave_kernel(
         tab2_w = load_table(page_place(1, 0), tab2_words[0], "tab2_w")
         nc.sync.dma_start(idx3[:], offs3)
         nc.sync.dma_start(idx4[:], offs4)
-        field_raw = [load_raw(page_place(1, 1), field, 0, "field_raw0"), load_raw(page_place(0, 0), field, 1, "field_raw1")]
-        w_raw = {("w3", 0): load_raw("z_w1", w3, 0, "w3_raw0")}
-        w_raw["w2", 0] = load_raw(page_place(1, 0), w2, 0, "w2_raw0")
+        field_rows = field.rearrange("(p i) c -> p i c", i=PACK)
+        field_raw = [load_raw(page_place(1, 1), field, 0, "field_raw0")]
+        field_raw.append(placed(page_place(0, 0), [P, PACK, UNIT], F32, "field_raw1"))
+        nc.sync.dma_start(field_raw[1][:], field_rows[:, :, BANK : BANK + UNIT])
+        field_raw.append(in_region(0, [P, PACK, UNIT], F32, "field_raw2"))
+        nc.sync.dma_start(field_raw[2][:], field_rows[:, :, BANK + UNIT :])
+        first_raw = pair.tile([P, 2, PACK, BANK], F32, name="first_raw", align_bytes=64, offset=0)
+        for x, src in enumerate((w3, w2)):
+            nc.sync.dma_start(first_raw[:, x], src.rearrange("(p i) c -> p i c", i=PACK)[:, :, :BANK])
 
         neg_log_wg = [held([P, 4, PACK, QUADS, 32], F32, "neg_log_wg%d" % h) for h in range(2)]
         log_wg = {}
@@ -155,10 +162,16 @@ def tile_list_stellarator_mode_weave_kernel(
             queue = nc.scalar if h == 0 else nc.gpsimd
             queue.dma_start(v_sc1[0 : P - 16, 0, cols].bitcast(I32), v_sc0[16:P, cols].bitcast(I32))
         v_w = [placed("planes00", [P, 2, BANK], U32, "v_w0"), in_region(2, [P, 2, BANK], U32, "v_w1")]
-        for g in range(2):
-            for h in range(2):
-                entries = idx[:, LIST_COLS * h : LIST_COLS * (h + 1)]
-                nc.vector.tensor_copy(v_w[h][:, g, :], tab_w[g][:].indirect(entries))
+        def gather_words(g, start, width):
+            h, at = divmod(start, BANK)
+            entries = idx[:, start // 16 : (start + width) // 16]
+            nc.vector.tensor_copy(v_w[h][:, g, at : at + width], tab_w[g][:].indirect(entries))
+
+        gather_words(0, 0, BANK)
+        gather_words(0, BANK, BANK)
+        gather_words(1, 0, P)
+        gather_words(1, P, BANK - P)
+        gather_words(1, BANK, BANK)
         v2_w = held([P, S], U32, "v2_w")
         v2_sc = held([P, S], U8, "v2_sc")
         nc.vector.tensor_copy(v2_sc[:], tab2_sc[:, 0, :].indirect(idx2[:]))
@@ -175,37 +188,44 @@ def tile_list_stellarator_mode_weave_kernel(
 
         q_w = {name: [held([P, BANK], U32, "q_%s%d" % (name, x)) for x in range(2)] for name in ("w2", "w3", "field")}
         q_sc = {name: [held([P, BANK], U8, "qs_%s%d" % (name, x)) for x in range(2)] for name in ("w2", "w3", "field")}
-        grouped = in_region(0, [P, BANK * PACK], BF16, "field_g0")
-        weave(nc.vector.tensor_copy, grouped, field_raw[0][:])
-        pieces = [slice(0, BANK // 2), slice(BANK // 2, BANK)]
-        woven = [placed(page_place(0, 1 + x), [P, BANK * PACK // 2], BF16, "field_g1") for x in range(2)]
-        weave(nc.vector.tensor_copy, woven[0], field_raw[1][:, :, pieces[0]])
-        quantise(grouped, q_w["field"][0][:], q_sc["field"][0][:])
-        weave(nc.vector.tensor_copy, woven[1], field_raw[1][:, :, pieces[1]])
+        woven = [placed(page_place(0, 2), [P, BANK * PACK], BF16, "field_g0")]
+        woven.append(placed(page_place(0, 1), [P, UNIT * PACK], BF16, "field_g1"))
         for x in range(2):
-            quantise(woven[x], q_w["field"][1][:, pieces[x]], q_sc["field"][1][:, pieces[x]])
+            weave(nc.vector.tensor_copy, woven[x], field_raw[x][:])
+        quantise(woven[0], q_w["field"][0][:], q_sc["field"][0][:])
+        quantise(woven[1], q_w["field"][1][:, :UNIT], q_sc["field"][1][:, :UNIT])
 
-        def prepare_edge_operands():
-            prepare_weight("w3", 0, 0, 2)
-            prepare_weight("w2", 0, 0, 2, page_place(0, 3))
+        def prepare_last_field_quarter():
+            grouped = placed("log_t", [P, UNIT * PACK], BF16, "field_g2")
+            weave(nc.scalar.copy, grouped, field_raw[2][:])
+            quantise(grouped, q_w["field"][1][:, UNIT:], q_sc["field"][1][:, UNIT:])
 
-        def prepare_weight(name, a, first=0, lanes=PACK, place=None):
-            if place is None:
-                grouped = in_region(1 - a if name == "w3" else 3, [P, P * PACK * lanes], BF16, "%s_g%d" % (name, a))[:]
-            else:
-                grouped = placed(place, [P, P * PACK * lanes], BF16, name + "_g0")[:]
+        def prepare_first_weights(first, place):
+            grouped = placed(place, [P, 2, 2 * P * PACK], BF16, "first_g")
             nc.scalar.copy(
-                grouped.rearrange("p (t m i) -> p m t i", t=lanes, i=PACK),
-                w_raw[name, a][:].rearrange("p i (m t) -> p m t i", t=PACK)[:, :, first : first + lanes, :],
+                grouped[:].rearrange("p w (t m i) -> p w m i t", t=2, i=PACK),
+                first_raw[:].rearrange("p w i (m t) -> p w m i t", t=PACK)[:, :, :, :, first : first + 2],
             )
-            cols = slice(P * first, P * (first + lanes))
-            nc.vector.quantize_mx(out=q_w[name][a][:, cols].bitcast(E4M3), scales=q_sc[name][a][:, cols], in_=grouped)
+            cols = slice(P * first, P * (first + 2))
+            for x, name in enumerate(("w3", "w2")):
+                quantise(grouped[:, x], q_w[name][0][:, cols], q_sc[name][0][:, cols])
+
+        def prepare_second_weight(name):
+            grouped = in_region(0 if name == "w3" else 3, [P, BANK * PACK], BF16, name + "_g1")
+            nc.scalar.copy(
+                grouped[:].rearrange("p (t m i) -> p m i t", t=PACK, i=PACK),
+                second_raw[name][:].rearrange("p i (m t) -> p m i t", t=PACK),
+            )
+            quantise(grouped, q_w[name][1][:], q_sc[name][1][:])
 
         pages, turned_sums = {}, {}
 
         def page(a, t):
             if (a, t) not in pages:
-                pages[a, t] = placed(page_place(a, t), [P, T2], F32, "page%d%d" % (a, t))
+                if a == 1 and t >= 2:
+                    pages[a, t] = pair.tile([P, T2], F32, name="page%d%d" % (a, t), align_bytes=64, offset=4 * T2 * (t - 2))
+                else:
+                    pages[a, t] = placed(page_place(a, t), [P, T2], F32, "page%d%d" % (a, t))
             return pages[a, t]
 
         def core_product(a, h, jb, role):
@@ -306,31 +326,27 @@ def tile_list_stellarator_mode_weave_kernel(
                 if t in after_lane:
                     after_lane[t]()
 
-        def edge_sum(a, t, h, role, dst):
+        def edge_sum(a, t, start, width, role, dst):
             rows = slice(P * t, P * (t + 1))
-            cols = slice(BANK * h, BANK * (h + 1))
-            acc = bank(role, "acc_edge")
+            cols = slice(start, start + width)
+            h, at = divmod(start, BANK)
+            part = slice(at, at + width)
+            acc = bank(role, "acc_edge")[:, :width]
             nc.tensor.matmul_mx(
-                out=acc[:], lhsT=q_w["w3"][a][:, rows].bitcast(E4M3), lhsT_scale=q_sc["w3"][a][:, rows],
-                rhs=q_w["field"][h][:].bitcast(E4M3), rhs_scale=q_sc["field"][h][:], start=True, stop=False,
+                out=acc, lhsT=q_w["w3"][a][:, rows].bitcast(E4M3), lhsT_scale=q_sc["w3"][a][:, rows],
+                rhs=q_w["field"][h][:, part].bitcast(E4M3), rhs_scale=q_sc["field"][h][:, part], start=True, stop=False,
             )
             nc.tensor.matmul_mx(
-                out=acc[:], lhsT=q_w["w2"][a][:, rows].bitcast(E4M3), lhsT_scale=q_sc["w2"][a][:, rows],
+                out=acc, lhsT=q_w["w2"][a][:, rows].bitcast(E4M3), lhsT_scale=q_sc["w2"][a][:, rows],
                 rhs=v2_w[:, cols].bitcast(E4M3), rhs_scale=v2_sc[:, cols], start=False, stop=True,
             )
-            nc.scalar.activation(dst, acc[:], ACT.Tanh)
+            nc.scalar.activation(dst, acc, ACT.Tanh)
 
         def edge_features(a, t):
             h2 = placed("w4_w", [P, S], F32, "h2") if (a, t) == (1, 2) else placed("h2", [P, S], F32, "h2", bufs=3)
             for h in range(2):
-                edge_sum(a, t, h, "turned" if (a, t) == (1, 3) else "product", h2[:, BANK * h : BANK * (h + 1)])
+                edge_sum(a, t, BANK * h, BANK, "turned" if (a, t) == (1, 3) else "product", h2[:, BANK * h : BANK * (h + 1)])
             nc.vector.tensor_tensor(page(a, t)[:].indirect(idx4[:]), h2[:], wg2_sb[t][:], MULT)
-
-        def last_edge_half(h, h2):
-            edge_sum(1, PACK - 1, h, "turned", h2)
-            entries = idx4[:, LIST_COLS * h : LIST_COLS * (h + 1)]
-            weights = wg2_sb[PACK - 1][:, BANK * h : BANK * (h + 1)]
-            nc.vector.tensor_tensor(page(1, PACK - 1)[:].indirect(entries), h2, weights, MULT)
 
         planes, z_g, z_w, z_sc, accs = {}, {}, {}, {}, {}
 
@@ -409,8 +425,7 @@ def tile_list_stellarator_mode_weave_kernel(
         stored = []
         wg2_sb = [load_wg2(0), load_wg2(1)]
         wg1_sb.append(load_wg1(1))
-        w_raw["w3", 1] = load_raw(page_place(1, 2), w3, 1, "w3_raw1")
-        w_raw["w2", 1] = load_raw(page_place(1, 3), w2, 1, "w2_raw1")
+        second_raw = {"w3": load_raw("z_w1", w3, 1, "w3_raw1"), "w2": load_raw(page_place(1, 0), w2, 1, "w2_raw1")}
         wg2_sb.extend([load_wg2(2), load_wg2(3)])
         w1_w.append(load_w1(1))
         load_scales(w1_sc[1], w1_scales, slice(BANK, 2 * BANK))
@@ -418,13 +433,13 @@ def tile_list_stellarator_mode_weave_kernel(
         nc.sync.dma_start(gain_sb[:], gain.rearrange("(a p t) -> p a t", a=2, t=PACK))
         load_scales(w4_sc, w4_scales, slice(0, N))
 
-        first_core_step({2: prepare_edge_operands})
-        prepare_weight("w3", 0, 2, 2, "b_t")
-        prepare_weight("w2", 0, 2, 2, "sq_t")
+        first_core_step({2: lambda: prepare_first_weights(0, page_place(0, 3))})
+        prepare_last_field_quarter()
+        prepare_first_weights(2, "b_t")
         edge_features(0, 0)
         edge_features(0, 1)
         edge_features(0, 2)
-        prepare_weight("w3", 1)
+        prepare_second_weight("w3")
         core_products(0, 1, range(4))
         turned = bank("product", "turned")
         for jb in range(4):
@@ -435,7 +450,7 @@ def tile_list_stellarator_mode_weave_kernel(
         nc.scalar.activation(by_lane, turned[:].rearrange("p (b m t) -> p b t m", b=4, t=PACK), ACT.Ln)
         take_logs(0, 1, "log_t")
         spread_log_wg(1, by_lane)
-        core_features(0, 1, {1: lambda: prepare_weight("w2", 1)})
+        core_features(0, 1, {1: lambda: prepare_second_weight("w2")})
         edge_features(0, 3)
         edge_features(1, 0)
         edge_features(1, 1)

@@ -119,12 +119,7 @@ def tile_list_stellarator_mode_weave_kernel(
         tab2_w = load_table(page_place(1, 0), tab2_words[0], "tab2_w")
         nc.sync.dma_start(idx3[:], offs3)
         nc.sync.dma_start(idx4[:], offs4)
-        field_rows = field.rearrange("(p i) c -> p i c", i=PACK)
-        field_raw = [load_raw(page_place(1, 1), field, 0, "field_raw0")]
-        field_raw.append(placed(page_place(0, 0), [P, PACK, UNIT], F32, "field_raw1"))
-        nc.sync.dma_start(field_raw[1][:], field_rows[:, :, BANK : BANK + UNIT])
-        field_raw.append(in_region(0, [P, PACK, UNIT], F32, "field_raw2"))
-        nc.sync.dma_start(field_raw[2][:], field_rows[:, :, BANK + UNIT :])
+        field_raw = [load_raw(page_place(0, 0), field, 0, "field_raw0"), load_raw(page_place(1, 1), field, 1, "field_raw1")]
         first_raw = pair.tile([P, 2, PACK, BANK], F32, name="first_raw", align_bytes=64, offset=0)
         for x, src in enumerate((w3, w2)):
             nc.sync.dma_start(first_raw[:, x], src.rearrange("(p i) c -> p i c", i=PACK)[:, :, :BANK])
@@ -188,17 +183,18 @@ def tile_list_stellarator_mode_weave_kernel(
 
         q_w = {name: [held([P, BANK], U32, "q_%s%d" % (name, x)) for x in range(2)] for name in ("w2", "w3", "field")}
         q_sc = {name: [held([P, BANK], U8, "qs_%s%d" % (name, x)) for x in range(2)] for name in ("w2", "w3", "field")}
-        woven = [placed(page_place(0, 2), [P, BANK * PACK], BF16, "field_g0")]
-        woven.append(placed(page_place(0, 1), [P, UNIT * PACK], BF16, "field_g1"))
-        for x in range(2):
-            weave(nc.vector.tensor_copy, woven[x], field_raw[x][:])
-        quantise(woven[0], q_w["field"][0][:], q_sc["field"][0][:])
-        quantise(woven[1], q_w["field"][1][:, :UNIT], q_sc["field"][1][:, :UNIT])
+        def prepare_first_field_half():
+            pieces = [slice(0, UNIT), slice(UNIT, BANK)]
+            woven = [placed(page_place(0, 1 + x), [P, UNIT * PACK], BF16, "field_g0") for x in range(2)]
+            for x in range(2):
+                weave(nc.vector.tensor_copy, woven[x], field_raw[0][:, :, pieces[x]])
+            for x in range(2):
+                quantise(woven[x], q_w["field"][0][:, pieces[x]], q_sc["field"][0][:, pieces[x]])
 
-        def prepare_last_field_quarter():
-            grouped = placed("log_t", [P, UNIT * PACK], BF16, "field_g2")
-            weave(nc.scalar.copy, grouped, field_raw[2][:])
-            quantise(grouped, q_w["field"][1][:, UNIT:], q_sc["field"][1][:, UNIT:])
+        def prepare_second_field_half():
+            grouped = placed("log_t", [P, BANK * PACK], BF16, "field_g1")
+            weave(nc.scalar.copy, grouped, field_raw[1][:])
+            quantise(grouped, q_w["field"][1][:], q_sc["field"][1][:])
 
         def prepare_first_weights(first, place):
             grouped = placed(place, [P, 2, 2 * P * PACK], BF16, "first_g")
@@ -302,25 +298,32 @@ def tile_list_stellarator_mode_weave_kernel(
                 nc.scalar.activation(log_t[:, jb, :], sq_t[:, jb, :], ACT.Ln, bias=1.0)
 
 
-            def copy_lane(t):
-                b_lanes[t] = placed("b_t", [P, 4, P], F32, "b_lane")
-                for jb in range(4):
-                    nc.scalar.copy(b_lanes[t][:, jb, :], sums[jb][:, t, :])
+            def copy_lanes(copy, dst, first, last, blocks=range(4)):
+                for jb in blocks:
+                    copy(dst[:, jb], sums[jb][:, first:last, :])
 
-            copy_lane(0)
+            first_lane = placed("z_sc1", [P, 4, 1, P], F32, "b_lane0")
+            copy_lanes(nc.vector.tensor_copy, first_lane, 0, 1, range(3))
+            copy_lanes(nc.scalar.copy, first_lane, 0, 1, [3])
+            prepare_first_field_half()
+            b_lanes[0] = first_lane[:, :, 0, :]
             for t in range(PACK):
                 a, h = 0, 0
                 rows = slice(P * t, P * (t + 1))
                 exponent = bank("turned", "exponent")
                 turn_and_add(exponent, log_t[:, :, rows], neg_log_wg[h][:, :, t].rearrange("p b g m -> p b (g m)"))
                 num = bank("turned", "num")
-                turn_and_add(num, b_lanes[t][:], sq_t[:, :, rows])
+                turn_and_add(num, b_lanes[t], sq_t[:, :, rows])
                 factor = factor_tile("factor")
                 nc.scalar.activation(factor[:], exponent[:], ACT.Exp, scale=-1.0)
                 numerator = numerator_tile("numerator")
                 nc.scalar.copy(numerator[:], num[:])
-                if t < PACK - 1:
-                    copy_lane(t + 1)
+                if t == 0:
+                    other_lanes = placed("z_sc1", [P, 4, PACK - 1, P], F32, "b_lanes")
+                    copy_lanes(nc.scalar.copy, other_lanes[:, :, 0:1], 1, 2)
+                    copy_lanes(nc.scalar.copy, other_lanes[:, :, 1:3], 2, PACK)
+                    for lane in range(1, PACK):
+                        b_lanes[lane] = other_lanes[:, :, lane - 1, :]
                 entries = idx3[:, LIST_COLS * h : LIST_COLS * (h + 1)]
                 nc.vector.tensor_tensor(page(a, t)[:].indirect(entries), numerator[:], factor[:], MULT)
                 if t in after_lane:
@@ -425,7 +428,7 @@ def tile_list_stellarator_mode_weave_kernel(
         stored = []
         wg2_sb = [load_wg2(0), load_wg2(1)]
         wg1_sb.append(load_wg1(1))
-        second_raw = {"w3": load_raw("z_w1", w3, 1, "w3_raw1"), "w2": load_raw(page_place(1, 0), w2, 1, "w2_raw1")}
+        second_raw = {"w3": load_raw("z_w1", w3, 1, "w3_raw1"), "w2": load_raw(page_place(1, 1), w2, 1, "w2_raw1")}
         wg2_sb.extend([load_wg2(2), load_wg2(3)])
         w1_w.append(load_w1(1))
         load_scales(w1_sc[1], w1_scales, slice(BANK, 2 * BANK))
@@ -434,7 +437,7 @@ def tile_list_stellarator_mode_weave_kernel(
         load_scales(w4_sc, w4_scales, slice(0, N))
 
         first_core_step({2: lambda: prepare_first_weights(0, page_place(0, 3))})
-        prepare_last_field_quarter()
+        prepare_second_field_half()
         prepare_first_weights(2, "b_t")
         edge_features(0, 0)
         edge_features(0, 1)

@@ -23,6 +23,7 @@ BANK = 512
 QUADS = 4
 LIST_COLS = BANK // 16
 UNIT = 256
+ON_VECTOR = 3
 BANKS = {"product": 4, "turned": 4}
 
 
@@ -482,6 +483,8 @@ def tile_list_stellarator_mode_weave_kernel(
             project(0, *unit)
         for t in range(3):
             round_page(1, t)
+        last_gain = pair.tile([P, 1], F32, name="last_gain", align_bytes=64, offset=0)
+        nc.scalar.copy(last_gain[:], gain_sb[:, 1, PACK - 1 :])
         ahead = 4
         for unit in units[:ahead]:
             round_cols(1, 3, *unit)
@@ -493,5 +496,5 @@ def tile_list_stellarator_mode_weave_kernel(
             if u > 0:
                 project(1, *units[u - 1])
                 if u - 1 + ahead < len(units):
-                    round_cols(1, 3, *units[u - 1 + ahead])
+                    round_cols(1, 3, *units[u - 1 + ahead], factor=last_gain[:], on_vector=u - 1 + ahead >= len(units) - ON_VECTOR)
         project(1, *units[-1], on_vector=(1,))

@@ -23,7 +23,7 @@ BANK = 512
 QUADS = 4
 LIST_COLS = BANK // 16
 UNIT = 256
-ON_VECTOR = 3
+ON_VECTOR = 2
 BANKS = {"product": 4, "turned": 4}
 
 
@@ -401,13 +401,14 @@ def tile_list_stellarator_mode_weave_kernel(
 
         out_banks = [role for role in ("product", "turned") for copies in range(BANKS[role])]
 
-        def project(a, start, width, on_vector=()):
+        def project(a, start, width, halves=(0, 1), apart=False, on_vector=()):
             cols = slice(start, start + width)
-            side_by_side = BANK // width
-            for nt in range(2):
+            side_by_side = 1 if apart else BANK // width
+            filled = side_by_side * width
+            for nt in halves:
                 key = (start, nt // side_by_side)
                 if key not in accs:
-                    accs[key] = bank(out_banks[len(accs)], "acc_out")
+                    accs[key] = bank(out_banks[len(accs) % len(out_banks)], "acc_out")
                 at = width * (nt % side_by_side)
                 rows = slice(P * nt, P * (nt + 1))
                 last = a == 1 and (nt + 1) % side_by_side == 0
@@ -421,10 +422,10 @@ def tile_list_stellarator_mode_weave_kernel(
                     res = factor_tile("res") if len(stored) % 2 == 0 else numerator_tile("res")
                     stored.append(key)
                     copy = nc.vector.tensor_copy if nt in on_vector else nc.scalar.copy
-                    copy(res[:], accs[key][:])
+                    copy(res[:, :filled], accs[key][:, :filled])
                     first = nt + 1 - side_by_side
                     dst = out.rearrange("(n p) c -> p n c", p=P)[:, first : nt + 1, cols]
-                    nc.sync.dma_start(dst, res[:].rearrange("p (n c) -> p n c", n=side_by_side))
+                    nc.sync.dma_start(dst, res[:, :filled].rearrange("p (n c) -> p n c", n=side_by_side))
 
         stored = []
         wg2_sb = [load_wg2(0), load_wg2(1)]
@@ -479,8 +480,9 @@ def tile_list_stellarator_mode_weave_kernel(
         w4_w = placed("w4_w", [P, 2, N], U32, "w4_w")
         nc.sync.dma_start(w4_w[:].bitcast(I32), w4_words.rearrange("a p c i -> p a (c i)").bitcast(I32))
         units = [(UNIT * u, UNIT) for u in range(T2 // UNIT)]
-        for unit in units:
+        for unit in units[:-1]:
             project(0, *unit)
+        project(0, *units[-1], halves=(0,), apart=True)
         for t in range(3):
             round_page(1, t)
         last_gain = pair.tile([P, 1], F32, name="last_gain", align_bytes=64, offset=0)
@@ -495,6 +497,8 @@ def tile_list_stellarator_mode_weave_kernel(
             quantise_z(1, *unit)
             if u > 0:
                 project(1, *units[u - 1])
+                if u == 1:
+                    project(0, *units[-1], halves=(1,), apart=True)
                 if u - 1 + ahead < len(units):
                     round_cols(1, 3, *units[u - 1 + ahead], factor=last_gain[:], on_vector=u - 1 + ahead >= len(units) - ON_VECTOR)
-        project(1, *units[-1], on_vector=(1,))
+        project(1, *units[-1], apart=True, on_vector=(0,))

@@ -497,7 +497,7 @@ def tile_list_stellarator_mode_weave_kernel(
             quantise_z(1, *unit)
             if u > 0:
                 project(1, *units[u - 1])
-                if u == 1:
+                if u == len(units) - 2:
                     project(0, *units[-1], halves=(1,), apart=True)
                 if u - 1 + ahead < len(units):
                     round_cols(1, 3, *units[u - 1 + ahead], factor=last_gain[:], on_vector=u - 1 + ahead >= len(units) - ON_VECTOR)

@@ -419,15 +419,16 @@ def tile_list_stellarator_mode_weave_kernel(
                     start=(a == 0 and at == 0), stop=last,
                 )
                 if last:
-                    res = factor_tile("res") if len(stored) % 2 == 0 else numerator_tile("res")
-                    stored.append(key)
+                    if start not in stored:
+                        stored[start] = factor_tile("res") if len(stored) % 2 == 0 else numerator_tile("res")
+                    res = stored[start]
                     copy = nc.vector.tensor_copy if nt in on_vector else nc.scalar.copy
-                    copy(res[:, :filled], accs[key][:, :filled])
-                    first = nt + 1 - side_by_side
-                    dst = out.rearrange("(n p) c -> p n c", p=P)[:, first : nt + 1, cols]
-                    nc.sync.dma_start(dst, res[:, :filled].rearrange("p (n c) -> p n c", n=side_by_side))
+                    copy(res[:, width * (nt + 1) - filled : width * (nt + 1)], accs[key][:, :filled])
+                    if nt == 1:
+                        dst = out.rearrange("(n p) c -> p n c", p=P)[:, :, cols]
+                        nc.sync.dma_start(dst, res[:].rearrange("p (n c) -> p n c", n=2))
 
-        stored = []
+        stored = {}
         wg2_sb = [load_wg2(0), load_wg2(1)]
         wg1_sb.append(load_wg1(1))
         second_raw = {"w3": load_raw("z_w1", w3, 1, "w3_raw1"), "w2": load_raw(page_place(1, 1), w2, 1, "w2_raw1")}

from contextlib import ExitStack

import concourse.mybir as mybir
from concourse.masks import make_identity

K, K2, H, N, T, S, T2 = 1024, 512, 1024, 256, 2048, 1024, 2048
FLOPS = 2 * K * H * S + 2 * 2 * K2 * H * S + 2 * H * N * T2

F32 = mybir.dt.float32
BF16 = mybir.dt.bfloat16
I32 = mybir.dt.int32
U32 = mybir.dt.uint32
U16 = mybir.dt.uint16
U8 = mybir.dt.uint8
E4M3 = mybir.dt.float8_e4m3fn_x4
E2M1 = mybir.dt.float4_e2m1fn_x4
ACT = mybir.ActivationFunctionType
MULT = mybir.AluOpType.mult

P = 128
PACK = 4
BANK = 512
QUADS = 4
LIST_COLS = BANK // 16
UNIT = 256
ON_VECTOR = 2
BANKS = {"product": 4, "turned": 4}


def tile_list_stellarator_mode_weave_kernel(
    tc, tab_words, tab_scales, tab2_words, tab2_scales, w1_words, w1_scales, w2, w3, field, gain,
    wg1, wg2, w4_words, w4_scales, offs, offs2, offs3, offs4, out,
):
    nc = tc.nc
    with ExitStack() as ctx:
        keep = ctx.enter_context(tc.tile_pool(name="keep", bufs=1))
        shared = ctx.enter_context(tc.tile_pool(name="shared", bufs=1))
        region = ctx.enter_context(tc.tile_pool(name="region", bufs=1))
        pair = ctx.enter_context(tc.tile_pool(name="pair", bufs=1))
        psum = ctx.enter_context(tc.psum_pool(name="psum", bufs=1))

        def held(shape, dtype, name):
            return keep.tile(shape, dtype, name=name, align_bytes=64)

        def placed(place, shape, dtype, name, bufs=1):
            return shared.tile(shape, dtype, name=name, tag=place, bufs=bufs, align_bytes=64)

        def bank(role, name):
            return psum.tile([P, BANK], F32, name=name, tag=role, bufs=BANKS[role])

        def factor_tile(name):
            return placed("factor", [P, BANK], F32, name, bufs=5)

        def numerator_tile(name):
            return placed("numerator", [P, BANK], F32, name, bufs=4)

        def in_region(quarter, shape, dtype, name):
            return region.tile(shape, dtype, name=name, align_bytes=64, offset=2 * PACK * BANK * quarter)

        def page_place(a, t):
            return "page%d%d" % (a, t)

        idx, idx2, idx3, idx4 = [held([P, S // 16], U16, "list%d" % i) for i in range(4)]
        tab_sc = placed("z_sc0", [P, 1, T], U8, "tab_sc")
        tab2_sc = placed("z_sc1", [P, 1, T], U8, "tab2_sc")
        w1_sc = [held([P, 2, BANK], U8, "w1_sc%d" % a) for a in range(2)]
        w4_sc = held([P, 2, N], U8, "w4_sc")
        v_sc1 = held([P, 1, S], U8, "v_sc1")
        nc.gpsimd.memset(tab_sc[:, 0, :].bitcast(I32), 0)
        for planes in (w1_sc[0], tab2_sc, w1_sc[1], w4_sc):
            nc.vector.memset(planes[:].rearrange("p g c -> p (g c)").bitcast(I32), 0)
        nc.vector.memset(v_sc1[96:P, 0, :].bitcast(I32), 0)
        ident = held([P, P], F32, "ident")
        make_identity(nc, ident[:])

        def load_scales(dst, src, cols):
            for r in range(4):
                rows = src.rearrange("g (q r) c -> q r g c", r=4)[:, r, :, cols]
                nc.sync.dma_start(dst[r:P:32, :, :].bitcast(I32), rows.bitcast(I32))

        def load_table(place, src, name):
            words = placed(place, [P, T], U32, name)
            nc.sync.dma_start(words[:].bitcast(I32), src.rearrange("p n i -> p (n i)").bitcast(I32))
            return words

        def load_w1(a):
            words = held([P, 2, 2 * BANK], U8, "w1_w%d" % a)
            src = w1_words.rearrange("g p c -> p g c")[:, :, 2 * BANK * a : 2 * BANK * (a + 1)]
            nc.sync.dma_start(words[:].bitcast(I32), src.bitcast(I32))
            return words

        def load_raw(place, src, half, name):
            raw = placed(place, [P, PACK, BANK], F32, name)
            rows = src.rearrange("(p i) c -> p i c", i=PACK)
            nc.sync.dma_start(raw[:], rows[:, :, BANK * half : BANK * (half + 1)])
            return raw

        def load_wg1(h):
            half = factor_tile("wg1_sb0") if h == 0 else held([P, BANK], F32, "wg1_sb1")
            nc.sync.dma_start(half[:], wg1[:, BANK * h : BANK * (h + 1)])
            return half

        def load_wg2(t):
            rows = held([P, S], F32, "wg2_sb%d" % t)
            for q in range(QUADS):
                nc.sync.dma_start(rows[32 * q : 32 * q + 32, :], wg2.rearrange("(m t) j -> m t j", t=PACK)[:, t, :])
            return rows

        nc.sync.dma_start(idx[:], offs)
        wg1_sb = [load_wg1(0)]
        for r in range(4):
            rows = tab_scales.rearrange("g (q r) c -> q g r c", r=4)[:, :, r, :]
            nc.sync.dma_start(tab_sc[r:P:16, 0, :].bitcast(I32), rows.bitcast(I32))
        tab_w = [load_table("z_w1", tab_words[0], "tab_w0")]
        tab_w.append(load_table(page_place(0, 1), tab_words[1], "tab_w1"))
        load_scales(w1_sc[0], w1_scales, slice(0, BANK))
        w1_w = [load_w1(0)]
        nc.sync.dma_start(idx2[:], offs2)
        load_scales(tab2_sc, tab2_scales, slice(0, T))
        tab2_w = load_table(page_place(1, 0), tab2_words[0], "tab2_w")
        nc.sync.dma_start(idx3[:], offs3)
        nc.sync.dma_start(idx4[:], offs4)
        field_raw = [load_raw(page_place(0, 0), field, 0, "field_raw0"), load_raw(page_place(1, 1), field, 1, "field_raw1")]
        first_raw = pair.tile([P, 2, PACK, BANK], F32, name="first_raw", align_bytes=64, offset=0)
        for x, src in enumerate((w3, w2)):
            nc.sync.dma_start(first_raw[:, x], src.rearrange("(p i) c -> p i c", i=PACK)[:, :, :BANK])

        neg_log_wg = [held([P, 4, PACK, QUADS, 32], F32, "neg_log_wg%d" % h) for h in range(2)]
        log_wg = {}

        def take_log_wg(h):
            log_wg[h] = factor_tile("log_wg")
            nc.scalar.activation(log_wg[h][:], wg1_sb[h][:], ACT.Ln)

        def turn_log_wg(h, role):
            turned = bank(role, "turned")
            for jb in range(4):
                cols = slice(P * jb, P * (jb + 1))
                nc.tensor.transpose(turned[:, cols], log_wg[h][:, cols], ident[:])
            spread_log_wg(h, turned[:].rearrange("p (b m t) -> p b t m", b=4, t=PACK))

        def spread_log_wg(h, by_lane):
            for jb in range(4):
                src = by_lane[:, jb]
                nc.scalar.activation(
                    neg_log_wg[h][:, jb], src.unsqueeze(2).to_broadcast([P, PACK, QUADS, 32]), ACT.Copy, scale=-1.0
                )

        take_log_wg(0)
        turn_log_wg(0, "product")

        v_sc0 = held([P, S], U8, "v_sc0")
        v_sc = [v_sc0[:], v_sc1[:, 0, :]]
        for h in range(2):
            cols = slice(BANK * h, BANK * (h + 1))
            entries = idx[:, LIST_COLS * h : LIST_COLS * (h + 1)]
            nc.vector.tensor_copy(v_sc0[:, cols], tab_sc[:, 0, :].indirect(entries))
            queue = nc.scalar if h == 0 else nc.gpsimd
            queue.dma_start(v_sc1[0 : P - 16, 0, cols].bitcast(I32), v_sc0[16:P, cols].bitcast(I32))
        v_w = [placed("planes00", [P, 2, BANK], U32, "v_w0"), in_region(2, [P, 2, BANK], U32, "v_w1")]
        def gather_words(g, start, width):
            h, at = divmod(start, BANK)
            entries = idx[:, start // 16 : (start + width) // 16]
            nc.vector.tensor_copy(v_w[h][:, g, at : at + width], tab_w[g][:].indirect(entries))

        gather_words(0, 0, BANK)
        gather_words(0, BANK, BANK)
        gather_words(1, 0, P)
        gather_words(1, P, BANK - P)
        gather_words(1, BANK, BANK)
        v2_w = held([P, S], U32, "v2_w")
        v2_sc = held([P, S], U8, "v2_sc")
        nc.vector.tensor_copy(v2_sc[:], tab2_sc[:, 0, :].indirect(idx2[:]))
        nc.vector.tensor_copy(v2_w[:], tab2_w[:].indirect(idx2[:]))

        def weave(copy, dst, planes):
            copy(
                dst[:].rearrange("p (c e i) -> p c i e", e=4, i=PACK),
                planes.rearrange("p i (c e) -> p c i e", e=4),
            )

        def quantise(src, words, scales):
            nc.vector.quantize_mx(out=words.bitcast(E4M3), scales=scales, in_=src[:])

        q_w = {name: [held([P, BANK], U32, "q_%s%d" % (name, x)) for x in range(2)] for name in ("w2", "w3", "field")}
        q_sc = {name: [held([P, BANK], U8, "qs_%s%d" % (name, x)) for x in range(2)] for name in ("w2", "w3", "field")}
        def prepare_first_field_half():
            pieces = [slice(0, UNIT), slice(UNIT, BANK)]
            woven = [placed(page_place(0, 1 + x), [P, UNIT * PACK], BF16, "field_g0") for x in range(2)]
            for x in range(2):
                weave(nc.vector.tensor_copy, woven[x], field_raw[0][:, :, pieces[x]])
            for x in range(2):
                quantise(woven[x], q_w["field"][0][:, pieces[x]], q_sc["field"][0][:, pieces[x]])

        def prepare_second_field_half():
            grouped = placed("log_t", [P, BANK * PACK], BF16, "field_g1")
            weave(nc.scalar.copy, grouped, field_raw[1][:])
            quantise(grouped, q_w["field"][1][:], q_sc["field"][1][:])

        def prepare_first_weights(first, place):
            grouped = placed(place, [P, 2, 2 * P * PACK], BF16, "first_g")
            nc.scalar.copy(
                grouped[:].rearrange("p w (t m i) -> p w m i t", t=2, i=PACK),
                first_raw[:].rearrange("p w i (m t) -> p w m i t", t=PACK)[:, :, :, :, first : first + 2],
            )
            cols = slice(P * first, P * (first + 2))
            for x, name in enumerate(("w3", "w2")):
                quantise(grouped[:, x], q_w[name][0][:, cols], q_sc[name][0][:, cols])

        def prepare_second_weight(name):
            grouped = in_region(0 if name == "w3" else 3, [P, BANK * PACK], BF16, name + "_g1")
            nc.scalar.copy(
                grouped[:].rearrange("p (t m i) -> p m i t", t=PACK, i=PACK),
                second_raw[name][:].rearrange("p i (m t) -> p m i t", t=PACK),
            )
            quantise(grouped, q_w[name][1][:], q_sc[name][1][:])

        pages, turned_sums = {}, {}

        def page(a, t):
            if (a, t) not in pages:
                if a == 1 and t >= 2:
                    pages[a, t] = pair.tile([P, T2], F32, name="page%d%d" % (a, t), align_bytes=64, offset=4 * T2 * (t - 2))
                else:
                    pages[a, t] = placed(page_place(a, t), [P, T2], F32, "page%d%d" % (a, t))
            return pages[a, t]

        def core_product(a, h, jb, role):
            acc = bank(role, "acc_core")
            cols = slice(P * jb, P * (jb + 1))
            for g in range(2):
                nc.tensor.matmul_mx(
                    out=acc[:],
                    lhsT=v_w[h][:, g, cols].bitcast(E4M3),
                    lhsT_scale=v_sc[g][:, BANK * h + P * jb : BANK * h + P * (jb + 1)],
                    rhs=w1_w[a][:, g, :].bitcast(E2M1),
                    rhs_scale=w1_sc[a][:, g, :],
                    start=(g == 0),
                    stop=(g == 1),
                )
            return acc[:].rearrange("p (m t) -> p t m", t=PACK)

        def core_products(a, h, blocks):
            if (a, h) not in turned_sums:
                places = ("planes00", "planes01") if (a, h) == (1, 1) else ("b_t", "sq_t")
                b_t = placed(places[0], [P, 4, BANK], F32, "b_t")
                sq_t = placed(places[1], [P, 4, BANK], F32, "sq_t")
                turned_sums[a, h] = (b_t, sq_t)
            b_t, sq_t = turned_sums[a, h]
            for jb in blocks:
                by_lane = core_product(a, h, jb, "product")
                nc.scalar.activation(sq_t[:, jb, :].rearrange("p (t m) -> p t m", t=PACK), by_lane, ACT.Square)
                nc.scalar.copy(b_t[:, jb, :].rearrange("p (t m) -> p t m", t=PACK), by_lane)

        def turn_and_add(dst, first, second):
            for jb in range(4):
                cols = slice(P * jb, P * (jb + 1))
                nc.tensor.matmul(dst[:, cols], first[:, jb, :], ident[:], start=True, stop=False, is_transpose=True)
                nc.tensor.matmul(dst[:, cols], second[:, jb, :], ident[:], start=False, stop=True, is_transpose=True)

        logs, numerators = {}, {}

        def take_logs(a, h, place):
            sq_t = turned_sums[a, h][1]
            logs[a, h] = placed(place, [P, 4, BANK], F32, "log_t")
            for t in range(PACK):
                rows = slice(P * t, P * (t + 1))
                nc.scalar.activation(logs[a, h][:, :, rows], sq_t[:, :, rows], ACT.Ln, bias=1.0)

        def make_numerator(a, h, t):
            b_t, sq_t = turned_sums[a, h]
            rows = slice(P * t, P * (t + 1))
            num = bank("turned", "num")
            turn_and_add(num, b_t[:, :, rows], sq_t[:, :, rows])
            numerators[a, h, t] = numerator_tile("numerator")
            nc.scalar.copy(numerators[a, h, t][:], num[:])

        def core_features(a, h, after_lane):
            for t in range(PACK):
                rows = slice(P * t, P * (t + 1))
                exponent = bank("turned", "exponent")
                turn_and_add(exponent, logs[a, h][:, :, rows], neg_log_wg[h][:, :, t].rearrange("p b g m -> p b (g m)"))
                factor = factor_tile("factor")
                nc.scalar.activation(factor[:], exponent[:], ACT.Exp, scale=-1.0)
                if (a, h, t) not in numerators:
                    make_numerator(a, h, t)
                entries = idx3[:, LIST_COLS * h : LIST_COLS * (h + 1)]
                nc.vector.tensor_tensor(page(a, t)[:].indirect(entries), numerators[a, h, t][:], factor[:], MULT)
                if t in after_lane:
                    after_lane[t]()

        def first_core_step(after_lane):
            sq_t = placed("sq_t", [P, 4, BANK], F32, "sq_t")
            log_t = placed("log_t", [P, 4, BANK], F32, "log_t")
            sums, b_lanes = [], {}
            for jb in range(4):
                sums.append(core_product(0, 0, jb, "product"))
                nc.scalar.activation(sq_t[:, jb, :].rearrange("p (t m) -> p t m", t=PACK), sums[jb], ACT.Square)
                nc.scalar.activation(log_t[:, jb, :], sq_t[:, jb, :], ACT.Ln, bias=1.0)


            def copy_lanes(copy, dst, first, last, blocks=range(4)):
                for jb in blocks:
                    copy(dst[:, jb], sums[jb][:, first:last, :])

            first_lane = placed("z_sc1", [P, 4, 1, P], F32, "b_lane0")
            copy_lanes(nc.vector.tensor_copy, first_lane, 0, 1, range(3))
            copy_lanes(nc.scalar.copy, first_lane, 0, 1, [3])
            prepare_first_field_half()
            b_lanes[0] = first_lane[:, :, 0, :]
            for t in range(PACK):
                a, h = 0, 0
                rows = slice(P * t, P * (t + 1))
                exponent = bank("turned", "exponent")
                turn_and_add(exponent, log_t[:, :, rows], neg_log_wg[h][:, :, t].rearrange("p b g m -> p b (g m)"))
                num = bank("turned", "num")
                turn_and_add(num, b_lanes[t], sq_t[:, :, rows])
                factor = factor_tile("factor")
                nc.scalar.activation(factor[:], exponent[:], ACT.Exp, scale=-1.0)
                numerator = numerator_tile("numerator")
                nc.scalar.copy(numerator[:], num[:])
                if t == 0:
                    other_lanes = placed("z_sc1", [P, 4, PACK - 1, P], F32, "b_lanes")
                    copy_lanes(nc.scalar.copy, other_lanes[:, :, 0:1], 1, 2)
                    copy_lanes(nc.scalar.copy, other_lanes[:, :, 1:3], 2, PACK)
                    for lane in range(1, PACK):
                        b_lanes[lane] = other_lanes[:, :, lane - 1, :]
                entries = idx3[:, LIST_COLS * h : LIST_COLS * (h + 1)]
                nc.vector.tensor_tensor(page(a, t)[:].indirect(entries), numerator[:], factor[:], MULT)
                if t in after_lane:
                    after_lane[t]()

        def edge_sum(a, t, start, width, role, dst):
            rows = slice(P * t, P * (t + 1))
            cols = slice(start, start + width)
            h, at = divmod(start, BANK)
            part = slice(at, at + width)
            acc = bank(role, "acc_edge")[:, :width]
            nc.tensor.matmul_mx(
                out=acc, lhsT=q_w["w3"][a][:, rows].bitcast(E4M3), lhsT_scale=q_sc["w3"][a][:, rows],
                rhs=q_w["field"][h][:, part].bitcast(E4M3), rhs_scale=q_sc["field"][h][:, part], start=True, stop=False,
            )
            nc.tensor.matmul_mx(
                out=acc, lhsT=q_w["w2"][a][:, rows].bitcast(E4M3), lhsT_scale=q_sc["w2"][a][:, rows],
                rhs=v2_w[:, cols].bitcast(E4M3), rhs_scale=v2_sc[:, cols], start=False, stop=True,
            )
            nc.scalar.activation(dst, acc, ACT.Tanh)

        def edge_features(a, t):
            h2 = placed("w4_w", [P, S], F32, "h2") if (a, t) == (1, 2) else placed("h2", [P, S], F32, "h2", bufs=3)
            for h in range(2):
                edge_sum(a, t, BANK * h, BANK, "turned" if (a, t) == (1, 3) else "product", h2[:, BANK * h : BANK * (h + 1)])
            nc.vector.tensor_tensor(page(a, t)[:].indirect(idx4[:]), h2[:], wg2_sb[t][:], MULT)

        planes, z_g, z_w, z_sc, accs = {}, {}, {}, {}, {}

        def lane_of(a, t, half):
            if a == 0:
                if 0 not in planes:
                    planes[0] = in_region(0, [P, PACK * T2], BF16, "planes0")
                return planes[0][:, T2 * t + 2 * BANK * half : T2 * t + 2 * BANK * (half + 1)]
            if (a, half) not in planes:
                planes[a, half] = placed("planes0%d" % half, [P, PACK * 2 * BANK], BF16, "pairs%d" % half)
            return planes[a, half][:].rearrange("p (u c e) -> p u c e", u=2, e=2)[:, t // 2, :, t % 2]

        def round_cols(a, t, start, width, factor=None, on_vector=False):
            half, at = divmod(start, 2 * BANK)
            dst = lane_of(a, t, half)[:, at : at + width]
            src = page(a, t)[:, start : start + width]
            factor = gain_sb[:, a, t : t + 1] if factor is None else factor
            if on_vector:
                nc.vector.tensor_scalar(dst, src, factor, None, MULT)
            else:
                nc.scalar.activation(dst, src, ACT.Copy, scale=factor)

        def round_page(a, t):
            for half in range(2):
                round_cols(a, t, 2 * BANK * half, 2 * BANK)

        def weave_z(a, start, width):
            half, at = divmod(start, 2 * BANK)
            cols = slice(at, at + width)
            if a == 0:
                grouped = placed(page_place(0, 1 + start // BANK % 3), [P, PACK * width], BF16, "z_g")
                z_g[a, start] = grouped[:]
                weave(nc.scalar.copy, grouped, planes[0][:].rearrange("p (i c) -> p i c", i=PACK)[:, :, start : start + width])
            else:
                if 1 not in z_g:
                    z_g[1] = in_region(0, [P, PACK * T2], BF16, "z1_g")
                z_g[a, start] = z_g[1][:, PACK * start : PACK * (start + width)]
                pairs = planes[a, half][:].bitcast(F32).rearrange("p (u c) -> p c u", u=2)
                words = z_g[a, start].bitcast(F32).rearrange("p (c u) -> p c u", u=2)
                nc.vector.tensor_copy(words, pairs[:, cols, :])

        def quantise_z(a, start, width):
            if a not in z_w:
                z_w[a] = placed((page_place(0, 0), "z_w1")[a], [P, T2], U32, "z_w%d" % a)
                z_sc[a] = placed("z_sc%d" % a, [P, T2], U8, "z_sc%d" % a)
            cols = slice(start, start + width)
            nc.vector.quantize_mx(out=z_w[a][:, cols].bitcast(E4M3), scales=z_sc[a][:, cols], in_=z_g[a, start])

        out_banks = [role for role in ("product", "turned") for copies in range(BANKS[role])]

        def project(a, start, width, halves=(0, 1), apart=False, on_vector=()):
            cols = slice(start, start + width)
            side_by_side = 1 if apart else BANK // width
            filled = side_by_side * width
            for nt in halves:
                key = (start, nt // side_by_side)
                if key not in accs:
                    accs[key] = bank(out_banks[len(accs) % len(out_banks)], "acc_out")
                at = width * (nt % side_by_side)
                rows = slice(P * nt, P * (nt + 1))
                last = a == 1 and (nt + 1) % side_by_side == 0
                nc.tensor.matmul_mx(
                    out=accs[key][:, at : at + width],
                    lhsT=w4_w[:, a, rows].bitcast(E4M3), lhsT_scale=w4_sc[:, a, rows],
                    rhs=z_w[a][:, cols].bitcast(E4M3), rhs_scale=z_sc[a][:, cols],
                    start=(a == 0 and at == 0), stop=last,
                )
                if last:
                    if start not in stored:
                        stored[start] = factor_tile("res") if len(stored) % 2 == 0 else numerator_tile("res")
                    res = stored[start]
                    copy = nc.vector.tensor_copy if nt in on_vector else nc.scalar.copy
                    copy(res[:, width * (nt + 1) - filled : width * (nt + 1)], accs[key][:, :filled])
                    if nt == 1:
                        dst = out.rearrange("(n p) c -> p n c", p=P)[:, :, cols]
                        nc.sync.dma_start(dst, res[:].rearrange("p (n c) -> p n c", n=2))

        stored = {}
        wg2_sb = [load_wg2(0), load_wg2(1)]
        wg1_sb.append(load_wg1(1))
        second_raw = {"w3": load_raw("z_w1", w3, 1, "w3_raw1"), "w2": load_raw(page_place(1, 1), w2, 1, "w2_raw1")}
        wg2_sb.extend([load_wg2(2), load_wg2(3)])
        w1_w.append(load_w1(1))
        load_scales(w1_sc[1], w1_scales, slice(BANK, 2 * BANK))
        gain_sb = held([P, 2, PACK], F32, "gain_sb")
        nc.sync.dma_start(gain_sb[:], gain.rearrange("(a p t) -> p a t", a=2, t=PACK))
        load_scales(w4_sc, w4_scales, slice(0, N))

        first_core_step({2: lambda: prepare_first_weights(0, page_place(0, 3))})
        prepare_second_field_half()
        prepare_first_weights(2, "b_t")
        edge_features(0, 0)
        edge_features(0, 1)
        edge_features(0, 2)
        prepare_second_weight("w3")
        core_products(0, 1, range(4))
        turned = bank("product", "turned")
        for jb in range(4):
            cols = slice(P * jb, P * (jb + 1))
            nc.tensor.transpose(turned[:, cols], wg1_sb[1][:, cols], ident[:])
        log_wg[1] = factor_tile("log_wg")
        by_lane = log_wg[1][:].rearrange("p (b t m) -> p b t m", b=4, t=PACK)
        nc.scalar.activation(by_lane, turned[:].rearrange("p (b m t) -> p b t m", b=4, t=PACK), ACT.Ln)
        take_logs(0, 1, "log_t")
        spread_log_wg(1, by_lane)
        core_features(0, 1, {1: lambda: prepare_second_weight("w2")})
        edge_features(0, 3)
        edge_features(1, 0)
        edge_features(1, 1)
        core_products(1, 0, range(4))
        take_logs(1, 0, "log_t")
        core_products(1, 1, range(4))
        take_logs(1, 1, "z_w1")
        core_features(1, 0, {})
        round_page(0, 0)
        round_page(0, 1)
        round_page(0, 2)
        round_page(0, 3)

        def finish_z0(c):
            weave_z(0, BANK * c, BANK)
            quantise_z(0, BANK * c, BANK)

        core_features(1, 1, {t: (lambda c=t: finish_z0(c)) for t in range(3)})
        edge_features(1, 2)
        edge_features(1, 3)
        finish_z0(3)
        w4_w = placed("w4_w", [P, 2, N], U32, "w4_w")
        nc.sync.dma_start(w4_w[:].bitcast(I32), w4_words.rearrange("a p c i -> p a (c i)").bitcast(I32))
        units = [(UNIT * u, UNIT) for u in range(T2 // UNIT)]
        for unit in units[:-1]:
            project(0, *unit)
        project(0, *units[-1], halves=(0,), apart=True)
        for t in range(3):
            round_page(1, t)
        last_gain = pair.tile([P, 1], F32, name="last_gain", align_bytes=64, offset=0)
        nc.scalar.copy(last_gain[:], gain_sb[:, 1, PACK - 1 :])
        ahead = 4
        for unit in units[:ahead]:
            round_cols(1, 3, *unit)
        weave_z(1, *units[0])
        for u, unit in enumerate(units):
            if u + 1 < len(units):
                weave_z(1, *units[u + 1])
            quantise_z(1, *unit)
            if u > 0:
                project(1, *units[u - 1])
                if u == len(units) - 2:
                    project(0, *units[-1], halves=(1,), apart=True)
                if u - 1 + ahead < len(units):
                    round_cols(1, 3, *units[u - 1 + ahead], factor=last_gain[:], on_vector=u - 1 + ahead >= len(units) - ON_VECTOR)
        project(1, *units[-1], apart=True, on_vector=(0,))
